import numpy as np
import ml_dtypes


def mxq(x, axis, fmt="e4m3"):
    dtype, down = {"e4m3": (ml_dtypes.float8_e4m3fn, 7), "e5m2": (ml_dtypes.float8_e5m2, 14)}[fmt]
    v = np.moveaxis(np.asarray(x, np.float32).astype(ml_dtypes.bfloat16).astype(np.float64), axis, -1)
    blocks = v.reshape(v.shape[:-1] + (-1, 32))
    amax = np.abs(blocks).max(-1, keepdims=True)
    byte = np.maximum(np.where(amax > 0, np.frexp(amax)[1] - 1 + 127, 0) - down, 1)
    scale = np.exp2(byte - 127.0)
    codes = (blocks / scale).astype(np.float32).astype(dtype).astype(np.float64)
    return np.moveaxis((codes * scale).reshape(v.shape), -1, axis)


WIDE = False


def mx_kscale(k):
    if not WIDE:
        return np.ones(k)
    levels = np.array([10, -10, 5, -5, 0])
    if k % 512:
        return np.exp2(np.random.permutation(np.resize(levels, k // 32))).repeat(32)
    a = np.empty((k // 512, 16))
    for p in range(k // 512):
        a[p, :8] = np.random.permutation(np.resize(levels, 8))
        for g in range(8):
            far = levels[np.abs(levels - a[p, g]) >= 10]
            a[p, g + 8] = far[np.random.randint(len(far))]
    return np.exp2(a.ravel()).repeat(32)


BF16 = ml_dtypes.bfloat16


def bf(x):
    return np.asarray(x, np.float32).astype(BF16)


def f64(x):
    return np.asarray(x).astype(np.float64)


S, K, C, A = 2048, 2048, 512, 1024


def draw0():
    s = mx_kscale(K)
    u = mx_kscale(S)
    mean = 0.5 * np.random.standard_normal(K)
    spectra = mean + np.random.standard_normal((S, K))
    return {
        "spectra": bf(spectra * s),
        "mean": bf(mean * s),
        "r": bf(np.random.standard_normal((K, C)) / np.sqrt(K) / s[:, None]),
        "weight": bf(np.random.uniform(0.5, 1.5, S) * u),
        "y": bf(np.random.standard_normal((S, A)) / np.sqrt(S) / u[:, None]),
        "inv_score": bf(np.random.uniform(0.5, 1.5, C)),
    }


def core(spectra, mean, r, weight, y, inv_score):
    xc = f64(spectra) - f64(mean)
    t = mxq(xc, 1, "e4m3") @ mxq(f64(r), 0, "e4m3")
    z = t * f64(weight)[:, None]
    cov = mxq(z, 0, "e4m3").T @ mxq(f64(y), 0, "e4m3")
    return cov * f64(inv_score)[:, None]


def e4m3fn_bytes(y):
    return np.clip(np.asarray(y, np.float64), -448.0, 448.0).astype(np.float32).astype(ml_dtypes.float8_e4m3fn).view(np.uint8)


def e4m3fn_values(b):
    return np.asarray(b, np.uint8).view(ml_dtypes.float8_e4m3fn).astype(np.float64)


def setup_inputs():
    d = draw0()
    x0 = np.asarray(d['y']).astype(np.float64)
    s = (np.max(np.abs(x0), axis=(1,), keepdims=True) / 448.0).astype(np.float32)
    out = {}
    for k, v in d.items():
        if k == 'y':
            out['y_bytes'] = e4m3fn_bytes(x0 / s.astype(np.float64))
            out['y_scale'] = s
        else:
            out[k] = v
    return out


def reference(spectra, mean, r, weight, y_bytes, y_scale, inv_score):
    return core(spectra, mean, r, weight, e4m3fn_values(y_bytes) * y_scale.astype(np.float64), inv_score)

@@ -1,0 +1,383 @@
+from contextlib import ExitStack
+
+import concourse.mybir as mybir
+from concourse.masks import make_identity
+
+S, K, C, A = 2048, 2048, 512, 1024
+P = 128
+PACK = 4
+PASS = P * PACK
+G_K = K // PASS
+G_S = S // PASS
+N_TILES = S // P
+HALF_A = A // 2
+
+FLOPS = 2 * S * K * C + 2 * S * C * A
+
+F32 = mybir.dt.float32
+BF16 = mybir.dt.bfloat16
+U32 = mybir.dt.uint32
+U8 = mybir.dt.uint8
+FP8 = mybir.dt.float8_e4m3fn
+FP8X4 = mybir.dt.float8_e4m3fn_x4
+COPY = mybir.ActivationFunctionType.Copy
+MULT = mybir.AluOpType.mult
+SUB = mybir.AluOpType.subtract
+ADD = mybir.AluOpType.add
+
+
+def tile_pls_concentration_loadings_s7_kernel(
+    tc, spectra, mean, r, weight, y_bytes, y_scale, inv_score, out
+):
+    nc = tc.nc
+    with ExitStack() as ctx:
+        keep = ctx.enter_context(tc.tile_pool(name="keep", bufs=1))
+        work = ctx.enter_context(tc.tile_pool(name="work", bufs=3))
+        psum = ctx.enter_context(tc.psum_pool(name="psum", bufs=1))
+
+        ident = keep.tile([P, P], F32, name="ident")
+        make_identity(nc, ident[:])
+
+        ctx.enter_context(tc.manual_schedule())
+
+        mean_sb = keep.tile([P, G_K, 2, 2], BF16, name="mean_sb")
+        weight_bf = keep.tile([P, G_S, PACK], BF16, name="weight_bf")
+        weight_sb = keep.tile([P, G_S * PACK], F32, name="weight_sb")
+        y_scale_sb = keep.tile([P, G_S, PACK], F32, name="y_scale_sb")
+        inv_bf = keep.tile([P, 4, 2], BF16, name="inv_bf")
+        inv_sb = keep.tile([P, 4], F32, name="inv_sb")
+        warm = keep.tile([P, 1], F32, name="warm")
+        zeros = keep.tile([P, 512], BF16, name="zeros")
+
+        x_raw = [keep.tile([P, K], BF16, name=f"x_raw{i}", align_bytes=64) for i in range(N_TILES)]
+        r_raw = [keep.tile([P, PACK, C], BF16, name=f"r_raw{g}", align_bytes=64) for g in range(G_K)]
+        y_raw = [keep.tile([P, PACK, A], U8, name=f"y_raw{g}", align_bytes=64) for g in range(G_S)]
+
+        x_hbm = spectra.rearrange("(g p j) k -> g j p k", p=P, j=PACK)
+        r_hbm = r.rearrange("(g p j) c -> g p j c", p=P, j=PACK)
+        y_hbm = y_bytes.rearrange("(g p j) a -> g p j a", p=P, j=PACK)
+
+        def load_x(i, pieces=1):
+            for n in range(pieces):
+                cols = slice(K * n // pieces, K * (n + 1) // pieces)
+                nc.sync.dma_start(out=x_raw[i][:, cols], in_=x_hbm[i // PACK, i % PACK][:, cols])
+
+        def load_r(g):
+            nc.sync.dma_start(out=r_raw[g][:], in_=r_hbm[g])
+
+        def load_y(g):
+            nc.sync.dma_start(out=y_raw[g][:], in_=y_hbm[g])
+
+        nc.vector.memset(zeros[:], 0.0)
+        nc.scalar.dma_start(
+            out=mean_sb[:].rearrange("p g u e -> p g (u e)"),
+            in_=mean.rearrange("(g p t) -> p g t", p=P, t=PACK),
+        )
+        load_x(0, 2)
+        for g in range(G_K):
+            load_r(g)
+        load_x(1)
+        load_y(0)
+        nc.sync.dma_start(
+            out=y_scale_sb[:], in_=y_scale.rearrange("(g p j) o -> p g (j o)", p=P, j=PACK)
+        )
+        nc.sync.dma_start(
+            out=weight_bf[:], in_=weight.rearrange("(g p j) -> p g j", p=P, j=PACK)
+        )
+        nc.sync.dma_start(
+            out=inv_bf[:, :, 0:1], in_=inv_score.rearrange("(m p o) -> p m o", p=P, o=1)
+        )
+        load_x(2)
+        load_x(3)
+        load_y(1)
+        for i in range(4, 8):
+            load_x(i)
+        load_y(2)
+        for i in range(8, 10):
+            load_x(i)
+        load_y(3)
+        for i in range(10, N_TILES):
+            load_x(i)
+
+        nc.vector.memset(warm[:], 0.0)
+        nc.scalar.activation(warm[:], warm[:], COPY)
+
+        r_codes = keep.tile([P, G_K, C], U32, name="r_codes", align_bytes=64)
+        r_scales = keep.tile([P, G_K, C], U8, name="r_scales", align_bytes=64)
+        y_codes = [keep.tile([P, A], U32, name=f"y_codes{g}", align_bytes=64) for g in range(G_S)]
+        y_scales = [keep.tile([P, A], U8, name=f"y_scales{g}", align_bytes=64) for g in range(G_S)]
+        z_codes = [keep.tile([P, C], U32, name=f"z_codes{g}", align_bytes=64) for g in range(G_S)]
+        z_scales = [keep.tile([P, C], U8, name=f"z_scales{g}", align_bytes=64) for g in range(G_S)]
+
+        def bank(b, name):
+            return psum.tile([P, 512], F32, tag=f"bank{b}", name=name)
+
+        def interleave(engine, dst, src):
+            dst = dst.rearrange("p (a i) j -> p a j i", i=4)
+            src = src.rearrange("p j (a i) -> p a j i", i=4)
+            if engine is nc.scalar:
+                nc.scalar.copy(out=dst, in_=src)
+            else:
+                nc.vector.tensor_copy(out=dst, in_=src)
+
+        r_grouped = {}
+
+        def interleave_r(g, c0, c1, engine):
+            if g not in r_grouped:
+                r_grouped[g] = work.tile([P, C, PACK], BF16, tag="r_grouped", name="r_grouped", bufs=4, align_bytes=64)
+            interleave(engine, r_grouped[g][:, c0:c1, :], r_raw[g][:, :, c0:c1])
+
+        def quantise_r(g):
+            nc.vector.quantize_mx(
+                out=r_codes[:, g, :].bitcast(FP8X4),
+                scales=r_scales[:, g, :],
+                in_=r_grouped[g][:].rearrange("p c j -> p (c j)"),
+            )
+
+        x_banks = {}
+        x_grouped = {}
+        x_codes = {}
+        x_scales = {}
+
+        def transpose_x(i):
+            words = x_raw[i][:].bitcast(F32)
+            for b in range(2):
+                ps = bank(b, "x_turned")
+                view = ps[:].rearrange("p (u g s) -> p u g s", u=2, g=2)
+                for gl in range(2):
+                    g = 2 * b + gl
+                    for u in range(2):
+                        nc.tensor.transpose(
+                            view[:, u, gl, :], words[:, 256 * g + u : 256 * (g + 1) : 2], ident[:]
+                        )
+                x_banks[i, b] = ps
+
+        def centre_x(i, b):
+            if b == 0:
+                x_grouped[i] = work.tile(
+                    [P, G_K, P, 2, 2], BF16, tag="x_grouped", name="x_grouped", align_bytes=64
+                )
+            nc.vector.tensor_tensor(
+                out=x_grouped[i][:, 2 * b : 2 * b + 2],
+                in0=x_banks[i, b][:].bitcast(BF16).rearrange(
+                    "p (u g s e) -> p g s u e", u=2, g=2, e=2
+                ),
+                in1=mean_sb[:, 2 * b : 2 * b + 2].unsqueeze(2).to_broadcast([P, 2, P, 2, 2]),
+                op=SUB,
+            )
+
+        def quantise_x(i, b):
+            if b == 0:
+                x_codes[i] = work.tile([P, G_K * P], U32, tag="x_codes", name="x_codes", align_bytes=64)
+                x_scales[i] = work.tile([P, G_K * P], U8, tag="x_scales", name="x_scales", align_bytes=64)
+            cols = slice(256 * b, 256 * (b + 1))
+            flat = x_grouped[i][:].rearrange("p g s u e -> p (g s u e)")
+            nc.vector.quantize_mx(
+                out=x_codes[i][:, cols].bitcast(FP8X4),
+                scales=x_scales[i][:, cols],
+                in_=flat[:, 1024 * b : 1024 * (b + 1)],
+            )
+
+        t_banks = {}
+        z_planes = {}
+        z_grouped = {}
+
+        def multiply_t(i, b, c0, c1):
+            ps = bank(b, "t_sum")
+            for g in range(G_K):
+                cols = slice(P * g, P * (g + 1))
+                nc.tensor.matmul_mx(
+                    out=ps[:, : c1 - c0],
+                    lhsT=x_codes[i][:, cols].bitcast(FP8X4),
+                    lhsT_scale=x_scales[i][:, cols],
+                    rhs=r_codes[:, g, c0:c1].bitcast(FP8X4),
+                    rhs_scale=r_scales[:, g, c0:c1],
+                    start=(g == 0),
+                    stop=(g == G_K - 1),
+                )
+            t_banks[i, c0] = ps
+
+        def weigh_t(i, c0, c1):
+            g, j = i // PACK, i % PACK
+            if g not in z_planes:
+                z_planes[g] = work.tile([P, PACK, C], BF16, tag="z_planes", name="z_planes", bufs=2, align_bytes=64)
+            nc.scalar.activation(
+                z_planes[g][:, j, c0:c1], t_banks[i, c0][:, : c1 - c0], COPY, scale=weight_sb[:, i : i + 1]
+            )
+
+        def interleave_z(g, c0, c1, engine):
+            if g not in z_grouped:
+                z_grouped[g] = work.tile(
+                    [P, C, PACK], BF16, tag="z_grouped", name="z_grouped", bufs=2, align_bytes=64
+                )
+            interleave(engine, z_grouped[g][:, c0:c1, :], z_planes[g][:, :, c0:c1])
+
+        def quantise_z(g, c0, c1):
+            nc.vector.quantize_mx(
+                out=z_codes[g][:, c0:c1].bitcast(FP8X4),
+                scales=z_scales[g][:, c0:c1],
+                in_=z_grouped[g][:].rearrange("p c j -> p (c j)")[:, PACK * c0 : PACK * c1],
+            )
+
+        y_planes = {}
+        y_grouped = {}
+        y_pooled = {}
+
+        def widen_y(g, h):
+            y_planes[g, h] = work.tile(
+                [P, PACK, HALF_A], BF16, tag="y_planes", name="y_planes", align_bytes=64
+            )
+            for j in range(PACK):
+                nc.scalar.activation(
+                    y_planes[g, h][:, j, :],
+                    y_raw[g][:, j, HALF_A * h : HALF_A * (h + 1)].bitcast(FP8),
+                    COPY,
+                    scale=y_scale_sb[:, g, j : j + 1],
+                )
+
+        def interleave_y(g, h, a0, a1, engine):
+            if engine is nc.gpsimd:
+                t = work.tile([P, a1 - a0, PACK], BF16, tag="y_pooled", name="y_pooled", bufs=1, align_bytes=64)
+            elif (g, h) not in y_grouped:
+                t = work.tile([P, HALF_A, PACK], BF16, tag="y_grouped", name="y_grouped", align_bytes=64)
+                y_grouped[g, h] = t
+            else:
+                t = y_grouped[g, h]
+            src = y_planes[g, h][:, :, a0:a1]
+            if engine is nc.gpsimd:
+                nc.gpsimd.tensor_scalar(
+                    out=t[:], in0=src.rearrange("p j a -> p a j"),
+                    scalar1=1.0, scalar2=0.0, op0=MULT, op1=ADD,
+                )
+                y_pooled[g, h, a0] = t
+            else:
+                interleave(engine, t[:, a0:a1, :], src)
+
+        def quantise_y(g, h, a0, a1, pooled=False):
+            cols = slice(HALF_A * h + a0, HALF_A * h + a1)
+            if pooled:
+                src = y_pooled[g, h, a0][:]
+            else:
+                src = y_grouped[g, h][:, a0:a1, :]
+            nc.vector.quantize_mx(
+                out=y_codes[g][:, cols].bitcast(FP8X4),
+                scales=y_scales[g][:, cols],
+                in_=src.rearrange("p a j -> p (a j)"),
+            )
+
+        cov_banks = {}
+
+        def multiply_cov(m, h, g):
+            if g == 0:
+                b = 4 + m if h == 0 else m
+                cov_banks[m, h] = bank(b, "cov_sum")
+            c_cols = slice(P * m, P * (m + 1))
+            a_cols = slice(HALF_A * h, HALF_A * (h + 1))
+            nc.tensor.matmul_mx(
+                out=cov_banks[m, h][:],
+                lhsT=z_codes[g][:, c_cols].bitcast(FP8X4),
+                lhsT_scale=z_scales[g][:, c_cols],
+                rhs=y_codes[g][:, a_cols].bitcast(FP8X4),
+                rhs_scale=y_scales[g][:, a_cols],
+                start=(g == 0),
+                stop=(g == G_S - 1),
+            )
+
+        def store_cov(m, h, engine):
+            res = keep.tile([P, HALF_A], F32, name=f"res{m}{h}")
+            if engine is nc.vector:
+                nc.vector.tensor_scalar(
+                    out=res[:], in0=cov_banks[m, h][:], scalar1=inv_sb[:, m : m + 1],
+                    scalar2=None, op0=MULT,
+                )
+            else:
+                nc.scalar.activation(res[:], cov_banks[m, h][:], COPY, scale=inv_sb[:, m : m + 1])
+            nc.sync.dma_start(
+                out=out[P * m : P * (m + 1), HALF_A * h : HALF_A * (h + 1)], in_=res[:]
+            )
+
+        chunks = [(0, 0), (1, 0), (0, 1), (2, 0), (1, 1), (3, 0), (2, 1), (3, 1)]
+        last = G_S - 1
+
+        idle = bank(7, "idle")
+        for n in range(3):
+            nc.tensor.matmul(idle[:], lhsT=zeros[:, :P], rhs=zeros[:], start=True, stop=True)
+        transpose_x(0)
+        interleave_r(0, 0, C, nc.scalar)
+        interleave_r(2, 0, C, nc.scalar)
+        for i in range(N_TILES):
+            n, piece = (i - 2) // 2, (i - 2) % 2
+            if i > 1:
+                interleave_y(*chunks[n], 128 * piece, 128 * (piece + 1), nc.gpsimd)
+            centre_x(i, 0)
+            centre_x(i, 1)
+            if i > 2 and i % 2 == 1 and i < 15:
+                quantise_y(*chunks[(i - 3) // 2], 256, HALF_A)
+            quantise_x(i, 0)
+            quantise_x(i, 1)
+            if i == 1:
+                nc.vector.tensor_copy(
+                    out=weight_sb[:], in_=weight_bf[:].rearrange("p g j -> p (g j)")
+                )
+                nc.vector.tensor_copy(out=inv_sb[:], in_=inv_bf[:, :, 0])
+            if i + 1 < N_TILES:
+                transpose_x(i + 1)
+            if i == 0:
+                interleave_r(1, 0, C, nc.vector)
+                quantise_r(0)
+                quantise_r(1)
+                interleave_r(3, 384, C, nc.scalar)
+                interleave_r(3, 0, 384, nc.vector)
+                quantise_r(2)
+                quantise_r(3)
+            if i + 1 < N_TILES:
+                multiply_t(i, 2 + i % 2, 0, C)
+            else:
+                for m in range(4):
+                    multiply_cov(m, 0, 2)
+                multiply_t(i, 3, 0, 256)
+                multiply_t(i, 1, 256, C)
+            if i % PACK == 1 and i > 1:
+                interleave_z(i // PACK - 1, 384, C, nc.scalar)
+                interleave_z(i // PACK - 1, 0, 384, nc.vector)
+            if i % PACK == 2 and i > 2:
+                quantise_z(i // PACK - 1, 0, C)
+            if i % 2 == 1 and i < 15:
+                widen_y(*chunks[(i - 1) // 2])
+            elif i % 2 == 0 and i > 0:
+                interleave_y(*chunks[(i - 2) // 2], 256, HALF_A, nc.scalar)
+            if i == 14:
+                widen_y(*chunks[7])
+            if i > 0:
+                weigh_t(i - 1, 0, C)
+            if i + 1 == N_TILES:
+                weigh_t(i, 0, 256)
+                weigh_t(i, 256, C)
+            if i > 1:
+                quantise_y(*chunks[n], 128 * piece, 128 * (piece + 1), pooled=True)
+            if i in (7, 8, 9, 10, 11, 12, 13, 14):
+                multiply_cov((i - 7) % PACK, 0, (i - 7) // PACK)
+
+        quantise_y(2, 1, 256, HALF_A)
+        interleave_y(3, 1, 0, 128, nc.gpsimd)
+        interleave_y(3, 1, 320, HALF_A, nc.scalar)
+        interleave_y(3, 1, 128, 320, nc.vector)
+        quantise_y(3, 1, 0, 128, pooled=True)
+        for m in (0, 2):
+            for g in range(G_S - 1):
+                multiply_cov(m, 1, g)
+        interleave_z(last, 0, 256, nc.vector)
+        quantise_y(3, 1, 128, 256)
+        interleave_z(last, 256, C, nc.vector)
+        quantise_z(last, 0, 256)
+        quantise_z(last, 256, C)
+        quantise_y(3, 1, 256, HALF_A)
+        for m in range(4):
+            multiply_cov(m, 0, last)
+            store_cov(m, 0, nc.vector if m % 2 else nc.scalar)
+        for m in (3, 1):
+            for g in range(G_S - 1):
+                multiply_cov(m, 1, g)
+        for m in (0, 2, 3, 1):
+            multiply_cov(m, 1, last)
+            store_cov(m, 1, nc.vector if m in (2, 1) else nc.scalar)

@@ -11,6 +11,8 @@ G_K = K // PASS
 G_S = S // PASS
 N_TILES = S // P
 HALF_A = A // 2
+HALF_C = C // 2
+Y_POOL = 176
 
 FLOPS = 2 * S * K * C + 2 * S * C * A
 
@@ -32,7 +34,8 @@ def tile_pls_concentration_loadings_s7_kernel(
     nc = tc.nc
     with ExitStack() as ctx:
         keep = ctx.enter_context(tc.tile_pool(name="keep", bufs=1))
-        work = ctx.enter_context(tc.tile_pool(name="work", bufs=3))
+        work = ctx.enter_context(tc.tile_pool(name="work", bufs=2))
+        stage = ctx.enter_context(tc.tile_pool(name="stage", bufs=1))
         psum = ctx.enter_context(tc.psum_pool(name="psum", bufs=1))
 
         ident = keep.tile([P, P], F32, name="ident")
@@ -46,8 +49,6 @@ def tile_pls_concentration_loadings_s7_kernel(
         y_scale_sb = keep.tile([P, G_S, PACK], F32, name="y_scale_sb")
         inv_bf = keep.tile([P, 4, 2], BF16, name="inv_bf")
         inv_sb = keep.tile([P, 4], F32, name="inv_sb")
-        warm = keep.tile([P, 1], F32, name="warm")
-        zeros = keep.tile([P, 512], BF16, name="zeros")
 
         x_raw = [keep.tile([P, K], BF16, name=f"x_raw{i}", align_bytes=64) for i in range(N_TILES)]
         r_raw = [keep.tile([P, PACK, C], BF16, name=f"r_raw{g}", align_bytes=64) for g in range(G_K)]
@@ -68,44 +69,36 @@ def tile_pls_concentration_loadings_s7_kernel(
         def load_y(g):
             nc.sync.dma_start(out=y_raw[g][:], in_=y_hbm[g])
 
-        nc.vector.memset(zeros[:], 0.0)
         nc.scalar.dma_start(
             out=mean_sb[:].rearrange("p g u e -> p g (u e)"),
             in_=mean.rearrange("(g p t) -> p g t", p=P, t=PACK),
         )
+        nc.scalar.dma_start(out=weight_bf[:], in_=weight.rearrange("(g p j) -> p g j", p=P, j=PACK))
+        nc.scalar.activation(weight_sb[:], weight_bf[:].rearrange("p g j -> p (g j)"), COPY)
         load_x(0, 2)
-        for g in range(G_K):
-            load_r(g)
+        load_r(0)
+        load_r(1)
         load_x(1)
-        load_y(0)
-        nc.sync.dma_start(
-            out=y_scale_sb[:], in_=y_scale.rearrange("(g p j) o -> p g (j o)", p=P, j=PACK)
-        )
-        nc.sync.dma_start(
-            out=weight_bf[:], in_=weight.rearrange("(g p j) -> p g j", p=P, j=PACK)
-        )
-        nc.sync.dma_start(
-            out=inv_bf[:, :, 0:1], in_=inv_score.rearrange("(m p o) -> p m o", p=P, o=1)
-        )
+        load_r(2)
         load_x(2)
+        load_r(3)
         load_x(3)
-        load_y(1)
-        for i in range(4, 8):
+        nc.sync.dma_start(out=y_scale_sb[:], in_=y_scale.rearrange("(g p j) o -> p g (j o)", p=P, j=PACK))
+        load_y(0)
+        load_x(4)
+        load_x(5)
+        nc.sync.dma_start(out=inv_bf[:, :, 0:1], in_=inv_score.rearrange("(m p o) -> p m o", p=P, o=1))
+        for g in range(1, G_S):
+            load_x(4 + 2 * g)
+            load_x(5 + 2 * g)
+            load_y(g)
+        for i in range(12, N_TILES):
             load_x(i)
-        load_y(2)
-        for i in range(8, 10):
-            load_x(i)
-        load_y(3)
-        for i in range(10, N_TILES):
-            load_x(i)
-
-        nc.vector.memset(warm[:], 0.0)
-        nc.scalar.activation(warm[:], warm[:], COPY)
 
         r_codes = keep.tile([P, G_K, C], U32, name="r_codes", align_bytes=64)
         r_scales = keep.tile([P, G_K, C], U8, name="r_scales", align_bytes=64)
-        y_codes = [keep.tile([P, A], U32, name=f"y_codes{g}", align_bytes=64) for g in range(G_S)]
-        y_scales = [keep.tile([P, A], U8, name=f"y_scales{g}", align_bytes=64) for g in range(G_S)]
+        y_codes = keep.tile([P, G_S * A], U32, name="y_codes", align_bytes=64)
+        y_scales = keep.tile([P, G_S * A], U8, name="y_scales", align_bytes=64)
         z_codes = [keep.tile([P, C], U32, name=f"z_codes{g}", align_bytes=64) for g in range(G_S)]
         z_scales = [keep.tile([P, C], U8, name=f"z_scales{g}", align_bytes=64) for g in range(G_S)]
 
@@ -113,36 +106,47 @@ def tile_pls_concentration_loadings_s7_kernel(
             return psum.tile([P, 512], F32, tag=f"bank{b}", name=name)
 
         def interleave(engine, dst, src):
-            dst = dst.rearrange("p (a i) j -> p a j i", i=4)
-            src = src.rearrange("p j (a i) -> p a j i", i=4)
-            if engine is nc.scalar:
-                nc.scalar.copy(out=dst, in_=src)
+            if engine is nc.gpsimd:
+                nc.gpsimd.tensor_scalar(
+                    out=dst, in0=src.rearrange("p j a -> p a j"),
+                    scalar1=1.0, scalar2=0.0, op0=MULT, op1=ADD,
+                )
             else:
-                nc.vector.tensor_copy(out=dst, in_=src)
+                dst = dst.rearrange("p (a i) j -> p a j i", i=4)
+                src = src.rearrange("p j (a i) -> p a j i", i=4)
+                if engine is nc.scalar:
+                    nc.scalar.copy(out=dst, in_=src)
+                else:
+                    nc.vector.tensor_copy(out=dst, in_=src)
+
+        def scale_out(engine, dst, src, factor):
+            if engine is nc.vector:
+                nc.vector.tensor_scalar(out=dst, in0=src, scalar1=factor, scalar2=None, op0=MULT)
+            else:
+                nc.scalar.activation(dst, src, COPY, scale=factor)
+
+        def quantise(codes, scales, grouped):
+            nc.vector.quantize_mx(out=codes.bitcast(FP8X4), scales=scales, in_=grouped)
 
         r_grouped = {}
 
         def interleave_r(g, c0, c1, engine):
             if g not in r_grouped:
-                r_grouped[g] = work.tile([P, C, PACK], BF16, tag="r_grouped", name="r_grouped", bufs=4, align_bytes=64)
+                r_grouped[g] = stage.tile([P, C, PACK], BF16, tag=("r_even", "r_odd", "r_even", "x_odd")[g], name=f"r_grouped{g}", align_bytes=64)
             interleave(engine, r_grouped[g][:, c0:c1, :], r_raw[g][:, :, c0:c1])
 
         def quantise_r(g):
-            nc.vector.quantize_mx(
-                out=r_codes[:, g, :].bitcast(FP8X4),
-                scales=r_scales[:, g, :],
-                in_=r_grouped[g][:].rearrange("p c j -> p (c j)"),
-            )
+            quantise(r_codes[:, g, :], r_scales[:, g, :], r_grouped[g][:].rearrange("p c j -> p (c j)"))
 
         x_banks = {}
         x_grouped = {}
         x_codes = {}
         x_scales = {}
 
-        def transpose_x(i):
+        def transpose_x(i, banks):
             words = x_raw[i][:].bitcast(F32)
             for b in range(2):
-                ps = bank(b, "x_turned")
+                ps = bank(banks[b], f"x_turned{i}{b}")
                 view = ps[:].rearrange("p (u g s) -> p u g s", u=2, g=2)
                 for gl in range(2):
                     g = 2 * b + gl
@@ -152,42 +156,39 @@ def tile_pls_concentration_loadings_s7_kernel(
                         )
                 x_banks[i, b] = ps
 
-        def centre_x(i, b):
-            if b == 0:
-                x_grouped[i] = work.tile(
-                    [P, G_K, P, 2, 2], BF16, tag="x_grouped", name="x_grouped", align_bytes=64
+        def centre_x(i):
+            tag = "y_slice" if i == 3 else ("x_even", "x_odd")[i % 2]
+            x_grouped[i] = stage.tile([P, G_K, P, 2, 2], BF16, tag=tag, name=f"x_grouped{i}", align_bytes=64)
+            for b in range(2):
+                nc.vector.tensor_tensor(
+                    out=x_grouped[i][:, 2 * b : 2 * b + 2],
+                    in0=x_banks[i, b][:].bitcast(BF16).rearrange(
+                        "p (u g s e) -> p g s u e", u=2, g=2, e=2
+                    ),
+                    in1=mean_sb[:, 2 * b : 2 * b + 2].unsqueeze(2).to_broadcast([P, 2, P, 2, 2]),
+                    op=SUB,
                 )
-            nc.vector.tensor_tensor(
-                out=x_grouped[i][:, 2 * b : 2 * b + 2],
-                in0=x_banks[i, b][:].bitcast(BF16).rearrange(
-                    "p (u g s e) -> p g s u e", u=2, g=2, e=2
-                ),
-                in1=mean_sb[:, 2 * b : 2 * b + 2].unsqueeze(2).to_broadcast([P, 2, P, 2, 2]),
-                op=SUB,
-            )
 
-        def quantise_x(i, b):
-            if b == 0:
-                x_codes[i] = work.tile([P, G_K * P], U32, tag="x_codes", name="x_codes", align_bytes=64)
-                x_scales[i] = work.tile([P, G_K * P], U8, tag="x_scales", name="x_scales", align_bytes=64)
-            cols = slice(256 * b, 256 * (b + 1))
+        def quantise_x(i, pieces=1):
+            x_codes[i] = work.tile([P, G_K * P], U32, tag="x_codes", name=f"x_codes{i}", bufs=5, align_bytes=64)
+            x_scales[i] = work.tile([P, G_K * P], U8, tag="x_scales", name=f"x_scales{i}", bufs=5, align_bytes=64)
             flat = x_grouped[i][:].rearrange("p g s u e -> p (g s u e)")
-            nc.vector.quantize_mx(
-                out=x_codes[i][:, cols].bitcast(FP8X4),
-                scales=x_scales[i][:, cols],
-                in_=flat[:, 1024 * b : 1024 * (b + 1)],
-            )
+            width = G_K * P // pieces
+            for n in range(pieces):
+                cols = slice(width * n, width * (n + 1))
+                quantise(x_codes[i][:, cols], x_scales[i][:, cols], flat[:, PACK * width * n : PACK * width * (n + 1)])
 
         t_banks = {}
         z_planes = {}
         z_grouped = {}
 
-        def multiply_t(i, b, c0, c1):
-            ps = bank(b, "t_sum")
-            for g in range(G_K):
+        def multiply_t(i, b, passes=range(G_K), c0=0, c1=C):
+            for g in passes:
+                if g == 0:
+                    t_banks[i, c0] = bank(b, f"t_sum{i}_{c0}")
                 cols = slice(P * g, P * (g + 1))
                 nc.tensor.matmul_mx(
-                    out=ps[:, : c1 - c0],
+                    out=t_banks[i, c0][:, : c1 - c0],
                     lhsT=x_codes[i][:, cols].bitcast(FP8X4),
                     lhsT_scale=x_scales[i][:, cols],
                     rhs=r_codes[:, g, c0:c1].bitcast(FP8X4),
@@ -195,189 +196,186 @@ def tile_pls_concentration_loadings_s7_kernel(
                     start=(g == 0),
                     stop=(g == G_K - 1),
                 )
-            t_banks[i, c0] = ps
 
-        def weigh_t(i, c0, c1):
+        def weigh_t(i, engine, c0=0, c1=C):
             g, j = i // PACK, i % PACK
             if g not in z_planes:
-                z_planes[g] = work.tile([P, PACK, C], BF16, tag="z_planes", name="z_planes", bufs=2, align_bytes=64)
-            nc.scalar.activation(
-                z_planes[g][:, j, c0:c1], t_banks[i, c0][:, : c1 - c0], COPY, scale=weight_sb[:, i : i + 1]
-            )
+                z_planes[g] = work.tile([P, PACK, C], BF16, tag="z_planes", name=f"z_planes{g}", align_bytes=64)
+            scale_out(engine, z_planes[g][:, j, c0:c1], t_banks[i, c0][:, : c1 - c0], weight_sb[:, i : i + 1])
 
         def interleave_z(g, c0, c1, engine):
             if g not in z_grouped:
-                z_grouped[g] = work.tile(
-                    [P, C, PACK], BF16, tag="z_grouped", name="z_grouped", bufs=2, align_bytes=64
-                )
+                z_grouped[g] = work.tile([P, C, PACK], BF16, tag="z_grouped", name=f"z_grouped{g}", align_bytes=64)
             interleave(engine, z_grouped[g][:, c0:c1, :], z_planes[g][:, :, c0:c1])
 
         def quantise_z(g, c0, c1):
-            nc.vector.quantize_mx(
-                out=z_codes[g][:, c0:c1].bitcast(FP8X4),
-                scales=z_scales[g][:, c0:c1],
-                in_=z_grouped[g][:].rearrange("p c j -> p (c j)")[:, PACK * c0 : PACK * c1],
+            quantise(
+                z_codes[g][:, c0:c1], z_scales[g][:, c0:c1],
+                z_grouped[g][:].rearrange("p c j -> p (c j)")[:, PACK * c0 : PACK * c1],
             )
 
         y_planes = {}
         y_grouped = {}
-        y_pooled = {}
 
-        def widen_y(g, h):
-            y_planes[g, h] = work.tile(
-                [P, PACK, HALF_A], BF16, tag="y_planes", name="y_planes", align_bytes=64
-            )
-            for j in range(PACK):
-                nc.scalar.activation(
-                    y_planes[g, h][:, j, :],
-                    y_raw[g][:, j, HALF_A * h : HALF_A * (h + 1)].bitcast(FP8),
-                    COPY,
-                    scale=y_scale_sb[:, g, j : j + 1],
-                )
+        def widen_y(n0, n1):
+            y_planes[n0] = work.tile([P, PACK, n1 - n0], BF16, tag="y_planes", name=f"y_planes{n0}", bufs=3, align_bytes=64)
+            for g in range(n0 // A, (n1 - 1) // A + 1):
+                lo, hi = max(n0, A * g), min(n1, A * (g + 1))
+                for j in range(PACK):
+                    nc.scalar.activation(
+                        y_planes[n0][:, j, lo - n0 : hi - n0], y_raw[g][:, j, lo - A * g : hi - A * g].bitcast(FP8), COPY,
+                        scale=y_scale_sb[:, g, j : j + 1],
+                    )
 
-        def interleave_y(g, h, a0, a1, engine):
-            if engine is nc.gpsimd:
-                t = work.tile([P, a1 - a0, PACK], BF16, tag="y_pooled", name="y_pooled", bufs=1, align_bytes=64)
-            elif (g, h) not in y_grouped:
-                t = work.tile([P, HALF_A, PACK], BF16, tag="y_grouped", name="y_grouped", align_bytes=64)
-                y_grouped[g, h] = t
-            else:
-                t = y_grouped[g, h]
-            src = y_planes[g, h][:, :, a0:a1]
-            if engine is nc.gpsimd:
-                nc.gpsimd.tensor_scalar(
-                    out=t[:], in0=src.rearrange("p j a -> p a j"),
-                    scalar1=1.0, scalar2=0.0, op0=MULT, op1=ADD,
-                )
-                y_pooled[g, h, a0] = t
-            else:
-                interleave(engine, t[:, a0:a1, :], src)
+        def interleave_y(n0, n1, b0, b1, engine, tag="y_slice"):
+            if n0 not in y_grouped:
+                y_grouped[n0] = stage.tile([P, n1 - n0, PACK], BF16, tag=tag, name=f"y_grouped{n0}", align_bytes=64)
+            interleave(engine, y_grouped[n0][:, b0:b1, :], y_planes[n0][:, :, b0:b1])
 
-        def quantise_y(g, h, a0, a1, pooled=False):
-            cols = slice(HALF_A * h + a0, HALF_A * h + a1)
-            if pooled:
-                src = y_pooled[g, h, a0][:]
-            else:
-                src = y_grouped[g, h][:, a0:a1, :]
-            nc.vector.quantize_mx(
-                out=y_codes[g][:, cols].bitcast(FP8X4),
-                scales=y_scales[g][:, cols],
-                in_=src.rearrange("p a j -> p (a j)"),
-            )
+        def quantise_y(n0, n1):
+            flat = y_grouped[n0][:].rearrange("p a j -> p (a j)")
+            done = 0
+            for width in (512, 256, 128, 64):
+                if n1 - n0 - done >= width:
+                    cols = slice(n0 + done, n0 + done + width)
+                    quantise(y_codes[:, cols], y_scales[:, cols], flat[:, PACK * done : PACK * (done + width)])
+                    done += width
 
         cov_banks = {}
 
-        def multiply_cov(m, h, g):
+        def multiply_cov(m, h, g, b=None):
             if g == 0:
-                b = 4 + m if h == 0 else m
-                cov_banks[m, h] = bank(b, "cov_sum")
+                cov_banks[m, h] = bank(b, f"cov_sum{m}{h}")
             c_cols = slice(P * m, P * (m + 1))
-            a_cols = slice(HALF_A * h, HALF_A * (h + 1))
+            a_cols = slice(A * g + HALF_A * h, A * g + HALF_A * (h + 1))
             nc.tensor.matmul_mx(
                 out=cov_banks[m, h][:],
                 lhsT=z_codes[g][:, c_cols].bitcast(FP8X4),
                 lhsT_scale=z_scales[g][:, c_cols],
-                rhs=y_codes[g][:, a_cols].bitcast(FP8X4),
-                rhs_scale=y_scales[g][:, a_cols],
+                rhs=y_codes[:, a_cols].bitcast(FP8X4),
+                rhs_scale=y_scales[:, a_cols],
                 start=(g == 0),
                 stop=(g == G_S - 1),
             )
 
         def store_cov(m, h, engine):
             res = keep.tile([P, HALF_A], F32, name=f"res{m}{h}")
-            if engine is nc.vector:
-                nc.vector.tensor_scalar(
-                    out=res[:], in0=cov_banks[m, h][:], scalar1=inv_sb[:, m : m + 1],
-                    scalar2=None, op0=MULT,
-                )
-            else:
-                nc.scalar.activation(res[:], cov_banks[m, h][:], COPY, scale=inv_sb[:, m : m + 1])
+            scale_out(engine, res[:], cov_banks[m, h][:], inv_sb[:, m : m + 1])
             nc.sync.dma_start(
                 out=out[P * m : P * (m + 1), HALF_A * h : HALF_A * (h + 1)], in_=res[:]
             )
 
-        chunks = [(0, 0), (1, 0), (0, 1), (2, 0), (1, 1), (3, 0), (2, 1), (3, 1)]
         last = G_S - 1
+        widths = [256, 320, 320] * 4 + [256, 256]
+        slices = [(sum(widths[:n]), sum(widths[: n + 1])) for n in range(len(widths))]
+        first_slice_step = 4
 
-        idle = bank(7, "idle")
-        for n in range(3):
-            nc.tensor.matmul(idle[:], lhsT=zeros[:, :P], rhs=zeros[:], start=True, stop=True)
-        transpose_x(0)
-        interleave_r(0, 0, C, nc.scalar)
-        interleave_r(2, 0, C, nc.scalar)
-        for i in range(N_TILES):
-            n, piece = (i - 2) // 2, (i - 2) % 2
-            if i > 1:
-                interleave_y(*chunks[n], 128 * piece, 128 * (piece + 1), nc.gpsimd)
-            centre_x(i, 0)
-            centre_x(i, 1)
-            if i > 2 and i % 2 == 1 and i < 15:
-                quantise_y(*chunks[(i - 3) // 2], 256, HALF_A)
-            quantise_x(i, 0)
-            quantise_x(i, 1)
-            if i == 1:
-                nc.vector.tensor_copy(
-                    out=weight_sb[:], in_=weight_bf[:].rearrange("p g j -> p (g j)")
-                )
-                nc.vector.tensor_copy(out=inv_sb[:], in_=inv_bf[:, :, 0])
-            if i + 1 < N_TILES:
-                transpose_x(i + 1)
-            if i == 0:
-                interleave_r(1, 0, C, nc.vector)
-                quantise_r(0)
-                quantise_r(1)
-                interleave_r(3, 384, C, nc.scalar)
-                interleave_r(3, 0, 384, nc.vector)
-                quantise_r(2)
-                quantise_r(3)
-            if i + 1 < N_TILES:
-                multiply_t(i, 2 + i % 2, 0, C)
+        transpose_x(0, (0, 1))
+        centre_x(0)
+        quantise_x(0, 2)
+        interleave_r(0, 0, HALF_C, nc.scalar)
+        interleave_r(0, HALF_C, C, nc.vector)
+        interleave_r(1, 0, HALF_C, nc.scalar)
+        interleave_r(1, HALF_C, C, nc.vector)
+        quantise_r(0)
+        quantise_r(1)
+        transpose_x(1, (2, 3))
+        interleave_r(2, 0, Y_POOL, nc.gpsimd)
+        interleave_r(2, Y_POOL, C, nc.scalar)
+        centre_x(1)
+        quantise_x(1, 2)
+        quantise_r(2)
+        multiply_t(0, 4, [0, 1])
+        transpose_x(2, (0, 1))
+        multiply_t(1, 5, [0, 1])
+        interleave_r(3, 0, Y_POOL, nc.gpsimd)
+        interleave_r(3, Y_POOL, C, nc.scalar)
+        centre_x(2)
+        quantise_r(3)
+        quantise_x(2, 2)
+        multiply_t(0, None, [2])
+        multiply_t(1, None, [2])
+        widen_y(*slices[0])
+        widen_y(*slices[1])
+
+        def z_piece(n):
+            return n // PACK, P * (n % PACK), P * (n % PACK + 1)
+
+        def z_pieces(i):
+            return [] if i < 6 else [i - 6]
+
+        for i in range(3, N_TILES):
+            use = 2 * i if i < 10 else 3 * i - 10
+            s = i - first_slice_step
+            pooled = Y_POOL if s > 0 else widths[0]
+            transpose_x(i, (use % 4, (use + 1) % 4))
+            if s >= 0:
+                interleave_y(*slices[s], 0, pooled, nc.gpsimd)
+            centre_x(i)
+            if i == 3:
+                multiply_t(0, None, [3])
+                multiply_t(1, None, [3])
             else:
-                for m in range(4):
-                    multiply_cov(m, 0, 2)
-                multiply_t(i, 3, 0, 256)
-                multiply_t(i, 1, 256, C)
-            if i % PACK == 1 and i > 1:
-                interleave_z(i // PACK - 1, 384, C, nc.scalar)
-                interleave_z(i // PACK - 1, 0, 384, nc.vector)
-            if i % PACK == 2 and i > 2:
-                quantise_z(i // PACK - 1, 0, C)
-            if i % 2 == 1 and i < 15:
-                widen_y(*chunks[(i - 1) // 2])
-            elif i % 2 == 0 and i > 0:
-                interleave_y(*chunks[(i - 2) // 2], 256, HALF_A, nc.scalar)
-            if i == 14:
-                widen_y(*chunks[7])
-            if i > 0:
-                weigh_t(i - 1, 0, C)
-            if i + 1 == N_TILES:
-                weigh_t(i, 0, 256)
-                weigh_t(i, 256, C)
-            if i > 1:
-                quantise_y(*chunks[n], 128 * piece, 128 * (piece + 1), pooled=True)
-            if i in (7, 8, 9, 10, 11, 12, 13, 14):
-                multiply_cov((i - 7) % PACK, 0, (i - 7) // PACK)
+                multiply_t(i - 2, 4 + (i - 2) % 4 if i < 10 else (use + 2) % 4)
+            if i == 4:
+                weigh_t(0, nc.vector)
+                weigh_t(1, nc.vector)
+            if i > 4:
+                weigh_t(i - 3, nc.scalar)
+            if s > 0:
+                interleave_y(*slices[s], pooled, widths[s], nc.scalar)
+            if 0 <= s < len(slices) - 2:
+                widen_y(*slices[s + 2])
+            if i + 1 == N_TILES or i < 4:
+                quantise_x(i, 2)
+            for n in z_pieces(i):
+                interleave_z(*z_piece(n), nc.vector)
+            for n in z_pieces(i - 1):
+                quantise_z(*z_piece(n))
+            if s >= 0:
+                quantise_y(*slices[s])
+            if 4 <= i < N_TILES - 1:
+                quantise_x(i)
+            for n in z_pieces(i - 2):
+                multiply_cov(n % PACK, 0, n // PACK, 4 + n % PACK)
+        nc.scalar.copy(out=inv_sb[:], in_=inv_bf[:, :, 0])
 
-        quantise_y(2, 1, 256, HALF_A)
-        interleave_y(3, 1, 0, 128, nc.gpsimd)
-        interleave_y(3, 1, 320, HALF_A, nc.scalar)
-        interleave_y(3, 1, 128, 320, nc.vector)
-        quantise_y(3, 1, 0, 128, pooled=True)
-        for m in (0, 2):
-            for g in range(G_S - 1):
-                multiply_cov(m, 1, g)
-        interleave_z(last, 0, 256, nc.vector)
-        quantise_y(3, 1, 128, 256)
-        interleave_z(last, 256, C, nc.vector)
-        quantise_z(last, 0, 256)
-        quantise_z(last, 256, C)
-        quantise_y(3, 1, 256, HALF_A)
-        for m in range(4):
+        multiply_t(14, 2)
+        multiply_t(15, 3, c1=HALF_C)
+        multiply_t(15, 0, c0=HALF_C)
+        weigh_t(13, nc.scalar)
+        interleave_y(*slices[12], 0, 256, nc.scalar, "r_odd")
+        weigh_t(14, nc.scalar)
+        weigh_t(15, nc.scalar, c1=HALF_C)
+        weigh_t(15, nc.scalar, c0=HALF_C)
+        interleave_z(2, HALF_C, C, nc.vector)
+        quantise_z(*z_piece(9))
+        quantise_z(2, HALF_C, C)
+        quantise_y(*slices[12])
+        interleave_z(3, 0, HALF_C, nc.vector)
+        interleave_z(3, 384, C, nc.scalar)
+        interleave_y(*slices[13], 0, 256, nc.scalar, "r_even")
+        interleave_z(3, HALF_C, 384, nc.vector)
+        quantise_z(3, 0, HALF_C)
+        quantise_z(3, HALF_C, C)
+        for m in range(2):
+            multiply_cov(m, 1, 0, m + 1)
+            multiply_cov(m, 1, 1)
+        for m in range(2):
+            multiply_cov(m, 0, 2)
+            multiply_cov(m, 1, 2)
+        for m in range(2):
             multiply_cov(m, 0, last)
-            store_cov(m, 0, nc.vector if m % 2 else nc.scalar)
-        for m in (3, 1):
-            for g in range(G_S - 1):
-                multiply_cov(m, 1, g)
-        for m in (0, 2, 3, 1):
+            store_cov(m, 0, nc.scalar if m % 2 else nc.vector)
+        quantise_y(*slices[13])
+        for m in range(2, 4):
+            multiply_cov(m, 0, 2)
+            multiply_cov(m, 0, last)
+            store_cov(m, 0, nc.scalar if m % 2 else nc.vector)
+        for m in range(2):
             multiply_cov(m, 1, last)
-            store_cov(m, 1, nc.vector if m in (2, 1) else nc.scalar)
+            store_cov(m, 1, nc.vector if m % 2 else nc.scalar)
+        for m in range(2, 4):
+            for g in range(G_S):
+                multiply_cov(m, 1, g, (m + 1) % 4)
+            store_cov(m, 1, nc.vector if m % 2 else nc.scalar)

@@ -77,23 +77,30 @@ def tile_pls_concentration_loadings_s7_kernel(
         nc.scalar.activation(weight_sb[:], weight_bf[:].rearrange("p g j -> p (g j)"), COPY)
         load_x(0, 2)
         load_r(0)
-        load_r(1)
         load_x(1)
-        load_r(2)
+        load_r(1)
         load_x(2)
-        load_r(3)
+        load_r(2)
         load_x(3)
+        load_r(3)
         nc.sync.dma_start(out=y_scale_sb[:], in_=y_scale.rearrange("(g p j) o -> p g (j o)", p=P, j=PACK))
         load_y(0)
         load_x(4)
         load_x(5)
         nc.sync.dma_start(out=inv_bf[:, :, 0:1], in_=inv_score.rearrange("(m p o) -> p m o", p=P, o=1))
-        for g in range(1, G_S):
-            load_x(4 + 2 * g)
-            load_x(5 + 2 * g)
-            load_y(g)
-        for i in range(12, N_TILES):
-            load_x(i)
+        load_x(6)
+        load_x(7)
+        load_y(1)
+        load_x(8)
+        load_x(9)
+        load_y(2)
+        load_x(10)
+        load_x(11)
+        load_y(3)
+        load_x(12)
+        load_x(13)
+        load_x(14)
+        load_x(15)
 
         r_codes = keep.tile([P, G_K, C], U32, name="r_codes", align_bytes=64)
         r_scales = keep.tile([P, G_K, C], U8, name="r_scales", align_bytes=64)
@@ -128,11 +135,17 @@ def tile_pls_concentration_loadings_s7_kernel(
         def quantise(codes, scales, grouped):
             nc.vector.quantize_mx(out=codes.bitcast(FP8X4), scales=scales, in_=grouped)
 
+        def warm_up(src, count):
+            idle = bank(7, "idle")
+            flat = src[:].rearrange("p j c -> p (j c)")
+            for n in range(count):
+                nc.tensor.matmul(idle[:], lhsT=flat[:, :P], rhs=flat[:, :512], start=True, stop=True)
+
         r_grouped = {}
 
         def interleave_r(g, c0, c1, engine):
             if g not in r_grouped:
-                r_grouped[g] = stage.tile([P, C, PACK], BF16, tag=("r_even", "r_odd", "r_even", "x_odd")[g], name=f"r_grouped{g}", align_bytes=64)
+                r_grouped[g] = stage.tile([P, C, PACK], BF16, tag=("tail_a", "x_even", "x_odd", "tail_a")[g], name=f"r_grouped{g}", align_bytes=64)
             interleave(engine, r_grouped[g][:, c0:c1, :], r_raw[g][:, :, c0:c1])
 
         def quantise_r(g):
@@ -157,7 +170,7 @@ def tile_pls_concentration_loadings_s7_kernel(
                 x_banks[i, b] = ps
 
         def centre_x(i):
-            tag = "y_slice" if i == 3 else ("x_even", "x_odd")[i % 2]
+            tag = {2: "tail_a", 3: "y_slice"}.get(i, ("x_even", "x_odd")[i % 2])
             x_grouped[i] = stage.tile([P, G_K, P, 2, 2], BF16, tag=tag, name=f"x_grouped{i}", align_bytes=64)
             for b in range(2):
                 nc.vector.tensor_tensor(
@@ -243,27 +256,25 @@ def tile_pls_concentration_loadings_s7_kernel(
 
         cov_banks = {}
 
-        def multiply_cov(m, h, g, b=None):
+        def multiply_cov(m, a0, g, b=None, width=HALF_A):
             if g == 0:
-                cov_banks[m, h] = bank(b, f"cov_sum{m}{h}")
+                cov_banks[m, a0] = bank(b, f"cov_sum{m}_{a0}")
             c_cols = slice(P * m, P * (m + 1))
-            a_cols = slice(A * g + HALF_A * h, A * g + HALF_A * (h + 1))
+            n_cols = slice(A * g + a0, A * g + a0 + width)
             nc.tensor.matmul_mx(
-                out=cov_banks[m, h][:],
+                out=cov_banks[m, a0][:, :width],
                 lhsT=z_codes[g][:, c_cols].bitcast(FP8X4),
                 lhsT_scale=z_scales[g][:, c_cols],
-                rhs=y_codes[:, a_cols].bitcast(FP8X4),
-                rhs_scale=y_scales[:, a_cols],
+                rhs=y_codes[:, n_cols].bitcast(FP8X4),
+                rhs_scale=y_scales[:, n_cols],
                 start=(g == 0),
                 stop=(g == G_S - 1),
             )
 
-        def store_cov(m, h, engine):
-            res = keep.tile([P, HALF_A], F32, name=f"res{m}{h}")
-            scale_out(engine, res[:], cov_banks[m, h][:], inv_sb[:, m : m + 1])
-            nc.sync.dma_start(
-                out=out[P * m : P * (m + 1), HALF_A * h : HALF_A * (h + 1)], in_=res[:]
-            )
+        def store_cov(m, a0, engine, width=HALF_A):
+            res = keep.tile([P, width], F32, name=f"res{m}_{a0}")
+            scale_out(engine, res[:], cov_banks[m, a0][:, :width], inv_sb[:, m : m + 1])
+            nc.sync.dma_start(out=out[P * m : P * (m + 1), a0 : a0 + width], in_=res[:])
 
         last = G_S - 1
         widths = [256, 320, 320] * 4 + [256, 256]
@@ -272,29 +283,35 @@ def tile_pls_concentration_loadings_s7_kernel(
 
         transpose_x(0, (0, 1))
         centre_x(0)
+        interleave_r(0, 0, 256, nc.scalar)
+        interleave_r(0, 256, 512, nc.vector)
         quantise_x(0, 2)
-        interleave_r(0, 0, HALF_C, nc.scalar)
-        interleave_r(0, HALF_C, C, nc.vector)
-        interleave_r(1, 0, HALF_C, nc.scalar)
-        interleave_r(1, HALF_C, C, nc.vector)
         quantise_r(0)
-        quantise_r(1)
         transpose_x(1, (2, 3))
-        interleave_r(2, 0, Y_POOL, nc.gpsimd)
-        interleave_r(2, Y_POOL, C, nc.scalar)
+        multiply_t(0, 4, [0])
+        interleave_r(1, 0, 176, nc.gpsimd)
+        interleave_r(1, 176, 512, nc.scalar)
         centre_x(1)
         quantise_x(1, 2)
-        quantise_r(2)
-        multiply_t(0, 4, [0, 1])
+        quantise_r(1)
         transpose_x(2, (0, 1))
-        multiply_t(1, 5, [0, 1])
-        interleave_r(3, 0, Y_POOL, nc.gpsimd)
-        interleave_r(3, Y_POOL, C, nc.scalar)
+        multiply_t(1, 5, [0])
+        multiply_t(0, 4, [1])
+        multiply_t(1, 5, [1])
+        interleave_r(2, 0, 176, nc.gpsimd)
+        interleave_r(2, 176, 512, nc.scalar)
         centre_x(2)
-        quantise_r(3)
         quantise_x(2, 2)
-        multiply_t(0, None, [2])
-        multiply_t(1, None, [2])
+        quantise_r(2)
+        transpose_x(3, (2, 3))
+        multiply_t(0, 4, [2])
+        multiply_t(1, 5, [2])
+        multiply_t(2, 6, [0, 1, 2])
+        interleave_r(3, 0, 176, nc.gpsimd)
+        interleave_r(3, 176, 512, nc.scalar)
+        centre_x(3)
+        quantise_x(3, 2)
+        quantise_r(3)
         widen_y(*slices[0])
         widen_y(*slices[1])
 
@@ -304,7 +321,7 @@ def tile_pls_concentration_loadings_s7_kernel(
         def z_pieces(i):
             return [] if i < 6 else [i - 6]
 
-        for i in range(3, N_TILES):
+        for i in range(4, N_TILES):
             use = 2 * i if i < 10 else 3 * i - 10
             s = i - first_slice_step
             pooled = Y_POOL if s > 0 else widths[0]
@@ -312,9 +329,9 @@ def tile_pls_concentration_loadings_s7_kernel(
             if s >= 0:
                 interleave_y(*slices[s], 0, pooled, nc.gpsimd)
             centre_x(i)
-            if i == 3:
-                multiply_t(0, None, [3])
-                multiply_t(1, None, [3])
+            if i == 4:
+                for n in range(3):
+                    multiply_t(n, None, [3])
             else:
                 multiply_t(i - 2, 4 + (i - 2) % 4 if i < 10 else (use + 2) % 4)
             if i == 4:
@@ -326,7 +343,7 @@ def tile_pls_concentration_loadings_s7_kernel(
                 interleave_y(*slices[s], pooled, widths[s], nc.scalar)
             if 0 <= s < len(slices) - 2:
                 widen_y(*slices[s + 2])
-            if i + 1 == N_TILES or i < 4:
+            if i + 1 == N_TILES:
                 quantise_x(i, 2)
             for n in z_pieces(i):
                 interleave_z(*z_piece(n), nc.vector)
@@ -334,9 +351,9 @@ def tile_pls_concentration_loadings_s7_kernel(
                 quantise_z(*z_piece(n))
             if s >= 0:
                 quantise_y(*slices[s])
-            if 4 <= i < N_TILES - 1:
+            if i < N_TILES - 1:
                 quantise_x(i)
-            for n in z_pieces(i - 2):
+            for n in z_pieces(i - 2) if i < 12 else []:
                 multiply_cov(n % PACK, 0, n // PACK, 4 + n % PACK)
         nc.scalar.copy(out=inv_sb[:], in_=inv_bf[:, :, 0])
 
@@ -344,38 +361,31 @@ def tile_pls_concentration_loadings_s7_kernel(
         multiply_t(15, 3, c1=HALF_C)
         multiply_t(15, 0, c0=HALF_C)
         weigh_t(13, nc.scalar)
-        interleave_y(*slices[12], 0, 256, nc.scalar, "r_odd")
         weigh_t(14, nc.scalar)
         weigh_t(15, nc.scalar, c1=HALF_C)
         weigh_t(15, nc.scalar, c0=HALF_C)
         interleave_z(2, HALF_C, C, nc.vector)
         quantise_z(*z_piece(9))
         quantise_z(2, HALF_C, C)
-        quantise_y(*slices[12])
         interleave_z(3, 0, HALF_C, nc.vector)
         interleave_z(3, 384, C, nc.scalar)
-        interleave_y(*slices[13], 0, 256, nc.scalar, "r_even")
+        interleave_y(*slices[-2], 0, 256, nc.scalar, "tail_a")
         interleave_z(3, HALF_C, 384, nc.vector)
         quantise_z(3, 0, HALF_C)
         quantise_z(3, HALF_C, C)
-        for m in range(2):
-            multiply_cov(m, 1, 0, m + 1)
-            multiply_cov(m, 1, 1)
-        for m in range(2):
-            multiply_cov(m, 0, 2)
-            multiply_cov(m, 1, 2)
-        for m in range(2):
-            multiply_cov(m, 0, last)
-            store_cov(m, 0, nc.scalar if m % 2 else nc.vector)
-        quantise_y(*slices[13])
-        for m in range(2, 4):
-            multiply_cov(m, 0, 2)
-            multiply_cov(m, 0, last)
-            store_cov(m, 0, nc.scalar if m % 2 else nc.vector)
-        for m in range(2):
-            multiply_cov(m, 1, last)
-            store_cov(m, 1, nc.vector if m % 2 else nc.scalar)
-        for m in range(2, 4):
+        interleave_y(*slices[-1], 0, 256, nc.vector, "tail_b")
+        for n in range(4, 16):
+            multiply_cov(n % PACK, 0, n // PACK)
+            if n // PACK == last:
+                store_cov(n % PACK, 0, nc.scalar if n % 2 else nc.vector)
+            if n == 12:
+                quantise_y(*slices[-2])
+                quantise_y(*slices[-1])
+        for m in range(3):
             for g in range(G_S):
-                multiply_cov(m, 1, g, (m + 1) % 4)
-            store_cov(m, 1, nc.vector if m % 2 else nc.scalar)
+                multiply_cov(m, HALF_A, g, m + 1)
+            store_cov(m, HALF_A, nc.vector if m % 2 else nc.scalar)
+        for a0, b, engine in ((512, 0, nc.vector), (768, 4, nc.scalar)):
+            for g in range(G_S):
+                multiply_cov(3, a0, g, b, 256)
+            store_cov(3, a0, engine, 256)

@@ -66,15 +66,13 @@ def tile_pls_concentration_loadings_s7_kernel(
         def load_r(g):
             nc.sync.dma_start(out=r_raw[g][:], in_=r_hbm[g])
 
-        def load_y(g):
-            nc.sync.dma_start(out=y_raw[g][:], in_=y_hbm[g])
+        def load_y(g, a0=0, a1=A):
+            nc.sync.dma_start(out=y_raw[g][:, :, a0:a1], in_=y_hbm[g][:, :, a0:a1])
 
         nc.scalar.dma_start(
             out=mean_sb[:].rearrange("p g u e -> p g (u e)"),
             in_=mean.rearrange("(g p t) -> p g t", p=P, t=PACK),
         )
-        nc.scalar.dma_start(out=weight_bf[:], in_=weight.rearrange("(g p j) -> p g j", p=P, j=PACK))
-        nc.scalar.activation(weight_sb[:], weight_bf[:].rearrange("p g j -> p (g j)"), COPY)
         load_x(0, 2)
         load_r(0)
         load_x(1)
@@ -84,8 +82,10 @@ def tile_pls_concentration_loadings_s7_kernel(
         load_x(3)
         load_r(3)
         nc.sync.dma_start(out=y_scale_sb[:], in_=y_scale.rearrange("(g p j) o -> p g (j o)", p=P, j=PACK))
-        load_y(0)
+        nc.sync.dma_start(out=weight_bf[:], in_=weight.rearrange("(g p j) -> p g j", p=P, j=PACK))
+        load_y(0, 0, 256)
         load_x(4)
+        load_y(0, 256, 1024)
         load_x(5)
         nc.sync.dma_start(out=inv_bf[:, :, 0:1], in_=inv_score.rearrange("(m p o) -> p m o", p=P, o=1))
         load_x(6)
@@ -122,7 +122,7 @@ def tile_pls_concentration_loadings_s7_kernel(
                 dst = dst.rearrange("p (a i) j -> p a j i", i=4)
                 src = src.rearrange("p j (a i) -> p a j i", i=4)
                 if engine is nc.scalar:
-                    nc.scalar.copy(out=dst, in_=src)
+                    nc.scalar.activation(dst, src, COPY)
                 else:
                     nc.vector.tensor_copy(out=dst, in_=src)
 
@@ -313,6 +313,7 @@ def tile_pls_concentration_loadings_s7_kernel(
         quantise_x(3, 2)
         quantise_r(3)
         widen_y(*slices[0])
+        nc.scalar.copy(out=weight_sb[:], in_=weight_bf[:].rearrange("p g j -> p (g j)"))
         widen_y(*slices[1])
 
         def z_piece(n):
@@ -341,7 +342,7 @@ def tile_pls_concentration_loadings_s7_kernel(
                 weigh_t(i - 3, nc.scalar)
             if s > 0:
                 interleave_y(*slices[s], pooled, widths[s], nc.scalar)
-            if 0 <= s < len(slices) - 2:
+            if 0 <= s < len(slices) - 3:
                 widen_y(*slices[s + 2])
             if i + 1 == N_TILES:
                 quantise_x(i, 2)
@@ -353,7 +354,7 @@ def tile_pls_concentration_loadings_s7_kernel(
                 quantise_y(*slices[s])
             if i < N_TILES - 1:
                 quantise_x(i)
-            for n in z_pieces(i - 2) if i < 12 else []:
+            for n in z_pieces(i - 2) if i < 14 else []:
                 multiply_cov(n % PACK, 0, n // PACK, 4 + n % PACK)
         nc.scalar.copy(out=inv_sb[:], in_=inv_bf[:, :, 0])
 
@@ -364,27 +365,41 @@ def tile_pls_concentration_loadings_s7_kernel(
         weigh_t(14, nc.scalar)
         weigh_t(15, nc.scalar, c1=HALF_C)
         weigh_t(15, nc.scalar, c0=HALF_C)
-        interleave_z(2, HALF_C, C, nc.vector)
-        quantise_z(*z_piece(9))
-        quantise_z(2, HALF_C, C)
-        interleave_z(3, 0, HALF_C, nc.vector)
-        interleave_z(3, 384, C, nc.scalar)
         interleave_y(*slices[-2], 0, 256, nc.scalar, "tail_a")
-        interleave_z(3, HALF_C, 384, nc.vector)
+        widen_y(*slices[-1])
+        quantise_z(*z_piece(9))
+        interleave_z(2, HALF_C, C, nc.vector)
+        interleave_z(3, 0, HALF_C, nc.vector)
+        quantise_z(2, HALF_C, C)
         quantise_z(3, 0, HALF_C)
+        interleave_z(3, HALF_C, C, nc.vector)
+        quantise_y(*slices[-2])
         quantise_z(3, HALF_C, C)
-        interleave_y(*slices[-1], 0, 256, nc.vector, "tail_b")
-        for n in range(4, 16):
+        for n in range(6, 10):
             multiply_cov(n % PACK, 0, n // PACK)
-            if n // PACK == last:
-                store_cov(n % PACK, 0, nc.scalar if n % 2 else nc.vector)
-            if n == 12:
-                quantise_y(*slices[-2])
-                quantise_y(*slices[-1])
-        for m in range(3):
-            for g in range(G_S):
+        for m in range(2):
+            for g in range(2):
                 multiply_cov(m, HALF_A, g, m + 1)
-            store_cov(m, HALF_A, nc.vector if m % 2 else nc.scalar)
+        for m in range(2):
+            multiply_cov(m, 0, last)
+            store_cov(m, 0, nc.scalar if m else nc.vector)
+        interleave_y(*slices[-1], 0, 256, nc.vector, "tail_b")
+        quantise_y(*slices[-1])
+        for m in range(2, 4):
+            multiply_cov(m, 0, 2)
+        for m in range(2):
+            multiply_cov(m, HALF_A, 2)
+        for m in range(2, 4):
+            multiply_cov(m, 0, last)
+            store_cov(m, 0, nc.vector if m % 2 else nc.scalar)
+        multiply_cov(2, HALF_A, 0, 3)
+        multiply_cov(2, HALF_A, 1)
+        for m in range(2):
+            multiply_cov(m, HALF_A, last)
+            store_cov(m, HALF_A, nc.vector if m else nc.scalar)
+        multiply_cov(2, HALF_A, 2)
+        multiply_cov(2, HALF_A, last)
+        store_cov(2, HALF_A, nc.scalar)
         for a0, b, engine in ((512, 0, nc.vector), (768, 4, nc.scalar)):
             for g in range(G_S):
                 multiply_cov(3, a0, g, b, 256)

@@ -13,6 +13,8 @@ N_TILES = S // P
 HALF_A = A // 2
 HALF_C = C // 2
 Y_POOL = 176
+Y_POOL_PAIR = 400
+Z_SCALAR = 0
 
 FLOPS = 2 * S * K * C + 2 * S * C * A
 
@@ -87,16 +89,16 @@ def tile_pls_concentration_loadings_s7_kernel(
         load_x(4)
         load_y(0, 256, 1024)
         load_x(5)
-        nc.sync.dma_start(out=inv_bf[:, :, 0:1], in_=inv_score.rearrange("(m p o) -> p m o", p=P, o=1))
         load_x(6)
-        load_x(7)
         load_y(1)
+        nc.sync.dma_start(out=inv_bf[:, :, 0:1], in_=inv_score.rearrange("(m p o) -> p m o", p=P, o=1))
+        load_x(7)
         load_x(8)
-        load_x(9)
         load_y(2)
+        load_x(9)
         load_x(10)
-        load_x(11)
         load_y(3)
+        load_x(11)
         load_x(12)
         load_x(13)
         load_x(14)
@@ -135,12 +137,6 @@ def tile_pls_concentration_loadings_s7_kernel(
         def quantise(codes, scales, grouped):
             nc.vector.quantize_mx(out=codes.bitcast(FP8X4), scales=scales, in_=grouped)
 
-        def warm_up(src, count):
-            idle = bank(7, "idle")
-            flat = src[:].rearrange("p j c -> p (j c)")
-            for n in range(count):
-                nc.tensor.matmul(idle[:], lhsT=flat[:, :P], rhs=flat[:, :512], start=True, stop=True)
-
         r_grouped = {}
 
         def interleave_r(g, c0, c1, engine):
@@ -169,27 +165,34 @@ def tile_pls_concentration_loadings_s7_kernel(
                         )
                 x_banks[i, b] = ps
 
-        def centre_x(i):
-            tag = {2: "tail_a", 3: "y_slice"}.get(i, ("x_even", "x_odd")[i % 2])
-            x_grouped[i] = stage.tile([P, G_K, P, 2, 2], BF16, tag=tag, name=f"x_grouped{i}", align_bytes=64)
-            for b in range(2):
-                nc.vector.tensor_tensor(
-                    out=x_grouped[i][:, 2 * b : 2 * b + 2],
-                    in0=x_banks[i, b][:].bitcast(BF16).rearrange(
-                        "p (u g s e) -> p g s u e", u=2, g=2, e=2
-                    ),
-                    in1=mean_sb[:, 2 * b : 2 * b + 2].unsqueeze(2).to_broadcast([P, 2, P, 2, 2]),
-                    op=SUB,
-                )
+        def centre_x(first, count=1):
+            tag = {2: "tail_a", 3: "y_slice"}.get(first, ("x_even", "x_odd")[len(x_grouped) % 2])
+            x_grouped[first] = stage.tile(
+                [P, count, G_K, P, 2, 2], BF16, tag=tag, name=f"x_grouped{first}", align_bytes=64
+            )
+            for n in range(count):
+                for b in range(2):
+                    nc.vector.tensor_tensor(
+                        out=x_grouped[first][:, n, 2 * b : 2 * b + 2],
+                        in0=x_banks[first + n, b][:].bitcast(BF16).rearrange(
+                            "p (u g s e) -> p g s u e", u=2, g=2, e=2
+                        ),
+                        in1=mean_sb[:, 2 * b : 2 * b + 2].unsqueeze(2).to_broadcast([P, 2, P, 2, 2]),
+                        op=SUB,
+                    )
 
-        def quantise_x(i, pieces=1):
-            x_codes[i] = work.tile([P, G_K * P], U32, tag="x_codes", name=f"x_codes{i}", bufs=5, align_bytes=64)
-            x_scales[i] = work.tile([P, G_K * P], U8, tag="x_scales", name=f"x_scales{i}", bufs=5, align_bytes=64)
-            flat = x_grouped[i][:].rearrange("p g s u e -> p (g s u e)")
-            width = G_K * P // pieces
+        def quantise_x(first, pieces=1, count=1):
+            words = count * G_K * P
+            codes = work.tile([P, words], U32, tag="x_codes", name=f"x_codes{first}", bufs=4, align_bytes=64)
+            scales = work.tile([P, words], U8, tag="x_scales", name=f"x_scales{first}", bufs=4, align_bytes=64)
+            flat = x_grouped[first][:].rearrange("p n g s u e -> p (n g s u e)")
+            width = words // pieces
             for n in range(pieces):
                 cols = slice(width * n, width * (n + 1))
-                quantise(x_codes[i][:, cols], x_scales[i][:, cols], flat[:, PACK * width * n : PACK * width * (n + 1)])
+                quantise(codes[:, cols], scales[:, cols], flat[:, PACK * width * n : PACK * width * (n + 1)])
+            for n in range(count):
+                x_codes[first + n] = codes[:, G_K * P * n : G_K * P * (n + 1)]
+                x_scales[first + n] = scales[:, G_K * P * n : G_K * P * (n + 1)]
 
         t_banks = {}
         z_planes = {}
@@ -245,14 +248,10 @@ def tile_pls_concentration_loadings_s7_kernel(
                 y_grouped[n0] = stage.tile([P, n1 - n0, PACK], BF16, tag=tag, name=f"y_grouped{n0}", align_bytes=64)
             interleave(engine, y_grouped[n0][:, b0:b1, :], y_planes[n0][:, :, b0:b1])
 
-        def quantise_y(n0, n1):
+        def quantise_y(n0, b0, b1):
             flat = y_grouped[n0][:].rearrange("p a j -> p (a j)")
-            done = 0
-            for width in (512, 256, 128, 64):
-                if n1 - n0 - done >= width:
-                    cols = slice(n0 + done, n0 + done + width)
-                    quantise(y_codes[:, cols], y_scales[:, cols], flat[:, PACK * done : PACK * (done + width)])
-                    done += width
+            cols = slice(n0 + b0, n0 + b1)
+            quantise(y_codes[:, cols], y_scales[:, cols], flat[:, PACK * b0 : PACK * b1])
 
         cov_banks = {}
 
@@ -277,9 +276,8 @@ def tile_pls_concentration_loadings_s7_kernel(
             nc.sync.dma_start(out=out[P * m : P * (m + 1), a0 : a0 + width], in_=res[:])
 
         last = G_S - 1
-        widths = [256, 320, 320] * 4 + [256, 256]
+        widths = [256, 640, 576, 640, 576, 640, 256, 256, 256]
         slices = [(sum(widths[:n]), sum(widths[: n + 1])) for n in range(len(widths))]
-        first_slice_step = 4
 
         transpose_x(0, (0, 1))
         centre_x(0)
@@ -316,75 +314,83 @@ def tile_pls_concentration_loadings_s7_kernel(
         nc.scalar.copy(out=weight_sb[:], in_=weight_bf[:].rearrange("p g j -> p (g j)"))
         widen_y(*slices[1])
 
-        def z_piece(n):
-            return n // PACK, P * (n % PACK), P * (n % PACK + 1)
+        transpose_x(4, (0, 1))
+        interleave_y(*slices[0], 0, widths[0], nc.gpsimd)
+        centre_x(4)
+        for n in range(3):
+            multiply_t(n, None, [3])
+        weigh_t(0, nc.vector)
+        weigh_t(1, nc.vector)
+        quantise_y(slices[0][0], 0, widths[0])
+        quantise_x(4)
 
-        def z_pieces(i):
-            return [] if i < 6 else [i - 6]
+        for s in range(1, 6):
+            i = 2 * s + 3
+            first = 2 * (s % 2)
+            half = s - 2
+            g, c0 = half // 2, HALF_C * (half % 2)
+            transpose_x(i, (first, first + 1))
+            transpose_x(i + 1, (2 - first, 3 - first))
+            interleave_y(*slices[s], 0, Y_POOL_PAIR, nc.gpsimd)
+            centre_x(i, 2)
+            if half > 0:
+                for m in range(2):
+                    n = 2 * (half - 1) + m
+                    multiply_cov(n % PACK, 0, n // PACK, 4 + n % PACK)
+            for n in (i - 2, i - 1):
+                multiply_t(n, 4 + n % 4 if n < 8 else first + n - i + 2)
+            weigh_t(i - 3, nc.scalar)
+            interleave_y(*slices[s], Y_POOL_PAIR, widths[s], nc.scalar)
+            if s == 5:
+                interleave_z(g, c0, c0 + HALF_C, nc.scalar)
+            widen_y(*slices[s + 1])
+            weigh_t(i - 2, nc.scalar)
+            if 0 <= half < 3:
+                interleave_z(g, c0, c0 + HALF_C, nc.vector)
+            quantise_y(slices[s][0], 0, 512)
+            if half >= 0:
+                quantise_z(g, c0, c0 + HALF_C)
+            quantise_y(slices[s][0], 512, widths[s])
+            quantise_x(i, count=2)
 
-        for i in range(4, N_TILES):
-            use = 2 * i if i < 10 else 3 * i - 10
-            s = i - first_slice_step
-            pooled = Y_POOL if s > 0 else widths[0]
-            transpose_x(i, (use % 4, (use + 1) % 4))
-            if s >= 0:
-                interleave_y(*slices[s], 0, pooled, nc.gpsimd)
-            centre_x(i)
-            if i == 4:
-                for n in range(3):
-                    multiply_t(n, None, [3])
-            else:
-                multiply_t(i - 2, 4 + (i - 2) % 4 if i < 10 else (use + 2) % 4)
-            if i == 4:
-                weigh_t(0, nc.vector)
-                weigh_t(1, nc.vector)
-            if i > 4:
-                weigh_t(i - 3, nc.scalar)
-            if s > 0:
-                interleave_y(*slices[s], pooled, widths[s], nc.scalar)
-            if 0 <= s < len(slices) - 3:
-                widen_y(*slices[s + 2])
-            if i + 1 == N_TILES:
-                quantise_x(i, 2)
-            for n in z_pieces(i):
-                interleave_z(*z_piece(n), nc.vector)
-            for n in z_pieces(i - 1):
-                quantise_z(*z_piece(n))
-            if s >= 0:
-                quantise_y(*slices[s])
-            if i < N_TILES - 1:
-                quantise_x(i)
-            for n in z_pieces(i - 2) if i < 14 else []:
-                multiply_cov(n % PACK, 0, n // PACK, 4 + n % PACK)
+        transpose_x(15, (0, 1))
+        interleave_y(*slices[6], 0, Y_POOL, nc.gpsimd)
+        centre_x(15)
+        quantise_x(15, 2)
+        multiply_t(13, 2)
+        multiply_t(14, 3)
+        multiply_t(15, 0, c1=HALF_C)
+        multiply_t(15, 1, c0=HALF_C)
+        weigh_t(12, nc.scalar)
+        interleave_y(*slices[6], Y_POOL, widths[6], nc.scalar)
+        widen_y(*slices[7])
+        widen_y(*slices[8])
         nc.scalar.copy(out=inv_sb[:], in_=inv_bf[:, :, 0])
-
-        multiply_t(14, 2)
-        multiply_t(15, 3, c1=HALF_C)
-        multiply_t(15, 0, c0=HALF_C)
         weigh_t(13, nc.scalar)
         weigh_t(14, nc.scalar)
         weigh_t(15, nc.scalar, c1=HALF_C)
         weigh_t(15, nc.scalar, c0=HALF_C)
-        interleave_y(*slices[-2], 0, 256, nc.scalar, "tail_a")
-        widen_y(*slices[-1])
-        quantise_z(*z_piece(9))
+        interleave_y(*slices[7], 0, 256, nc.scalar, "tail_a")
+        interleave_y(*slices[8], 0, 256, nc.scalar, "tail_b")
+        interleave_z(2, 0, HALF_C, nc.vector)
+        quantise_y(slices[6][0], 0, widths[6])
+        quantise_z(2, 0, HALF_C)
         interleave_z(2, HALF_C, C, nc.vector)
         interleave_z(3, 0, HALF_C, nc.vector)
         quantise_z(2, HALF_C, C)
         quantise_z(3, 0, HALF_C)
         interleave_z(3, HALF_C, C, nc.vector)
-        quantise_y(*slices[-2])
+        quantise_y(slices[7][0], 0, 256)
         quantise_z(3, HALF_C, C)
         for n in range(6, 10):
             multiply_cov(n % PACK, 0, n // PACK)
         for m in range(2):
             for g in range(2):
-                multiply_cov(m, HALF_A, g, m + 1)
+                multiply_cov(m, HALF_A, g, m + 2)
         for m in range(2):
             multiply_cov(m, 0, last)
             store_cov(m, 0, nc.scalar if m else nc.vector)
-        interleave_y(*slices[-1], 0, 256, nc.vector, "tail_b")
-        quantise_y(*slices[-1])
+        quantise_y(slices[8][0], 0, 256)
         for m in range(2, 4):
             multiply_cov(m, 0, 2)
         for m in range(2):
@@ -392,7 +398,7 @@ def tile_pls_concentration_loadings_s7_kernel(
         for m in range(2, 4):
             multiply_cov(m, 0, last)
             store_cov(m, 0, nc.vector if m % 2 else nc.scalar)
-        multiply_cov(2, HALF_A, 0, 3)
+        multiply_cov(2, HALF_A, 0, 0)
         multiply_cov(2, HALF_A, 1)
         for m in range(2):
             multiply_cov(m, HALF_A, last)
@@ -400,7 +406,7 @@ def tile_pls_concentration_loadings_s7_kernel(
         multiply_cov(2, HALF_A, 2)
         multiply_cov(2, HALF_A, last)
         store_cov(2, HALF_A, nc.scalar)
-        for a0, b, engine in ((512, 0, nc.vector), (768, 4, nc.scalar)):
+        for a0, b, engine in ((512, 1, nc.vector), (768, 4, nc.scalar)):
             for g in range(G_S):
                 multiply_cov(3, a0, g, b, 256)
             store_cov(3, a0, engine, 256)

@@ -14,7 +14,8 @@ HALF_A = A // 2
 HALF_C = C // 2
 Y_POOL = 176
 Y_POOL_PAIR = 400
-Z_SCALAR = 0
+Z_SCALAR = 64
+Y_BUFS = 4
 
 FLOPS = 2 * S * K * C + 2 * S * C * A
 
@@ -151,6 +152,7 @@ def tile_pls_concentration_loadings_s7_kernel(
         x_grouped = {}
         x_codes = {}
         x_scales = {}
+        x_quantised = {}
 
         def transpose_x(i, banks):
             words = x_raw[i][:].bitcast(F32)
@@ -181,18 +183,21 @@ def tile_pls_concentration_loadings_s7_kernel(
                         op=SUB,
                     )
 
-        def quantise_x(first, pieces=1, count=1):
+        def quantise_x(first, pieces=1, count=1, only=None):
             words = count * G_K * P
-            codes = work.tile([P, words], U32, tag="x_codes", name=f"x_codes{first}", bufs=4, align_bytes=64)
-            scales = work.tile([P, words], U8, tag="x_scales", name=f"x_scales{first}", bufs=4, align_bytes=64)
+            if first not in x_codes:
+                codes = work.tile([P, words], U32, tag="x_codes", name=f"x_codes{first}", bufs=4, align_bytes=64)
+                scales = work.tile([P, words], U8, tag="x_scales", name=f"x_scales{first}", bufs=4, align_bytes=64)
+                x_quantised[first] = (codes, scales)
+                for n in range(count):
+                    x_codes[first + n] = codes[:, G_K * P * n : G_K * P * (n + 1)]
+                    x_scales[first + n] = scales[:, G_K * P * n : G_K * P * (n + 1)]
+            codes, scales = x_quantised[first]
             flat = x_grouped[first][:].rearrange("p n g s u e -> p (n g s u e)")
             width = words // pieces
-            for n in range(pieces):
+            for n in range(pieces) if only is None else [only]:
                 cols = slice(width * n, width * (n + 1))
                 quantise(codes[:, cols], scales[:, cols], flat[:, PACK * width * n : PACK * width * (n + 1)])
-            for n in range(count):
-                x_codes[first + n] = codes[:, G_K * P * n : G_K * P * (n + 1)]
-                x_scales[first + n] = scales[:, G_K * P * n : G_K * P * (n + 1)]
 
         t_banks = {}
         z_planes = {}
@@ -233,24 +238,27 @@ def tile_pls_concentration_loadings_s7_kernel(
         y_planes = {}
         y_grouped = {}
 
-        def widen_y(n0, n1):
-            y_planes[n0] = work.tile([P, PACK, n1 - n0], BF16, tag="y_planes", name=f"y_planes{n0}", bufs=3, align_bytes=64)
-            for g in range(n0 // A, (n1 - 1) // A + 1):
-                lo, hi = max(n0, A * g), min(n1, A * (g + 1))
+        def widen_y(s):
+            y_planes[s] = work.tile([P, PACK, widths[s]], BF16, tag="y_planes", name=f"y_planes{s}", bufs=Y_BUFS, align_bytes=64)
+            at = 0
+            for g, a0, a1 in slices[s]:
                 for j in range(PACK):
                     nc.scalar.activation(
-                        y_planes[n0][:, j, lo - n0 : hi - n0], y_raw[g][:, j, lo - A * g : hi - A * g].bitcast(FP8), COPY,
+                        y_planes[s][:, j, at : at + a1 - a0], y_raw[g][:, j, a0:a1].bitcast(FP8), COPY,
                         scale=y_scale_sb[:, g, j : j + 1],
                     )
+                at += a1 - a0
 
-        def interleave_y(n0, n1, b0, b1, engine, tag="y_slice"):
-            if n0 not in y_grouped:
-                y_grouped[n0] = stage.tile([P, n1 - n0, PACK], BF16, tag=tag, name=f"y_grouped{n0}", align_bytes=64)
-            interleave(engine, y_grouped[n0][:, b0:b1, :], y_planes[n0][:, :, b0:b1])
+        def interleave_y(s, b0, b1, engine, tag="y_slice"):
+            if s not in y_grouped:
+                y_grouped[s] = stage.tile([P, widths[s], PACK], BF16, tag=tag, name=f"y_grouped{s}", align_bytes=64)
+            interleave(engine, y_grouped[s][:, b0:b1, :], y_planes[s][:, :, b0:b1])
 
-        def quantise_y(n0, b0, b1):
-            flat = y_grouped[n0][:].rearrange("p a j -> p (a j)")
-            cols = slice(n0 + b0, n0 + b1)
+        def quantise_y(s, b0, b1):
+            flat = y_grouped[s][:].rearrange("p a j -> p (a j)")
+            n0 = columns[s][b0]
+            assert columns[s][b1 - 1] == n0 + b1 - b0 - 1
+            cols = slice(n0, n0 + b1 - b0)
             quantise(y_codes[:, cols], y_scales[:, cols], flat[:, PACK * b0 : PACK * b1])
 
         cov_banks = {}
@@ -276,8 +284,9 @@ def tile_pls_concentration_loadings_s7_kernel(
             nc.sync.dma_start(out=out[P * m : P * (m + 1), a0 : a0 + width], in_=res[:])
 
         last = G_S - 1
-        widths = [256, 640, 576, 640, 576, 640, 256, 256, 256]
-        slices = [(sum(widths[:n]), sum(widths[: n + 1])) for n in range(len(widths))]
+        slices = [[(0, 0, 256)], [(0, 256, 832)], [(0, 832, 1024), (1, 0, 384)], [(1, 384, 960)], [(1, 960, 1024), (2, 0, 512)], [(2, 512, 768), (3, 0, 256)], [(3, 256, 512)], [(2, 768, 1024)], [(3, 512, 768)], [(3, 768, 1024)]]
+        widths = [sum(a1 - a0 for g, a0, a1 in pieces) for pieces in slices]
+        columns = [[A * g + a for g, a0, a1 in pieces for a in range(a0, a1)] for pieces in slices]
 
         transpose_x(0, (0, 1))
         centre_x(0)
@@ -310,18 +319,18 @@ def tile_pls_concentration_loadings_s7_kernel(
         centre_x(3)
         quantise_x(3, 2)
         quantise_r(3)
-        widen_y(*slices[0])
+        widen_y(0)
         nc.scalar.copy(out=weight_sb[:], in_=weight_bf[:].rearrange("p g j -> p (g j)"))
-        widen_y(*slices[1])
+        widen_y(1)
 
         transpose_x(4, (0, 1))
-        interleave_y(*slices[0], 0, widths[0], nc.gpsimd)
+        interleave_y(0, 0, widths[0], nc.gpsimd)
         centre_x(4)
         for n in range(3):
             multiply_t(n, None, [3])
         weigh_t(0, nc.vector)
-        weigh_t(1, nc.vector)
-        quantise_y(slices[0][0], 0, widths[0])
+        weigh_t(1, nc.scalar)
+        quantise_y(0, 0, widths[0])
         quantise_x(4)
 
         for s in range(1, 6):
@@ -331,7 +340,7 @@ def tile_pls_concentration_loadings_s7_kernel(
             g, c0 = half // 2, HALF_C * (half % 2)
             transpose_x(i, (first, first + 1))
             transpose_x(i + 1, (2 - first, 3 - first))
-            interleave_y(*slices[s], 0, Y_POOL_PAIR, nc.gpsimd)
+            interleave_y(s, 0, Y_POOL_PAIR, nc.gpsimd)
             centre_x(i, 2)
             if half > 0:
                 for m in range(2):
@@ -340,21 +349,31 @@ def tile_pls_concentration_loadings_s7_kernel(
             for n in (i - 2, i - 1):
                 multiply_t(n, 4 + n % 4 if n < 8 else first + n - i + 2)
             weigh_t(i - 3, nc.scalar)
-            interleave_y(*slices[s], Y_POOL_PAIR, widths[s], nc.scalar)
-            if s == 5:
-                interleave_z(g, c0, c0 + HALF_C, nc.scalar)
-            widen_y(*slices[s + 1])
-            weigh_t(i - 2, nc.scalar)
-            if 0 <= half < 3:
-                interleave_z(g, c0, c0 + HALF_C, nc.vector)
-            quantise_y(slices[s][0], 0, 512)
+            interleave_y(s, Y_POOL_PAIR, widths[s], nc.scalar)
             if half >= 0:
+                interleave_z(g, c0, c0 + (HALF_C if s == 5 else Z_SCALAR), nc.scalar)
+            widen_y(s + 1)
+            if s == 5:
+                widen_y(7)
+            weigh_t(i - 2, nc.scalar)
+            if s < 5:
+                if half >= 0:
+                    interleave_z(g, c0 + Z_SCALAR, c0 + HALF_C, nc.vector)
+                quantise_y(s, 0, 512)
+                if half >= 0:
+                    quantise_z(g, c0, c0 + HALF_C)
+                quantise_y(s, 512, widths[s])
+                quantise_x(i, count=2)
+            else:
+                quantise_x(i, 2, 2, 0)
+                quantise_y(s, 0, 256)
                 quantise_z(g, c0, c0 + HALF_C)
-            quantise_y(slices[s][0], 512, widths[s])
-            quantise_x(i, count=2)
+                quantise_x(i, 2, 2, 1)
+                quantise_y(s, 256, 512)
+                interleave_y(7, 0, 256, nc.vector, "tail_a")
 
         transpose_x(15, (0, 1))
-        interleave_y(*slices[6], 0, Y_POOL, nc.gpsimd)
+        interleave_y(6, 0, Y_POOL, nc.gpsimd)
         centre_x(15)
         quantise_x(15, 2)
         multiply_t(13, 2)
@@ -362,26 +381,27 @@ def tile_pls_concentration_loadings_s7_kernel(
         multiply_t(15, 0, c1=HALF_C)
         multiply_t(15, 1, c0=HALF_C)
         weigh_t(12, nc.scalar)
-        interleave_y(*slices[6], Y_POOL, widths[6], nc.scalar)
-        widen_y(*slices[7])
-        widen_y(*slices[8])
+        interleave_y(6, Y_POOL, widths[6], nc.scalar)
         nc.scalar.copy(out=inv_sb[:], in_=inv_bf[:, :, 0])
+        widen_y(8)
         weigh_t(13, nc.scalar)
-        weigh_t(14, nc.scalar)
+        widen_y(9)
+        interleave_z(2, 0, HALF_C, nc.vector)
+        quantise_y(6, 0, widths[6])
+        quantise_z(2, 0, HALF_C)
+        weigh_t(14, nc.vector)
         weigh_t(15, nc.scalar, c1=HALF_C)
         weigh_t(15, nc.scalar, c0=HALF_C)
-        interleave_y(*slices[7], 0, 256, nc.scalar, "tail_a")
-        interleave_y(*slices[8], 0, 256, nc.scalar, "tail_b")
-        interleave_z(2, 0, HALF_C, nc.vector)
-        quantise_y(slices[6][0], 0, widths[6])
-        quantise_z(2, 0, HALF_C)
+        interleave_y(8, 0, 256, nc.scalar, "tail_b")
+        interleave_y(9, 0, 256, nc.scalar, "x_odd")
         interleave_z(2, HALF_C, C, nc.vector)
         interleave_z(3, 0, HALF_C, nc.vector)
         quantise_z(2, HALF_C, C)
         quantise_z(3, 0, HALF_C)
         interleave_z(3, HALF_C, C, nc.vector)
-        quantise_y(slices[7][0], 0, 256)
+        quantise_y(7, 0, 256)
         quantise_z(3, HALF_C, C)
+        quantise_y(8, 0, 256)
         for n in range(6, 10):
             multiply_cov(n % PACK, 0, n // PACK)
         for m in range(2):
@@ -390,21 +410,19 @@ def tile_pls_concentration_loadings_s7_kernel(
         for m in range(2):
             multiply_cov(m, 0, last)
             store_cov(m, 0, nc.scalar if m else nc.vector)
-        quantise_y(slices[8][0], 0, 256)
+        quantise_y(9, 0, 256)
+        for g in (2, last):
+            for m in range(2, 4):
+                multiply_cov(m, 0, g)
         for m in range(2, 4):
-            multiply_cov(m, 0, 2)
+            store_cov(m, 0, nc.vector if m % 2 else nc.scalar)
         for m in range(2):
             multiply_cov(m, HALF_A, 2)
-        for m in range(2, 4):
-            multiply_cov(m, 0, last)
-            store_cov(m, 0, nc.vector if m % 2 else nc.scalar)
-        multiply_cov(2, HALF_A, 0, 0)
-        multiply_cov(2, HALF_A, 1)
         for m in range(2):
             multiply_cov(m, HALF_A, last)
             store_cov(m, HALF_A, nc.vector if m else nc.scalar)
-        multiply_cov(2, HALF_A, 2)
-        multiply_cov(2, HALF_A, last)
+        for g in range(G_S):
+            multiply_cov(2, HALF_A, g, 0)
         store_cov(2, HALF_A, nc.scalar)
         for a0, b, engine in ((512, 1, nc.vector), (768, 4, nc.scalar)):
             for g in range(G_S):

@@ -13,9 +13,9 @@ N_TILES = S // P
 HALF_A = A // 2
 HALF_C = C // 2
 Y_POOL = 176
-Y_POOL_PAIR = 400
+Y_POOL_PAIR = 272
 Z_SCALAR = 64
-Y_BUFS = 4
+Y_BUFS = 5
 
 FLOPS = 2 * S * K * C + 2 * S * C * A
 
@@ -154,50 +154,42 @@ def tile_pls_concentration_loadings_s7_kernel(
         x_scales = {}
         x_quantised = {}
 
-        def transpose_x(i, banks):
-            words = x_raw[i][:].bitcast(F32)
-            for b in range(2):
-                ps = bank(banks[b], f"x_turned{i}{b}")
-                view = ps[:].rearrange("p (u g s) -> p u g s", u=2, g=2)
+        def transpose_x(h0, banks):
+            for h, b in enumerate(banks, h0):
+                words = x_raw[h // 2][:].bitcast(F32)
+                x_banks[h] = bank(b, f"x_turned{h}")
+                view = x_banks[h][:].rearrange("p (u g s) -> p u g s", u=2, g=2)
                 for gl in range(2):
-                    g = 2 * b + gl
+                    g = 2 * (h % 2) + gl
                     for u in range(2):
                         nc.tensor.transpose(
                             view[:, u, gl, :], words[:, 256 * g + u : 256 * (g + 1) : 2], ident[:]
                         )
-                x_banks[i, b] = ps
 
-        def centre_x(first, count=1):
-            tag = {2: "tail_a", 3: "y_slice"}.get(first, ("x_even", "x_odd")[len(x_grouped) % 2])
-            x_grouped[first] = stage.tile(
-                [P, count, G_K, P, 2, 2], BF16, tag=tag, name=f"x_grouped{first}", align_bytes=64
+        def centre_x(h0, count, tag=None):
+            tag = tag or ("x_even", "x_odd")[len(x_grouped) % 2]
+            x_grouped[h0] = stage.tile(
+                [P, count, 2, P, 2, 2], BF16, tag=tag, name=f"x_grouped{h0}", align_bytes=64
             )
+            codes = work.tile([P, 2 * P * count], U32, tag="x_codes", name=f"x_codes{h0}", bufs=4, align_bytes=64)
+            scales = work.tile([P, 2 * P * count], U8, tag="x_scales", name=f"x_scales{h0}", bufs=4, align_bytes=64)
+            x_quantised[h0] = (codes, scales)
             for n in range(count):
-                for b in range(2):
-                    nc.vector.tensor_tensor(
-                        out=x_grouped[first][:, n, 2 * b : 2 * b + 2],
-                        in0=x_banks[first + n, b][:].bitcast(BF16).rearrange(
-                            "p (u g s e) -> p g s u e", u=2, g=2, e=2
-                        ),
-                        in1=mean_sb[:, 2 * b : 2 * b + 2].unsqueeze(2).to_broadcast([P, 2, P, 2, 2]),
-                        op=SUB,
-                    )
+                b = (h0 + n) % 2
+                x_codes[h0 + n] = codes[:, 2 * P * n : 2 * P * (n + 1)]
+                x_scales[h0 + n] = scales[:, 2 * P * n : 2 * P * (n + 1)]
+                nc.vector.tensor_tensor(
+                    out=x_grouped[h0][:, n],
+                    in0=x_banks[h0 + n][:].bitcast(BF16).rearrange("p (u g s e) -> p g s u e", u=2, g=2, e=2),
+                    in1=mean_sb[:, 2 * b : 2 * b + 2].unsqueeze(2).to_broadcast([P, 2, P, 2, 2]),
+                    op=SUB,
+                )
 
-        def quantise_x(first, pieces=1, count=1, only=None):
-            words = count * G_K * P
-            if first not in x_codes:
-                codes = work.tile([P, words], U32, tag="x_codes", name=f"x_codes{first}", bufs=4, align_bytes=64)
-                scales = work.tile([P, words], U8, tag="x_scales", name=f"x_scales{first}", bufs=4, align_bytes=64)
-                x_quantised[first] = (codes, scales)
-                for n in range(count):
-                    x_codes[first + n] = codes[:, G_K * P * n : G_K * P * (n + 1)]
-                    x_scales[first + n] = scales[:, G_K * P * n : G_K * P * (n + 1)]
-            codes, scales = x_quantised[first]
-            flat = x_grouped[first][:].rearrange("p n g s u e -> p (n g s u e)")
-            width = words // pieces
-            for n in range(pieces) if only is None else [only]:
-                cols = slice(width * n, width * (n + 1))
-                quantise(codes[:, cols], scales[:, cols], flat[:, PACK * width * n : PACK * width * (n + 1)])
+        def quantise_x(h0, n0, n1):
+            codes, scales = x_quantised[h0]
+            flat = x_grouped[h0][:].rearrange("p n g s u e -> p (n g s u e)")
+            cols = slice(2 * P * n0, 2 * P * n1)
+            quantise(codes[:, cols], scales[:, cols], flat[:, PACK * cols.start : PACK * cols.stop])
 
         t_banks = {}
         z_planes = {}
@@ -207,11 +199,11 @@ def tile_pls_concentration_loadings_s7_kernel(
             for g in passes:
                 if g == 0:
                     t_banks[i, c0] = bank(b, f"t_sum{i}_{c0}")
-                cols = slice(P * g, P * (g + 1))
+                h, cols = 2 * i + g // 2, slice(P * (g % 2), P * (g % 2 + 1))
                 nc.tensor.matmul_mx(
                     out=t_banks[i, c0][:, : c1 - c0],
-                    lhsT=x_codes[i][:, cols].bitcast(FP8X4),
-                    lhsT_scale=x_scales[i][:, cols],
+                    lhsT=x_codes[h][:, cols].bitcast(FP8X4),
+                    lhsT_scale=x_scales[h][:, cols],
                     rhs=r_codes[:, g, c0:c1].bitcast(FP8X4),
                     rhs_scale=r_scales[:, g, c0:c1],
                     start=(g == 0),
@@ -284,147 +276,157 @@ def tile_pls_concentration_loadings_s7_kernel(
             nc.sync.dma_start(out=out[P * m : P * (m + 1), a0 : a0 + width], in_=res[:])
 
         last = G_S - 1
-        slices = [[(0, 0, 256)], [(0, 256, 832)], [(0, 832, 1024), (1, 0, 384)], [(1, 384, 960)], [(1, 960, 1024), (2, 0, 512)], [(2, 512, 768), (3, 0, 256)], [(3, 256, 512)], [(2, 768, 1024)], [(3, 512, 768)], [(3, 768, 1024)]]
+        slices = [[(0, 0, 256)], [(0, 256, 640)], [(0, 640, 1024)], [(1, 0, 512)], [(1, 512, 896)], [(1, 896, 1024), (2, 0, 256)], [(2, 256, 768)], [(3, 0, 256)], [(3, 256, 512)], [(2, 768, 1024)], [(3, 512, 768)], [(3, 768, 1024)]]
         widths = [sum(a1 - a0 for g, a0, a1 in pieces) for pieces in slices]
         columns = [[A * g + a for g, a0, a1 in pieces for a in range(a0, a1)] for pieces in slices]
 
         transpose_x(0, (0, 1))
-        centre_x(0)
+        centre_x(0, 2, "x_even")
         interleave_r(0, 0, 256, nc.scalar)
         interleave_r(0, 256, 512, nc.vector)
-        quantise_x(0, 2)
+        quantise_x(0, 0, 1)
+        quantise_x(0, 1, 2)
         quantise_r(0)
-        transpose_x(1, (2, 3))
+        transpose_x(2, (2, 3))
         multiply_t(0, 4, [0])
         interleave_r(1, 0, 176, nc.gpsimd)
         interleave_r(1, 176, 512, nc.scalar)
-        centre_x(1)
-        quantise_x(1, 2)
+        centre_x(2, 2, "x_odd")
+        quantise_x(2, 0, 1)
+        quantise_x(2, 1, 2)
         quantise_r(1)
-        transpose_x(2, (0, 1))
+        transpose_x(4, (0, 1))
         multiply_t(1, 5, [0])
         multiply_t(0, 4, [1])
         multiply_t(1, 5, [1])
         interleave_r(2, 0, 176, nc.gpsimd)
         interleave_r(2, 176, 512, nc.scalar)
-        centre_x(2)
-        quantise_x(2, 2)
+        centre_x(4, 2, "tail_a")
+        quantise_x(4, 0, 1)
+        quantise_x(4, 1, 2)
         quantise_r(2)
-        transpose_x(3, (2, 3))
+        transpose_x(6, (2, 3))
         multiply_t(0, 4, [2])
         multiply_t(1, 5, [2])
         multiply_t(2, 6, [0, 1, 2])
         interleave_r(3, 0, 176, nc.gpsimd)
         interleave_r(3, 176, 512, nc.scalar)
-        centre_x(3)
-        quantise_x(3, 2)
+        centre_x(6, 2, "y_slice")
+        quantise_x(6, 0, 1)
+        quantise_x(6, 1, 2)
         quantise_r(3)
         widen_y(0)
         nc.scalar.copy(out=weight_sb[:], in_=weight_bf[:].rearrange("p g j -> p (g j)"))
         widen_y(1)
 
-        transpose_x(4, (0, 1))
+        transpose_x(8, (0, 1))
         interleave_y(0, 0, widths[0], nc.gpsimd)
-        centre_x(4)
+        centre_x(8, 2)
         for n in range(3):
             multiply_t(n, None, [3])
         weigh_t(0, nc.vector)
-        weigh_t(1, nc.scalar)
+        weigh_t(1, nc.vector)
+        widen_y(2)
         quantise_y(0, 0, widths[0])
-        quantise_x(4)
+        quantise_x(8, 0, 2)
 
-        for s in range(1, 6):
-            i = 2 * s + 3
-            first = 2 * (s % 2)
-            half = s - 2
-            g, c0 = half // 2, HALF_C * (half % 2)
-            transpose_x(i, (first, first + 1))
-            transpose_x(i + 1, (2 - first, 3 - first))
+        run_banks = [(2, 3, 0), (1, 2, 3), (0, 1, 2), (3, 0, 1), (3, 0, 1), (0, 1, 2)]
+        t_after = [((3, 7), (4, 4)), ((5, 5),), ((6, 6), (7, 7)), ((8, 2),), ((9, 2), (10, 3)), ((11, 3),)]
+        weigh_in = [(2,), (3, 4), (5,), (6, 7), (8,), (9, 10)]
+        for run in range(6):
+            s = run + 1
+            h0 = 10 + 3 * run
+            transpose_x(h0, run_banks[run])
             interleave_y(s, 0, Y_POOL_PAIR, nc.gpsimd)
-            centre_x(i, 2)
-            if half > 0:
-                for m in range(2):
-                    n = 2 * (half - 1) + m
-                    multiply_cov(n % PACK, 0, n // PACK, 4 + n % PACK)
-            for n in (i - 2, i - 1):
-                multiply_t(n, 4 + n % 4 if n < 8 else first + n - i + 2)
-            weigh_t(i - 3, nc.scalar)
+            centre_x(h0, 3)
+            for n, b in t_after[run]:
+                multiply_t(n, b)
+            if run in (3, 5):
+                for m in range(4):
+                    multiply_cov(m, 0, (run - 3) // 2, 4 + m)
+            has_z = 1 <= run <= 4
+            g, c0 = (run - 1) // 2, HALF_C * ((run - 1) % 2)
+            for n in weigh_in[run]:
+                weigh_t(n, nc.scalar)
             interleave_y(s, Y_POOL_PAIR, widths[s], nc.scalar)
-            if half >= 0:
-                interleave_z(g, c0, c0 + (HALF_C if s == 5 else Z_SCALAR), nc.scalar)
-            widen_y(s + 1)
-            if s == 5:
-                widen_y(7)
-            weigh_t(i - 2, nc.scalar)
-            if s < 5:
-                if half >= 0:
-                    interleave_z(g, c0 + Z_SCALAR, c0 + HALF_C, nc.vector)
-                quantise_y(s, 0, 512)
-                if half >= 0:
-                    quantise_z(g, c0, c0 + HALF_C)
-                quantise_y(s, 512, widths[s])
-                quantise_x(i, count=2)
-            else:
-                quantise_x(i, 2, 2, 0)
-                quantise_y(s, 0, 256)
+            if has_z and Z_SCALAR:
+                interleave_z(g, c0, c0 + Z_SCALAR, nc.scalar)
+            widen_y(s + 2)
+            if has_z:
+                interleave_z(g, c0 + Z_SCALAR, c0 + HALF_C, nc.vector)
+            quantise_x(h0, 0, 1)
+            if widths[s] < 512:
+                quantise_y(s, 256, widths[s])
+            if has_z:
                 quantise_z(g, c0, c0 + HALF_C)
-                quantise_x(i, 2, 2, 1)
-                quantise_y(s, 256, 512)
-                interleave_y(7, 0, 256, nc.vector, "tail_a")
+            quantise_y(s, 0, 256 if widths[s] < 512 else 512)
+            quantise_x(h0, 1, 3)
 
-        transpose_x(15, (0, 1))
-        interleave_y(6, 0, Y_POOL, nc.gpsimd)
-        centre_x(15)
-        quantise_x(15, 2)
-        multiply_t(13, 2)
-        multiply_t(14, 3)
-        multiply_t(15, 0, c1=HALF_C)
-        multiply_t(15, 1, c0=HALF_C)
-        weigh_t(12, nc.scalar)
-        interleave_y(6, Y_POOL, widths[6], nc.scalar)
-        nc.scalar.copy(out=inv_sb[:], in_=inv_bf[:, :, 0])
-        widen_y(8)
-        weigh_t(13, nc.scalar)
+        transpose_x(28, (0, 1))
+        interleave_y(7, 0, Y_POOL, nc.gpsimd)
+        centre_x(28, 2)
+        multiply_t(12, 2)
+        weigh_t(11, nc.scalar)
+        interleave_y(7, Y_POOL, widths[7], nc.scalar)
         widen_y(9)
+        widen_y(10)
         interleave_z(2, 0, HALF_C, nc.vector)
-        quantise_y(6, 0, widths[6])
+        quantise_y(7, 0, 256)
+        quantise_x(28, 0, 2)
+
+        transpose_x(30, (3, 0))
+        interleave_y(8, 0, Y_POOL, nc.gpsimd)
+        centre_x(30, 2)
+        quantise_x(30, 0, 1)
+        quantise_x(30, 1, 2)
+        multiply_t(13, 1)
+        multiply_t(14, 2)
+        multiply_t(15, 3, c1=HALF_C)
+        multiply_t(15, 0, c0=HALF_C)
+        weigh_t(12, nc.scalar)
+        interleave_y(8, Y_POOL, widths[8], nc.scalar)
+        widen_y(11)
+        nc.scalar.copy(out=inv_sb[:], in_=inv_bf[:, :, 0])
+        weigh_t(13, nc.scalar)
         quantise_z(2, 0, HALF_C)
-        weigh_t(14, nc.vector)
+        interleave_z(2, HALF_C, C, nc.vector)
+        quantise_y(8, 0, 256)
+        quantise_z(2, HALF_C, C)
+        weigh_t(14, nc.scalar)
         weigh_t(15, nc.scalar, c1=HALF_C)
         weigh_t(15, nc.scalar, c0=HALF_C)
-        interleave_y(8, 0, 256, nc.scalar, "tail_b")
-        interleave_y(9, 0, 256, nc.scalar, "x_odd")
-        interleave_z(2, HALF_C, C, nc.vector)
+        interleave_y(9, 0, 256, nc.scalar, "tail_a")
+        interleave_y(10, 0, 256, nc.scalar, "tail_b")
+        interleave_y(11, 0, 256, nc.vector, "x_odd")
         interleave_z(3, 0, HALF_C, nc.vector)
-        quantise_z(2, HALF_C, C)
+        quantise_y(11, 0, 256)
         quantise_z(3, 0, HALF_C)
         interleave_z(3, HALF_C, C, nc.vector)
-        quantise_y(7, 0, 256)
+        quantise_y(9, 0, 256)
         quantise_z(3, HALF_C, C)
-        quantise_y(8, 0, 256)
-        for n in range(6, 10):
-            multiply_cov(n % PACK, 0, n // PACK)
+        for m in range(4):
+            multiply_cov(m, 0, 2)
         for m in range(2):
             for g in range(2):
-                multiply_cov(m, HALF_A, g, m + 2)
+                multiply_cov(m, HALF_A, g, m + 1)
         for m in range(2):
             multiply_cov(m, 0, last)
-            store_cov(m, 0, nc.scalar if m else nc.vector)
-        quantise_y(9, 0, 256)
-        for g in (2, last):
-            for m in range(2, 4):
-                multiply_cov(m, 0, g)
+            store_cov(m, 0, nc.vector if m else nc.scalar)
+        quantise_y(10, 0, 256)
+        for g in range(2):
+            multiply_cov(2, HALF_A, g, 3)
         for m in range(2, 4):
-            store_cov(m, 0, nc.vector if m % 2 else nc.scalar)
+            multiply_cov(m, 0, last)
+            store_cov(m, 0, nc.scalar if m % 2 else nc.vector)
         for m in range(2):
             multiply_cov(m, HALF_A, 2)
         for m in range(2):
             multiply_cov(m, HALF_A, last)
-            store_cov(m, HALF_A, nc.vector if m else nc.scalar)
-        for g in range(G_S):
-            multiply_cov(2, HALF_A, g, 0)
-        store_cov(2, HALF_A, nc.scalar)
-        for a0, b, engine in ((512, 1, nc.vector), (768, 4, nc.scalar)):
+            store_cov(m, HALF_A, nc.scalar if m % 2 else nc.vector)
+        for g in range(2, G_S):
+            multiply_cov(2, HALF_A, g)
+        store_cov(2, HALF_A, nc.vector)
+        for a0, b, engine in ((512, 0, nc.scalar), (768, 4, nc.vector)):
             for g in range(G_S):
                 multiply_cov(3, a0, g, b, 256)
             store_cov(3, a0, engine, 256)

@@ -13,8 +13,7 @@ N_TILES = S // P
 HALF_A = A // 2
 HALF_C = C // 2
 Y_POOL = 176
-Y_POOL_PAIR = 272
-Z_SCALAR = 64
+Z_SCALAR = 32
 Y_BUFS = 5
 
 FLOPS = 2 * S * K * C + 2 * S * C * A
@@ -90,16 +89,16 @@ def tile_pls_concentration_loadings_s7_kernel(
         load_x(4)
         load_y(0, 256, 1024)
         load_x(5)
-        load_x(6)
-        load_y(1)
         nc.sync.dma_start(out=inv_bf[:, :, 0:1], in_=inv_score.rearrange("(m p o) -> p m o", p=P, o=1))
+        load_x(6)
         load_x(7)
+        load_y(1)
         load_x(8)
-        load_y(2)
         load_x(9)
+        load_y(2)
         load_x(10)
-        load_y(3)
         load_x(11)
+        load_y(3)
         load_x(12)
         load_x(13)
         load_x(14)
@@ -276,7 +275,7 @@ def tile_pls_concentration_loadings_s7_kernel(
             nc.sync.dma_start(out=out[P * m : P * (m + 1), a0 : a0 + width], in_=res[:])
 
         last = G_S - 1
-        slices = [[(0, 0, 256)], [(0, 256, 640)], [(0, 640, 1024)], [(1, 0, 512)], [(1, 512, 896)], [(1, 896, 1024), (2, 0, 256)], [(2, 256, 768)], [(3, 0, 256)], [(3, 256, 512)], [(2, 768, 1024)], [(3, 512, 768)], [(3, 768, 1024)]]
+        slices = [[(0, 0, 256)], [(0, 256, 576)], [(0, 576, 832)], [(0, 832, 1024), (1, 0, 128)], [(1, 128, 384)], [(1, 384, 640)], [(1, 640, 960)], [(1, 960, 1024), (2, 0, 192)], [(2, 192, 512)], [(2, 512, 768)], [(3, 0, 256)], [(3, 256, 512)], [(2, 768, 1024)], [(3, 512, 768)], [(3, 768, 1024)]]
         widths = [sum(a1 - a0 for g, a0, a1 in pieces) for pieces in slices]
         columns = [[A * g + a for g, a0, a1 in pieces for a in range(a0, a1)] for pieces in slices]
 
@@ -330,52 +329,50 @@ def tile_pls_concentration_loadings_s7_kernel(
         quantise_y(0, 0, widths[0])
         quantise_x(8, 0, 2)
 
-        run_banks = [(2, 3, 0), (1, 2, 3), (0, 1, 2), (3, 0, 1), (3, 0, 1), (0, 1, 2)]
-        t_after = [((3, 7), (4, 4)), ((5, 5),), ((6, 6), (7, 7)), ((8, 2),), ((9, 2), (10, 3)), ((11, 3),)]
-        weigh_in = [(2,), (3, 4), (5,), (6, 7), (8,), (9, 10)]
-        for run in range(6):
-            s = run + 1
-            h0 = 10 + 3 * run
-            transpose_x(h0, run_banks[run])
-            interleave_y(s, 0, Y_POOL_PAIR, nc.gpsimd)
-            centre_x(h0, 3)
-            for n, b in t_after[run]:
-                multiply_t(n, b)
-            if run in (3, 5):
-                for m in range(4):
-                    multiply_cov(m, 0, (run - 3) // 2, 4 + m)
-            has_z = 1 <= run <= 4
-            g, c0 = (run - 1) // 2, HALF_C * ((run - 1) % 2)
-            for n in weigh_in[run]:
-                weigh_t(n, nc.scalar)
-            interleave_y(s, Y_POOL_PAIR, widths[s], nc.scalar)
-            if has_z and Z_SCALAR:
-                interleave_z(g, c0, c0 + Z_SCALAR, nc.scalar)
+        def z_piece(n):
+            return n // PACK, P * (n % PACK), P * (n % PACK + 1)
+
+        for i in range(5, 14):
+            s = i - 4
+            use = 2 * i if i < 10 else 3 * i - 10
+            transpose_x(2 * i, (use % 4, (use + 1) % 4))
+            interleave_y(s, 0, Y_POOL, nc.gpsimd)
+            centre_x(2 * i, 2)
+            multiply_t(i - 2, 4 + (i - 2) % 4 if i < 10 else (use + 2) % 4)
+            if i >= 8:
+                multiply_cov((i - 8) % PACK, 0, (i - 8) // PACK, 4 + (i - 8) % PACK)
+            weigh_t(i - 3, nc.scalar)
+            interleave_y(s, Y_POOL, widths[s], nc.scalar)
+            if i >= 6:
+                g, c0, c1 = z_piece(i - 6)
+                if Z_SCALAR:
+                    interleave_z(g, c0, c0 + Z_SCALAR, nc.scalar)
             widen_y(s + 2)
-            if has_z:
-                interleave_z(g, c0 + Z_SCALAR, c0 + HALF_C, nc.vector)
-            quantise_x(h0, 0, 1)
-            if widths[s] < 512:
+            if i >= 6:
+                interleave_z(g, c0 + Z_SCALAR, c1, nc.vector)
+            if i >= 7:
+                quantise_z(*z_piece(i - 7))
+            if widths[s] > 256:
                 quantise_y(s, 256, widths[s])
-            if has_z:
-                quantise_z(g, c0, c0 + HALF_C)
-            quantise_y(s, 0, 256 if widths[s] < 512 else 512)
-            quantise_x(h0, 1, 3)
+            quantise_y(s, 0, 256)
+            quantise_x(2 * i, 0, 2)
 
         transpose_x(28, (0, 1))
-        interleave_y(7, 0, Y_POOL, nc.gpsimd)
+        interleave_y(10, 0, Y_POOL, nc.gpsimd)
         centre_x(28, 2)
         multiply_t(12, 2)
+        multiply_cov(2, 0, 1)
         weigh_t(11, nc.scalar)
-        interleave_y(7, Y_POOL, widths[7], nc.scalar)
-        widen_y(9)
-        widen_y(10)
+        interleave_y(10, Y_POOL, widths[10], nc.scalar)
+        widen_y(12)
+        widen_y(13)
         interleave_z(2, 0, HALF_C, nc.vector)
-        quantise_y(7, 0, 256)
+        quantise_z(*z_piece(7))
+        quantise_y(10, 0, 256)
         quantise_x(28, 0, 2)
 
         transpose_x(30, (3, 0))
-        interleave_y(8, 0, Y_POOL, nc.gpsimd)
+        interleave_y(11, 0, Y_POOL, nc.gpsimd)
         centre_x(30, 2)
         quantise_x(30, 0, 1)
         quantise_x(30, 1, 2)
@@ -384,26 +381,27 @@ def tile_pls_concentration_loadings_s7_kernel(
         multiply_t(15, 3, c1=HALF_C)
         multiply_t(15, 0, c0=HALF_C)
         weigh_t(12, nc.scalar)
-        interleave_y(8, Y_POOL, widths[8], nc.scalar)
-        widen_y(11)
+        interleave_y(11, Y_POOL, widths[11], nc.scalar)
+        widen_y(14)
         nc.scalar.copy(out=inv_sb[:], in_=inv_bf[:, :, 0])
         weigh_t(13, nc.scalar)
         quantise_z(2, 0, HALF_C)
         interleave_z(2, HALF_C, C, nc.vector)
-        quantise_y(8, 0, 256)
+        quantise_y(11, 0, 256)
         quantise_z(2, HALF_C, C)
         weigh_t(14, nc.scalar)
         weigh_t(15, nc.scalar, c1=HALF_C)
         weigh_t(15, nc.scalar, c0=HALF_C)
-        interleave_y(9, 0, 256, nc.scalar, "tail_a")
-        interleave_y(10, 0, 256, nc.scalar, "tail_b")
-        interleave_y(11, 0, 256, nc.vector, "x_odd")
+        interleave_y(12, 0, 256, nc.scalar, "tail_a")
+        interleave_y(13, 0, 256, nc.scalar, "tail_b")
+        interleave_y(14, 0, 256, nc.vector, "x_odd")
         interleave_z(3, 0, HALF_C, nc.vector)
-        quantise_y(11, 0, 256)
+        quantise_y(14, 0, 256)
         quantise_z(3, 0, HALF_C)
         interleave_z(3, HALF_C, C, nc.vector)
-        quantise_y(9, 0, 256)
+        quantise_y(12, 0, 256)
         quantise_z(3, HALF_C, C)
+        multiply_cov(3, 0, 1)
         for m in range(4):
             multiply_cov(m, 0, 2)
         for m in range(2):
@@ -412,7 +410,7 @@ def tile_pls_concentration_loadings_s7_kernel(
         for m in range(2):
             multiply_cov(m, 0, last)
             store_cov(m, 0, nc.vector if m else nc.scalar)
-        quantise_y(10, 0, 256)
+        quantise_y(13, 0, 256)
         for g in range(2):
             multiply_cov(2, HALF_A, g, 3)
         for m in range(2, 4):

@@ -13,7 +13,7 @@ N_TILES = S // P
 HALF_A = A // 2
 HALF_C = C // 2
 Y_POOL = 176
-Z_SCALAR = 32
+Z_SCALAR = 16
 Y_BUFS = 5
 
 FLOPS = 2 * S * K * C + 2 * S * C * A

@@ -12,8 +12,8 @@ G_S = S // PASS
 N_TILES = S // P
 HALF_A = A // 2
 HALF_C = C // 2
-Y_POOL = 176
-Z_SCALAR = 16
+Y_POOL = 192
+Z_SCALAR = 24
 Y_BUFS = 5
 
 FLOPS = 2 * S * K * C + 2 * S * C * A

@@ -12,9 +12,16 @@ G_S = S // PASS
 N_TILES = S // P
 HALF_A = A // 2
 HALF_C = C // 2
-Y_POOL = 192
-Z_SCALAR = 24
-Y_BUFS = 5
+POOL = 200
+R_POOL = 200
+Y_VECTOR = 96
+SORTED = ()
+V_WEIGH = 1
+TAIL_S = 448
+WARM = (0, 0)
+EXTRA = (9, 11, 12, 13, 14)
+X_BUFS = 12
+Y_ORDER = [(0, 0), (0, 1), (1, 0), (1, 1), (2, 0), (3, 0), (2, 1), (3, 1)]
 
 FLOPS = 2 * S * K * C + 2 * S * C * A
 
@@ -52,7 +59,7 @@ def tile_pls_concentration_loadings_s7_kernel(
         inv_bf = keep.tile([P, 4, 2], BF16, name="inv_bf")
         inv_sb = keep.tile([P, 4], F32, name="inv_sb")
 
-        x_raw = [keep.tile([P, K], BF16, name=f"x_raw{i}", align_bytes=64) for i in range(N_TILES)]
+        x_raw = {}
         r_raw = [keep.tile([P, PACK, C], BF16, name=f"r_raw{g}", align_bytes=64) for g in range(G_K)]
         y_raw = [keep.tile([P, PACK, A], U8, name=f"y_raw{g}", align_bytes=64) for g in range(G_S)]
 
@@ -61,6 +68,7 @@ def tile_pls_concentration_loadings_s7_kernel(
         y_hbm = y_bytes.rearrange("(g p j) a -> g p j a", p=P, j=PACK)
 
         def load_x(i, pieces=1):
+            x_raw[i] = work.tile([P, K], BF16, tag="x_raw", name=f"x_raw{i}", bufs=X_BUFS, align_bytes=64)
             for n in range(pieces):
                 cols = slice(K * n // pieces, K * (n + 1) // pieces)
                 nc.sync.dma_start(out=x_raw[i][:, cols], in_=x_hbm[i // PACK, i % PACK][:, cols])
@@ -83,13 +91,12 @@ def tile_pls_concentration_loadings_s7_kernel(
         load_r(2)
         load_x(3)
         load_r(3)
-        nc.sync.dma_start(out=y_scale_sb[:], in_=y_scale.rearrange("(g p j) o -> p g (j o)", p=P, j=PACK))
-        nc.sync.dma_start(out=weight_bf[:], in_=weight.rearrange("(g p j) -> p g j", p=P, j=PACK))
-        load_y(0, 0, 256)
         load_x(4)
+        nc.sync.dma_start(out=y_scale_sb[:], in_=y_scale.rearrange("(g p j) o -> p g (j o)", p=P, j=PACK))
+        load_y(0, 0, 256)
+        nc.sync.dma_start(out=weight_bf[:], in_=weight.rearrange("(g p j) -> p g j", p=P, j=PACK))
         load_y(0, 256, 1024)
         load_x(5)
-        nc.sync.dma_start(out=inv_bf[:, :, 0:1], in_=inv_score.rearrange("(m p o) -> p m o", p=P, o=1))
         load_x(6)
         load_x(7)
         load_y(1)
@@ -98,11 +105,8 @@ def tile_pls_concentration_loadings_s7_kernel(
         load_y(2)
         load_x(10)
         load_x(11)
+        nc.sync.dma_start(out=inv_bf[:, :, 0:1], in_=inv_score.rearrange("(m p o) -> p m o", p=P, o=1))
         load_y(3)
-        load_x(12)
-        load_x(13)
-        load_x(14)
-        load_x(15)
 
         r_codes = keep.tile([P, G_K, C], U32, name="r_codes", align_bytes=64)
         r_scales = keep.tile([P, G_K, C], U8, name="r_scales", align_bytes=64)
@@ -153,6 +157,12 @@ def tile_pls_concentration_loadings_s7_kernel(
         x_scales = {}
         x_quantised = {}
 
+        x_sorted = {}
+
+        def sort_x(i):
+            x_sorted[i] = work.tile([P, 2, K // PACK], F32, tag="x_sorted", name=f"x_sorted{i}", align_bytes=64)
+            nc.scalar.copy(out=x_sorted[i][:], in_=x_raw[i][:].bitcast(F32).rearrange("p (w u) -> p u w", u=2))
+
         def transpose_x(h0, banks):
             for h, b in enumerate(banks, h0):
                 words = x_raw[h // 2][:].bitcast(F32)
@@ -161,17 +171,19 @@ def tile_pls_concentration_loadings_s7_kernel(
                 for gl in range(2):
                     g = 2 * (h % 2) + gl
                     for u in range(2):
-                        nc.tensor.transpose(
-                            view[:, u, gl, :], words[:, 256 * g + u : 256 * (g + 1) : 2], ident[:]
-                        )
+                        if h // 2 in x_sorted:
+                            source = x_sorted[h // 2][:, u, P * g : P * (g + 1)]
+                        else:
+                            source = words[:, 256 * g + u : 256 * (g + 1) : 2]
+                        nc.tensor.transpose(view[:, u, gl, :], source, ident[:])
 
         def centre_x(h0, count, tag=None):
-            tag = tag or ("x_even", "x_odd")[len(x_grouped) % 2]
+            tag = tag or ("x_even", "x_odd")[h0 // 2 % 2]
             x_grouped[h0] = stage.tile(
                 [P, count, 2, P, 2, 2], BF16, tag=tag, name=f"x_grouped{h0}", align_bytes=64
             )
-            codes = work.tile([P, 2 * P * count], U32, tag="x_codes", name=f"x_codes{h0}", bufs=4, align_bytes=64)
-            scales = work.tile([P, 2 * P * count], U8, tag="x_scales", name=f"x_scales{h0}", bufs=4, align_bytes=64)
+            codes = work.tile([P, 2 * P * count], U32, tag="x_codes", name=f"x_codes{h0}", bufs=5, align_bytes=64)
+            scales = work.tile([P, 2 * P * count], U8, tag="x_scales", name=f"x_scales{h0}", bufs=5, align_bytes=64)
             x_quantised[h0] = (codes, scales)
             for n in range(count):
                 b = (h0 + n) % 2
@@ -189,6 +201,11 @@ def tile_pls_concentration_loadings_s7_kernel(
             flat = x_grouped[h0][:].rearrange("p n g s u e -> p (n g s u e)")
             cols = slice(2 * P * n0, 2 * P * n1)
             quantise(codes[:, cols], scales[:, cols], flat[:, PACK * cols.start : PACK * cols.stop])
+
+        def warm_up(count):
+            idle = bank(7, "warm_up")
+            for n in range(count):
+                nc.tensor.matmul(idle[:], lhsT=x_raw[0][:, :P], rhs=x_raw[0][:, :512], start=True, stop=True)
 
         t_banks = {}
         z_planes = {}
@@ -215,42 +232,48 @@ def tile_pls_concentration_loadings_s7_kernel(
                 z_planes[g] = work.tile([P, PACK, C], BF16, tag="z_planes", name=f"z_planes{g}", align_bytes=64)
             scale_out(engine, z_planes[g][:, j, c0:c1], t_banks[i, c0][:, : c1 - c0], weight_sb[:, i : i + 1])
 
-        def interleave_z(g, c0, c1, engine):
-            if g not in z_grouped:
-                z_grouped[g] = work.tile([P, C, PACK], BF16, tag="z_grouped", name=f"z_grouped{g}", align_bytes=64)
-            interleave(engine, z_grouped[g][:, c0:c1, :], z_planes[g][:, :, c0:c1])
+        def interleave_z(n, b0, b1, engine, tag="z_half"):
+            g, c0 = n // 2, HALF_C * (n % 2)
+            if n not in z_grouped:
+                z_grouped[n] = stage.tile([P, HALF_C, PACK], BF16, tag=tag, name=f"z_grouped{n}", align_bytes=64)
+            interleave(engine, z_grouped[n][:, b0:b1, :], z_planes[g][:, :, c0 + b0 : c0 + b1])
 
-        def quantise_z(g, c0, c1):
-            quantise(
-                z_codes[g][:, c0:c1], z_scales[g][:, c0:c1],
-                z_grouped[g][:].rearrange("p c j -> p (c j)")[:, PACK * c0 : PACK * c1],
-            )
+        def quantise_z(n):
+            g, cols = n // 2, slice(HALF_C * (n % 2), HALF_C * (n % 2 + 1))
+            quantise(z_codes[g][:, cols], z_scales[g][:, cols], z_grouped[n][:].rearrange("p c j -> p (c j)"))
 
-        y_planes = {}
+        edges = [0, 256] + [HALF_A * n for n in range(1, len(Y_ORDER) + 1)]
+        y_planes = {
+            n0: keep.tile([P, PACK, n1 - n0], BF16, name=f"y_planes{n0}", align_bytes=64)
+            for n0, n1 in zip(edges, edges[1:])
+        }
         y_grouped = {}
 
-        def widen_y(s):
-            y_planes[s] = work.tile([P, PACK, widths[s]], BF16, tag="y_planes", name=f"y_planes{s}", bufs=Y_BUFS, align_bytes=64)
-            at = 0
-            for g, a0, a1 in slices[s]:
-                for j in range(PACK):
-                    nc.scalar.activation(
-                        y_planes[s][:, j, at : at + a1 - a0], y_raw[g][:, j, a0:a1].bitcast(FP8), COPY,
-                        scale=y_scale_sb[:, g, j : j + 1],
-                    )
-                at += a1 - a0
+        def widen_y(n, rows=range(PACK), a0=0, a1=HALF_A):
+            g, half = Y_ORDER[n]
+            for j in rows:
+                nc.scalar.activation(
+                    y_planes[HALF_A * n + a0][:, j, :],
+                    y_raw[g][:, j, HALF_A * half + a0 : HALF_A * half + a1].bitcast(FP8),
+                    COPY, scale=y_scale_sb[:, g, j : j + 1],
+                )
 
-        def interleave_y(s, b0, b1, engine, tag="y_slice"):
-            if s not in y_grouped:
-                y_grouped[s] = stage.tile([P, widths[s], PACK], BF16, tag=tag, name=f"y_grouped{s}", align_bytes=64)
-            interleave(engine, y_grouped[s][:, b0:b1, :], y_planes[s][:, :, b0:b1])
+        rows_left = [(n, j) for n in range(1, len(Y_ORDER)) for j in range(PACK)]
 
-        def quantise_y(s, b0, b1):
-            flat = y_grouped[s][:].rearrange("p a j -> p (a j)")
-            n0 = columns[s][b0]
-            assert columns[s][b1 - 1] == n0 + b1 - b0 - 1
-            cols = slice(n0, n0 + b1 - b0)
-            quantise(y_codes[:, cols], y_scales[:, cols], flat[:, PACK * b0 : PACK * b1])
+        def widen_next(count):
+            for n, j in rows_left[:count]:
+                widen_y(n, [j])
+                rows_left.remove((n, j))
+
+        def interleave_y(n0, n1, b0, b1, engine, tag="y_slice"):
+            if n0 not in y_grouped:
+                y_grouped[n0] = stage.tile([P, n1 - n0, PACK], BF16, tag=tag, name=f"y_grouped{n0}", align_bytes=64)
+            edge = max(e for e in edges if e <= n0 + b0)
+            a0 = n0 + b0 - edge
+            interleave(engine, y_grouped[n0][:, b0:b1, :], y_planes[edge][:, :, a0 : a0 + b1 - b0])
+
+        def quantise_y(n0, n1):
+            quantise(y_codes[:, n0:n1], y_scales[:, n0:n1], y_grouped[n0][:].rearrange("p a j -> p (a j)"))
 
         cov_banks = {}
 
@@ -258,7 +281,8 @@ def tile_pls_concentration_loadings_s7_kernel(
             if g == 0:
                 cov_banks[m, a0] = bank(b, f"cov_sum{m}_{a0}")
             c_cols = slice(P * m, P * (m + 1))
-            n_cols = slice(A * g + a0, A * g + a0 + width)
+            n0 = HALF_A * Y_ORDER.index((g, a0 // HALF_A)) + a0 % HALF_A
+            n_cols = slice(n0, n0 + width)
             nc.tensor.matmul_mx(
                 out=cov_banks[m, a0][:, :width],
                 lhsT=z_codes[g][:, c_cols].bitcast(FP8X4),
@@ -275,9 +299,6 @@ def tile_pls_concentration_loadings_s7_kernel(
             nc.sync.dma_start(out=out[P * m : P * (m + 1), a0 : a0 + width], in_=res[:])
 
         last = G_S - 1
-        slices = [[(0, 0, 256)], [(0, 256, 576)], [(0, 576, 832)], [(0, 832, 1024), (1, 0, 128)], [(1, 128, 384)], [(1, 384, 640)], [(1, 640, 960)], [(1, 960, 1024), (2, 0, 192)], [(2, 192, 512)], [(2, 512, 768)], [(3, 0, 256)], [(3, 256, 512)], [(2, 768, 1024)], [(3, 512, 768)], [(3, 768, 1024)]]
-        widths = [sum(a1 - a0 for g, a0, a1 in pieces) for pieces in slices]
-        columns = [[A * g + a for g, a0, a1 in pieces for a in range(a0, a1)] for pieces in slices]
 
         transpose_x(0, (0, 1))
         centre_x(0, 2, "x_even")
@@ -286,10 +307,14 @@ def tile_pls_concentration_loadings_s7_kernel(
         quantise_x(0, 0, 1)
         quantise_x(0, 1, 2)
         quantise_r(0)
+        if WARM[0]:
+            warm_up(WARM[0])
         transpose_x(2, (2, 3))
         multiply_t(0, 4, [0])
-        interleave_r(1, 0, 176, nc.gpsimd)
-        interleave_r(1, 176, 512, nc.scalar)
+        if WARM[1]:
+            warm_up(WARM[1])
+        interleave_r(1, 0, R_POOL, nc.gpsimd)
+        interleave_r(1, R_POOL, 512, nc.scalar)
         centre_x(2, 2, "x_odd")
         quantise_x(2, 0, 1)
         quantise_x(2, 1, 2)
@@ -298,81 +323,82 @@ def tile_pls_concentration_loadings_s7_kernel(
         multiply_t(1, 5, [0])
         multiply_t(0, 4, [1])
         multiply_t(1, 5, [1])
-        interleave_r(2, 0, 176, nc.gpsimd)
-        interleave_r(2, 176, 512, nc.scalar)
+        interleave_r(2, 0, R_POOL, nc.gpsimd)
+        interleave_r(2, R_POOL, 512, nc.scalar)
         centre_x(4, 2, "tail_a")
         quantise_x(4, 0, 1)
         quantise_x(4, 1, 2)
         quantise_r(2)
         transpose_x(6, (2, 3))
-        multiply_t(0, 4, [2])
-        multiply_t(1, 5, [2])
-        multiply_t(2, 6, [0, 1, 2])
-        interleave_r(3, 0, 176, nc.gpsimd)
-        interleave_r(3, 176, 512, nc.scalar)
+        multiply_t(2, 6, [0, 1])
+        for n in range(3):
+            multiply_t(n, None, [2])
+        interleave_r(3, 0, R_POOL, nc.gpsimd)
+        interleave_r(3, R_POOL, 512, nc.scalar)
         centre_x(6, 2, "y_slice")
         quantise_x(6, 0, 1)
         quantise_x(6, 1, 2)
         quantise_r(3)
-        widen_y(0)
+        widen_y(0, a1=256)
         nc.scalar.copy(out=weight_sb[:], in_=weight_bf[:].rearrange("p g j -> p (g j)"))
-        widen_y(1)
+        widen_y(0, a0=256)
 
         transpose_x(8, (0, 1))
-        interleave_y(0, 0, widths[0], nc.gpsimd)
-        centre_x(8, 2)
+        interleave_y(0, 256, 0, 256, nc.gpsimd, "z_half")
+        centre_x(8, 1, "y_slice")
+        centre_x(9, 1, "x_even")
+        multiply_t(3, 7, [0, 1])
         for n in range(3):
             multiply_t(n, None, [3])
         weigh_t(0, nc.vector)
-        weigh_t(1, nc.vector)
-        widen_y(2)
-        quantise_y(0, 0, widths[0])
-        quantise_x(8, 0, 2)
+        weigh_t(1, nc.vector if V_WEIGH else nc.scalar)
+        weigh_t(2, nc.scalar)
+        widen_next(2)
+        quantise_x(8, 0, 1)
+        quantise_x(9, 0, 1)
 
-        def z_piece(n):
-            return n // PACK, P * (n % PACK), P * (n % PACK + 1)
-
-        for i in range(5, 14):
-            s = i - 4
+        for i in range(5, 15):
             use = 2 * i if i < 10 else 3 * i - 10
+            n0 = 256 * (i - 4 - (i + 1) % 2)
+            z = (i - 6) // 2
+            if i + 7 < N_TILES:
+                load_x(i + 7)
             transpose_x(2 * i, (use % 4, (use + 1) % 4))
-            interleave_y(s, 0, Y_POOL, nc.gpsimd)
+            if i % 2:
+                interleave_y(n0, n0 + 512, 0, POOL, nc.gpsimd)
+            else:
+                interleave_z(z, 0, POOL, nc.gpsimd)
             centre_x(2 * i, 2)
-            multiply_t(i - 2, 4 + (i - 2) % 4 if i < 10 else (use + 2) % 4)
+            multiply_t(i - 2, 4 + (i - 2) % 4 if i < 10 else (use + 2) % 4, range(2 if i == 5 else 0, G_K))
             if i >= 8:
                 multiply_cov((i - 8) % PACK, 0, (i - 8) // PACK, 4 + (i - 8) % PACK)
-            weigh_t(i - 3, nc.scalar)
-            interleave_y(s, Y_POOL, widths[s], nc.scalar)
-            if i >= 6:
-                g, c0, c1 = z_piece(i - 6)
-                if Z_SCALAR:
-                    interleave_z(g, c0, c0 + Z_SCALAR, nc.scalar)
-            widen_y(s + 2)
-            if i >= 6:
-                interleave_z(g, c0 + Z_SCALAR, c1, nc.vector)
-            if i >= 7:
-                quantise_z(*z_piece(i - 7))
-            if widths[s] > 256:
-                quantise_y(s, 256, widths[s])
-            quantise_y(s, 0, 256)
+            if i % 2:
+                if i == 5:
+                    weigh_t(i - 2, nc.scalar)
+                widen_next(3 if i in EXTRA else 2)
+                if i + 2 in SORTED:
+                    sort_x(i + 2)
+                if i > 5:
+                    weigh_t(i - 2, nc.scalar)
+                interleave_y(n0, n0 + 512, 256 + Y_VECTOR, 512, nc.scalar)
+                if i > 5:
+                    quantise_z(z)
+                else:
+                    quantise_y(0, 256)
+            else:
+                widen_next(3 if i in EXTRA else 2)
+                interleave_y(n0, n0 + 512, POOL, 256, nc.vector)
+                if Y_VECTOR:
+                    interleave_y(n0, n0 + 512, 256, 256 + Y_VECTOR, nc.vector)
+                interleave_z(z, POOL, HALF_C, nc.vector)
+                quantise_y(n0, n0 + 512)
+                if i + 2 in SORTED:
+                    sort_x(i + 2)
+                weigh_t(i - 2, nc.scalar)
             quantise_x(2 * i, 0, 2)
 
-        transpose_x(28, (0, 1))
-        interleave_y(10, 0, Y_POOL, nc.gpsimd)
-        centre_x(28, 2)
-        multiply_t(12, 2)
-        multiply_cov(2, 0, 1)
-        weigh_t(11, nc.scalar)
-        interleave_y(10, Y_POOL, widths[10], nc.scalar)
-        widen_y(12)
-        widen_y(13)
-        interleave_z(2, 0, HALF_C, nc.vector)
-        quantise_z(*z_piece(7))
-        quantise_y(10, 0, 256)
-        quantise_x(28, 0, 2)
-
         transpose_x(30, (3, 0))
-        interleave_y(11, 0, Y_POOL, nc.gpsimd)
+        interleave_y(2816, 3328, 0, POOL, nc.gpsimd)
         centre_x(30, 2)
         quantise_x(30, 0, 1)
         quantise_x(30, 1, 2)
@@ -380,49 +406,46 @@ def tile_pls_concentration_loadings_s7_kernel(
         multiply_t(14, 2)
         multiply_t(15, 3, c1=HALF_C)
         multiply_t(15, 0, c0=HALF_C)
-        weigh_t(12, nc.scalar)
-        interleave_y(11, Y_POOL, widths[11], nc.scalar)
-        widen_y(14)
-        nc.scalar.copy(out=inv_sb[:], in_=inv_bf[:, :, 0])
+        interleave_y(2816, 3328, POOL, 256, nc.scalar)
+        interleave_y(2816, 3328, 256, 512, nc.scalar)
+        widen_next(1)
         weigh_t(13, nc.scalar)
-        quantise_z(2, 0, HALF_C)
-        interleave_z(2, HALF_C, C, nc.vector)
-        quantise_y(11, 0, 256)
-        quantise_z(2, HALF_C, C)
+        nc.scalar.copy(out=inv_sb[:], in_=inv_bf[:, :, 0])
+        widen_next(1)
+        quantise_z(4)
+        interleave_z(5, 0, HALF_C, nc.vector, "tail_a")
+        quantise_y(2816, 3328)
+        quantise_z(5)
         weigh_t(14, nc.scalar)
         weigh_t(15, nc.scalar, c1=HALF_C)
         weigh_t(15, nc.scalar, c0=HALF_C)
-        interleave_y(12, 0, 256, nc.scalar, "tail_a")
-        interleave_y(13, 0, 256, nc.scalar, "tail_b")
-        interleave_y(14, 0, 256, nc.vector, "x_odd")
-        interleave_z(3, 0, HALF_C, nc.vector)
-        quantise_y(14, 0, 256)
-        quantise_z(3, 0, HALF_C)
-        interleave_z(3, HALF_C, C, nc.vector)
-        quantise_y(12, 0, 256)
-        quantise_z(3, HALF_C, C)
+        widen_next(4)
+        interleave_z(6, 0, HALF_C, nc.vector)
+        interleave_y(3584, 4096, 0, TAIL_S, nc.scalar, "tail_b")
+        interleave_z(7, 0, HALF_C, nc.vector, "tail_a")
+        quantise_z(6)
+        quantise_z(7)
+        interleave_y(3328, 3584, 0, 256, nc.vector, "x_odd")
+        interleave_y(3584, 4096, TAIL_S, 512, nc.vector)
+        quantise_y(3328, 3584)
+        quantise_y(3584, 4096)
         multiply_cov(3, 0, 1)
         for m in range(4):
             multiply_cov(m, 0, 2)
-        for m in range(2):
-            for g in range(2):
-                multiply_cov(m, HALF_A, g, m + 1)
-        for m in range(2):
-            multiply_cov(m, 0, last)
-            store_cov(m, 0, nc.vector if m else nc.scalar)
-        quantise_y(13, 0, 256)
         for g in range(2):
-            multiply_cov(2, HALF_A, g, 3)
-        for m in range(2, 4):
+            multiply_cov(0, HALF_A, g, 1)
+        multiply_cov(1, HALF_A, 0, 2)
+        for m in range(4):
             multiply_cov(m, 0, last)
-            store_cov(m, 0, nc.scalar if m % 2 else nc.vector)
-        for m in range(2):
-            multiply_cov(m, HALF_A, 2)
-        for m in range(2):
-            multiply_cov(m, HALF_A, last)
-            store_cov(m, HALF_A, nc.scalar if m % 2 else nc.vector)
+            store_cov(m, 0, nc.scalar)
+        multiply_cov(1, HALF_A, 1)
         for g in range(2, G_S):
-            multiply_cov(2, HALF_A, g)
+            for m in range(2):
+                multiply_cov(m, HALF_A, g)
+        for m in range(2):
+            store_cov(m, HALF_A, nc.scalar if m else nc.vector)
+        for g in range(G_S):
+            multiply_cov(2, HALF_A, g, 3)
         store_cov(2, HALF_A, nc.vector)
         for a0, b, engine in ((512, 0, nc.scalar), (768, 4, nc.vector)):
             for g in range(G_S):

@@ -14,12 +14,12 @@ HALF_A = A // 2
 HALF_C = C // 2
 POOL = 200
 R_POOL = 200
-Y_VECTOR = 96
+Y_VECTOR = 64
 SORTED = ()
 V_WEIGH = 1
 TAIL_S = 448
 WARM = (0, 0)
-EXTRA = (9, 11, 12, 13, 14)
+EXTRA = (8, 9, 11, 12, 13, 14)
 X_BUFS = 12
 Y_ORDER = [(0, 0), (0, 1), (1, 0), (1, 1), (2, 0), (3, 0), (2, 1), (3, 1)]
 
@@ -277,7 +277,7 @@ def tile_pls_concentration_loadings_s7_kernel(
 
         cov_banks = {}
 
-        def multiply_cov(m, a0, g, b=None, width=HALF_A):
+        def multiply_cov(m, a0, g, b=None, width=HALF_A, final=G_S - 1):
             if g == 0:
                 cov_banks[m, a0] = bank(b, f"cov_sum{m}_{a0}")
             c_cols = slice(P * m, P * (m + 1))
@@ -290,7 +290,7 @@ def tile_pls_concentration_loadings_s7_kernel(
                 rhs=y_codes[:, n_cols].bitcast(FP8X4),
                 rhs_scale=y_scales[:, n_cols],
                 start=(g == 0),
-                stop=(g == G_S - 1),
+                stop=(g == final),
             )
 
         def store_cov(m, a0, engine, width=HALF_A):
@@ -346,17 +346,19 @@ def tile_pls_concentration_loadings_s7_kernel(
         transpose_x(8, (0, 1))
         interleave_y(0, 256, 0, 256, nc.gpsimd, "z_half")
         centre_x(8, 1, "y_slice")
-        centre_x(9, 1, "x_even")
-        multiply_t(3, 7, [0, 1])
+        centre_x(9, 1, "tail_a")
+        multiply_t(3, 7, [0])
         for n in range(3):
             multiply_t(n, None, [3])
+        multiply_t(3, None, [1])
         weigh_t(0, nc.vector)
         weigh_t(1, nc.vector if V_WEIGH else nc.scalar)
-        weigh_t(2, nc.scalar)
         widen_next(2)
+        weigh_t(2, nc.scalar)
         quantise_x(8, 0, 1)
         quantise_x(9, 0, 1)
 
+        shared = ("y_slice", "x_even")
         for i in range(5, 15):
             use = 2 * i if i < 10 else 3 * i - 10
             n0 = 256 * (i - 4 - (i + 1) % 2)
@@ -365,41 +367,39 @@ def tile_pls_concentration_loadings_s7_kernel(
                 load_x(i + 7)
             transpose_x(2 * i, (use % 4, (use + 1) % 4))
             if i % 2:
-                interleave_y(n0, n0 + 512, 0, POOL, nc.gpsimd)
+                interleave_y(n0, n0 + 512, 0, POOL, nc.gpsimd, shared[i // 2 % 2])
             else:
                 interleave_z(z, 0, POOL, nc.gpsimd)
-            centre_x(2 * i, 2)
+            centre_x(2 * i, 2, "x_odd" if i % 2 else shared[i // 2 % 2])
             multiply_t(i - 2, 4 + (i - 2) % 4 if i < 10 else (use + 2) % 4, range(2 if i == 5 else 0, G_K))
             if i >= 8:
                 multiply_cov((i - 8) % PACK, 0, (i - 8) // PACK, 4 + (i - 8) % PACK)
             if i % 2:
-                if i == 5:
-                    weigh_t(i - 2, nc.scalar)
                 widen_next(3 if i in EXTRA else 2)
                 if i + 2 in SORTED:
                     sort_x(i + 2)
-                if i > 5:
-                    weigh_t(i - 2, nc.scalar)
+                weigh_t(i - 2, nc.scalar)
                 interleave_y(n0, n0 + 512, 256 + Y_VECTOR, 512, nc.scalar)
+                interleave_y(n0, n0 + 512, POOL, 256, nc.vector)
                 if i > 5:
                     quantise_z(z)
                 else:
                     quantise_y(0, 256)
             else:
                 widen_next(3 if i in EXTRA else 2)
-                interleave_y(n0, n0 + 512, POOL, 256, nc.vector)
                 if Y_VECTOR:
                     interleave_y(n0, n0 + 512, 256, 256 + Y_VECTOR, nc.vector)
                 interleave_z(z, POOL, HALF_C, nc.vector)
-                quantise_y(n0, n0 + 512)
                 if i + 2 in SORTED:
                     sort_x(i + 2)
                 weigh_t(i - 2, nc.scalar)
             quantise_x(2 * i, 0, 2)
+            if i % 2 == 0:
+                quantise_y(n0, n0 + 512)
 
         transpose_x(30, (3, 0))
-        interleave_y(2816, 3328, 0, POOL, nc.gpsimd)
-        centre_x(30, 2)
+        interleave_y(2816, 3328, 0, POOL, nc.gpsimd, shared[1])
+        centre_x(30, 2, "x_odd")
         quantise_x(30, 0, 1)
         quantise_x(30, 1, 2)
         multiply_t(13, 1)
@@ -424,11 +424,11 @@ def tile_pls_concentration_loadings_s7_kernel(
         interleave_y(3584, 4096, 0, TAIL_S, nc.scalar, "tail_b")
         interleave_z(7, 0, HALF_C, nc.vector, "tail_a")
         quantise_z(6)
-        quantise_z(7)
-        interleave_y(3328, 3584, 0, 256, nc.vector, "x_odd")
         interleave_y(3584, 4096, TAIL_S, 512, nc.vector)
-        quantise_y(3328, 3584)
+        quantise_z(7)
+        interleave_y(3328, 3584, 0, 256, nc.vector, shared[0])
         quantise_y(3584, 4096)
+        quantise_y(3328, 3584)
         multiply_cov(3, 0, 1)
         for m in range(4):
             multiply_cov(m, 0, 2)
@@ -439,9 +439,9 @@ def tile_pls_concentration_loadings_s7_kernel(
             multiply_cov(m, 0, last)
             store_cov(m, 0, nc.scalar)
         multiply_cov(1, HALF_A, 1)
-        for g in range(2, G_S):
+        for g in (3, 2):
             for m in range(2):
-                multiply_cov(m, HALF_A, g)
+                multiply_cov(m, HALF_A, g, final=2)
         for m in range(2):
             store_cov(m, HALF_A, nc.scalar if m else nc.vector)
         for g in range(G_S):

@@ -12,12 +12,14 @@ G_S = S // PASS
 N_TILES = S // P
 HALF_A = A // 2
 HALF_C = C // 2
-POOL = 200
-R_POOL = 200
-Y_VECTOR = 64
+POOL = 192
+R_POOL = 192
+Y_VECTOR = 80
 SORTED = ()
 V_WEIGH = 1
-TAIL_S = 448
+TAIL_S = 192
+TAIL_V = 64
+EARLY = 1
 WARM = (0, 0)
 EXTRA = (8, 9, 11, 12, 13, 14)
 X_BUFS = 12
@@ -89,12 +91,12 @@ def tile_pls_concentration_loadings_s7_kernel(
         load_r(1)
         load_x(2)
         load_r(2)
+        nc.sync.dma_start(out=y_scale_sb[:], in_=y_scale.rearrange("(g p j) o -> p g (j o)", p=P, j=PACK))
+        nc.sync.dma_start(out=weight_bf[:], in_=weight.rearrange("(g p j) -> p g j", p=P, j=PACK))
         load_x(3)
         load_r(3)
         load_x(4)
-        nc.sync.dma_start(out=y_scale_sb[:], in_=y_scale.rearrange("(g p j) o -> p g (j o)", p=P, j=PACK))
         load_y(0, 0, 256)
-        nc.sync.dma_start(out=weight_bf[:], in_=weight.rearrange("(g p j) -> p g j", p=P, j=PACK))
         load_y(0, 256, 1024)
         load_x(5)
         load_x(6)
@@ -277,7 +279,7 @@ def tile_pls_concentration_loadings_s7_kernel(
 
         cov_banks = {}
 
-        def multiply_cov(m, a0, g, b=None, width=HALF_A, final=G_S - 1):
+        def multiply_cov(m, a0, g, b=None, width=HALF_A):
             if g == 0:
                 cov_banks[m, a0] = bank(b, f"cov_sum{m}_{a0}")
             c_cols = slice(P * m, P * (m + 1))
@@ -290,7 +292,7 @@ def tile_pls_concentration_loadings_s7_kernel(
                 rhs=y_codes[:, n_cols].bitcast(FP8X4),
                 rhs_scale=y_scales[:, n_cols],
                 start=(g == 0),
-                stop=(g == final),
+                stop=(g == G_S - 1),
             )
 
         def store_cov(m, a0, engine, width=HALF_A):
@@ -421,14 +423,15 @@ def tile_pls_concentration_loadings_s7_kernel(
         weigh_t(15, nc.scalar, c0=HALF_C)
         widen_next(4)
         interleave_z(6, 0, HALF_C, nc.vector)
+        interleave_y(3328, 3584, 0, 256, nc.scalar, shared[0])
         interleave_y(3584, 4096, 0, TAIL_S, nc.scalar, "tail_b")
         interleave_z(7, 0, HALF_C, nc.vector, "tail_a")
         quantise_z(6)
-        interleave_y(3584, 4096, TAIL_S, 512, nc.vector)
+        interleave_y(3584, 4096, TAIL_S, TAIL_S + TAIL_V, nc.vector)
         quantise_z(7)
-        interleave_y(3328, 3584, 0, 256, nc.vector, shared[0])
-        quantise_y(3584, 4096)
+        interleave_y(3584, 4096, TAIL_S + TAIL_V, 512, nc.vector)
         quantise_y(3328, 3584)
+        quantise_y(3584, 4096)
         multiply_cov(3, 0, 1)
         for m in range(4):
             multiply_cov(m, 0, 2)
@@ -439,12 +442,14 @@ def tile_pls_concentration_loadings_s7_kernel(
             multiply_cov(m, 0, last)
             store_cov(m, 0, nc.scalar)
         multiply_cov(1, HALF_A, 1)
-        for g in (3, 2):
-            for m in range(2):
-                multiply_cov(m, HALF_A, g, final=2)
         for m in range(2):
+            multiply_cov(m, HALF_A, 2)
+        for g in range(EARLY):
+            multiply_cov(2, HALF_A, g, 3)
+        for m in range(2):
+            multiply_cov(m, HALF_A, last)
             store_cov(m, HALF_A, nc.scalar if m else nc.vector)
-        for g in range(G_S):
+        for g in range(EARLY, G_S):
             multiply_cov(2, HALF_A, g, 3)
         store_cov(2, HALF_A, nc.vector)
         for a0, b, engine in ((512, 0, nc.scalar), (768, 4, nc.vector)):

@@ -16,8 +16,9 @@ POOL = 192
 R_POOL = 192
 Y_VECTOR = 80
 SORTED = ()
+GAP = 64
 V_WEIGH = 1
-TAIL_S = 192
+TAIL_S = 224
 TAIL_V = 64
 EARLY = 1
 WARM = (0, 0)
@@ -55,9 +56,10 @@ def tile_pls_concentration_loadings_s7_kernel(
         ctx.enter_context(tc.manual_schedule())
 
         mean_sb = keep.tile([P, G_K, 2, 2], BF16, name="mean_sb")
-        weight_bf = keep.tile([P, G_S, PACK], BF16, name="weight_bf")
+        first_weight = keep.tile([P, 1, PACK], BF16, name="first_weight")
+        later_weight = keep.tile([P, G_S - 1, PACK], BF16, name="later_weight")
         weight_sb = keep.tile([P, G_S * PACK], F32, name="weight_sb")
-        y_scale_sb = keep.tile([P, G_S, PACK], F32, name="y_scale_sb")
+        y_scale_sb = [keep.tile([P, PACK], F32, name=f"y_scale_sb{g}") for g in range(G_S)]
         inv_bf = keep.tile([P, 4, 2], BF16, name="inv_bf")
         inv_sb = keep.tile([P, 4], F32, name="inv_sb")
 
@@ -81,33 +83,40 @@ def tile_pls_concentration_loadings_s7_kernel(
         def load_y(g, a0=0, a1=A):
             nc.sync.dma_start(out=y_raw[g][:, :, a0:a1], in_=y_hbm[g][:, :, a0:a1])
 
-        nc.scalar.dma_start(
-            out=mean_sb[:].rearrange("p g u e -> p g (u e)"),
-            in_=mean.rearrange("(g p t) -> p g t", p=P, t=PACK),
-        )
+        def load_scale(g):
+            nc.sync.dma_start(out=y_scale_sb[g][:], in_=y_scale_hbm[:, g])
+
+        mean_hbm = mean.rearrange("(g p t) -> p g t", p=P, t=PACK)
+        y_scale_hbm = y_scale.rearrange("(g p j) o -> p g (j o)", p=P, j=PACK)
+        weight_hbm = weight.rearrange("(g p j) -> p g j", p=P, j=PACK)
+        nc.scalar.dma_start(out=mean_sb[:].rearrange("p g u e -> p g (u e)"), in_=mean_hbm)
         load_x(0, 2)
         load_r(0)
         load_x(1)
         load_r(1)
         load_x(2)
         load_r(2)
-        nc.sync.dma_start(out=y_scale_sb[:], in_=y_scale.rearrange("(g p j) o -> p g (j o)", p=P, j=PACK))
-        nc.sync.dma_start(out=weight_bf[:], in_=weight.rearrange("(g p j) -> p g j", p=P, j=PACK))
         load_x(3)
         load_r(3)
+        load_scale(0)
         load_x(4)
         load_y(0, 0, 256)
+        nc.sync.dma_start(out=first_weight[:], in_=weight_hbm[:, :1])
         load_y(0, 256, 1024)
         load_x(5)
         load_x(6)
-        load_x(7)
+        nc.sync.dma_start(out=later_weight[:], in_=weight_hbm[:, 1:])
+        load_scale(1)
         load_y(1)
+        load_x(7)
         load_x(8)
         load_x(9)
+        load_scale(2)
         load_y(2)
         load_x(10)
         load_x(11)
         nc.sync.dma_start(out=inv_bf[:, :, 0:1], in_=inv_score.rearrange("(m p o) -> p m o", p=P, o=1))
+        load_scale(3)
         load_y(3)
 
         r_codes = keep.tile([P, G_K, C], U32, name="r_codes", align_bytes=64)
@@ -257,7 +266,7 @@ def tile_pls_concentration_loadings_s7_kernel(
                 nc.scalar.activation(
                     y_planes[HALF_A * n + a0][:, j, :],
                     y_raw[g][:, j, HALF_A * half + a0 : HALF_A * half + a1].bitcast(FP8),
-                    COPY, scale=y_scale_sb[:, g, j : j + 1],
+                    COPY, scale=y_scale_sb[g][:, j : j + 1],
                 )
 
         rows_left = [(n, j) for n in range(1, len(Y_ORDER)) for j in range(PACK)]
@@ -342,7 +351,7 @@ def tile_pls_concentration_loadings_s7_kernel(
         quantise_x(6, 1, 2)
         quantise_r(3)
         widen_y(0, a1=256)
-        nc.scalar.copy(out=weight_sb[:], in_=weight_bf[:].rearrange("p g j -> p (g j)"))
+        nc.scalar.copy(out=weight_sb[:, :PACK], in_=first_weight[:, 0])
         widen_y(0, a0=256)
 
         transpose_x(8, (0, 1))
@@ -389,6 +398,8 @@ def tile_pls_concentration_loadings_s7_kernel(
                     quantise_y(0, 256)
             else:
                 widen_next(3 if i in EXTRA else 2)
+                if i == 6:
+                    nc.scalar.copy(out=weight_sb[:, PACK:], in_=later_weight[:].rearrange("p g j -> p (g j)"))
                 if Y_VECTOR:
                     interleave_y(n0, n0 + 512, 256, 256 + Y_VECTOR, nc.vector)
                 interleave_z(z, POOL, HALF_C, nc.vector)
@@ -410,10 +421,9 @@ def tile_pls_concentration_loadings_s7_kernel(
         multiply_t(15, 0, c0=HALF_C)
         interleave_y(2816, 3328, POOL, 256, nc.scalar)
         interleave_y(2816, 3328, 256, 512, nc.scalar)
-        widen_next(1)
         weigh_t(13, nc.scalar)
         nc.scalar.copy(out=inv_sb[:], in_=inv_bf[:, :, 0])
-        widen_next(1)
+        interleave_y(3328, 3584, 0, GAP, nc.scalar, shared[0])
         quantise_z(4)
         interleave_z(5, 0, HALF_C, nc.vector, "tail_a")
         quantise_y(2816, 3328)
@@ -421,9 +431,8 @@ def tile_pls_concentration_loadings_s7_kernel(
         weigh_t(14, nc.scalar)
         weigh_t(15, nc.scalar, c1=HALF_C)
         weigh_t(15, nc.scalar, c0=HALF_C)
-        widen_next(4)
         interleave_z(6, 0, HALF_C, nc.vector)
-        interleave_y(3328, 3584, 0, 256, nc.scalar, shared[0])
+        interleave_y(3328, 3584, GAP, 256, nc.scalar)
         interleave_y(3584, 4096, 0, TAIL_S, nc.scalar, "tail_b")
         interleave_z(7, 0, HALF_C, nc.vector, "tail_a")
         quantise_z(6)
@@ -452,7 +461,7 @@ def tile_pls_concentration_loadings_s7_kernel(
         for g in range(EARLY, G_S):
             multiply_cov(2, HALF_A, g, 3)
         store_cov(2, HALF_A, nc.vector)
-        for a0, b, engine in ((512, 0, nc.scalar), (768, 4, nc.vector)):
+        for a0, width, b, engine in ((512, 256, 0, nc.scalar), (768, 128, 4, nc.vector), (896, 128, 5, nc.scalar)):
             for g in range(G_S):
-                multiply_cov(3, a0, g, b, 256)
-            store_cov(3, a0, engine, 256)
+                multiply_cov(3, a0, g, b, width)
+            store_cov(3, a0, engine, width)

@@ -64,15 +64,15 @@ def tile_pls_concentration_loadings_s7_kernel(
         inv_sb = keep.tile([P, 4], F32, name="inv_sb")
 
         x_raw = {}
-        r_raw = [keep.tile([P, PACK, C], BF16, name=f"r_raw{g}", align_bytes=64) for g in range(G_K)]
-        y_raw = [keep.tile([P, PACK, A], U8, name=f"y_raw{g}", align_bytes=64) for g in range(G_S)]
+        r_raw = [keep.tile([P, PACK, C], BF16, name=f"r_raw{g}", align_bytes=256) for g in range(G_K)]
+        y_raw = [keep.tile([P, PACK, A], U8, name=f"y_raw{g}", align_bytes=256) for g in range(G_S)]
 
         x_hbm = spectra.rearrange("(g p j) k -> g j p k", p=P, j=PACK)
         r_hbm = r.rearrange("(g p j) c -> g p j c", p=P, j=PACK)
         y_hbm = y_bytes.rearrange("(g p j) a -> g p j a", p=P, j=PACK)
 
         def load_x(i, pieces=1):
-            x_raw[i] = work.tile([P, K], BF16, tag="x_raw", name=f"x_raw{i}", bufs=X_BUFS, align_bytes=64)
+            x_raw[i] = work.tile([P, K], BF16, tag="x_raw", name=f"x_raw{i}", bufs=X_BUFS, align_bytes=256)
             for n in range(pieces):
                 cols = slice(K * n // pieces, K * (n + 1) // pieces)
                 nc.sync.dma_start(out=x_raw[i][:, cols], in_=x_hbm[i // PACK, i % PACK][:, cols])
@@ -119,12 +119,12 @@ def tile_pls_concentration_loadings_s7_kernel(
         load_scale(3)
         load_y(3)
 
-        r_codes = keep.tile([P, G_K, C], U32, name="r_codes", align_bytes=64)
-        r_scales = keep.tile([P, G_K, C], U8, name="r_scales", align_bytes=64)
-        y_codes = keep.tile([P, G_S * A], U32, name="y_codes", align_bytes=64)
-        y_scales = keep.tile([P, G_S * A], U8, name="y_scales", align_bytes=64)
-        z_codes = [keep.tile([P, C], U32, name=f"z_codes{g}", align_bytes=64) for g in range(G_S)]
-        z_scales = [keep.tile([P, C], U8, name=f"z_scales{g}", align_bytes=64) for g in range(G_S)]
+        r_codes = keep.tile([P, G_K, C], U32, name="r_codes", align_bytes=256)
+        r_scales = keep.tile([P, G_K, C], U8, name="r_scales", align_bytes=256)
+        y_codes = keep.tile([P, G_S * A], U32, name="y_codes", align_bytes=256)
+        y_scales = keep.tile([P, G_S * A], U8, name="y_scales", align_bytes=256)
+        z_codes = [keep.tile([P, C], U32, name=f"z_codes{g}", align_bytes=256) for g in range(G_S)]
+        z_scales = [keep.tile([P, C], U8, name=f"z_scales{g}", align_bytes=256) for g in range(G_S)]
 
         def bank(b, name):
             return psum.tile([P, 512], F32, tag=f"bank{b}", name=name)
@@ -156,7 +156,7 @@ def tile_pls_concentration_loadings_s7_kernel(
 
         def interleave_r(g, c0, c1, engine):
             if g not in r_grouped:
-                r_grouped[g] = stage.tile([P, C, PACK], BF16, tag=("tail_a", "x_even", "x_odd", "tail_a")[g], name=f"r_grouped{g}", align_bytes=64)
+                r_grouped[g] = stage.tile([P, C, PACK], BF16, tag=("tail_a", "x_even", "x_odd", "tail_a")[g], name=f"r_grouped{g}", align_bytes=256)
             interleave(engine, r_grouped[g][:, c0:c1, :], r_raw[g][:, :, c0:c1])
 
         def quantise_r(g):
@@ -171,7 +171,7 @@ def tile_pls_concentration_loadings_s7_kernel(
         x_sorted = {}
 
         def sort_x(i):
-            x_sorted[i] = work.tile([P, 2, K // PACK], F32, tag="x_sorted", name=f"x_sorted{i}", align_bytes=64)
+            x_sorted[i] = work.tile([P, 2, K // PACK], F32, tag="x_sorted", name=f"x_sorted{i}", align_bytes=256)
             nc.scalar.copy(out=x_sorted[i][:], in_=x_raw[i][:].bitcast(F32).rearrange("p (w u) -> p u w", u=2))
 
         def transpose_x(h0, banks):
@@ -191,10 +191,10 @@ def tile_pls_concentration_loadings_s7_kernel(
         def centre_x(h0, count, tag=None):
             tag = tag or ("x_even", "x_odd")[h0 // 2 % 2]
             x_grouped[h0] = stage.tile(
-                [P, count, 2, P, 2, 2], BF16, tag=tag, name=f"x_grouped{h0}", align_bytes=64
+                [P, count, 2, P, 2, 2], BF16, tag=tag, name=f"x_grouped{h0}", align_bytes=256
             )
-            codes = work.tile([P, 2 * P * count], U32, tag="x_codes", name=f"x_codes{h0}", bufs=5, align_bytes=64)
-            scales = work.tile([P, 2 * P * count], U8, tag="x_scales", name=f"x_scales{h0}", bufs=5, align_bytes=64)
+            codes = work.tile([P, 2 * P * count], U32, tag="x_codes", name=f"x_codes{h0}", bufs=5, align_bytes=256)
+            scales = work.tile([P, 2 * P * count], U8, tag="x_scales", name=f"x_scales{h0}", bufs=5, align_bytes=256)
             x_quantised[h0] = (codes, scales)
             for n in range(count):
                 b = (h0 + n) % 2
@@ -240,13 +240,13 @@ def tile_pls_concentration_loadings_s7_kernel(
         def weigh_t(i, engine, c0=0, c1=C):
             g, j = i // PACK, i % PACK
             if g not in z_planes:
-                z_planes[g] = work.tile([P, PACK, C], BF16, tag="z_planes", name=f"z_planes{g}", align_bytes=64)
+                z_planes[g] = work.tile([P, PACK, C], BF16, tag="z_planes", name=f"z_planes{g}", align_bytes=256)
             scale_out(engine, z_planes[g][:, j, c0:c1], t_banks[i, c0][:, : c1 - c0], weight_sb[:, i : i + 1])
 
         def interleave_z(n, b0, b1, engine, tag="z_half"):
             g, c0 = n // 2, HALF_C * (n % 2)
             if n not in z_grouped:
-                z_grouped[n] = stage.tile([P, HALF_C, PACK], BF16, tag=tag, name=f"z_grouped{n}", align_bytes=64)
+                z_grouped[n] = stage.tile([P, HALF_C, PACK], BF16, tag=tag, name=f"z_grouped{n}", align_bytes=256)
             interleave(engine, z_grouped[n][:, b0:b1, :], z_planes[g][:, :, c0 + b0 : c0 + b1])
 
         def quantise_z(n):
@@ -255,7 +255,7 @@ def tile_pls_concentration_loadings_s7_kernel(
 
         edges = [0, 256] + [HALF_A * n for n in range(1, len(Y_ORDER) + 1)]
         y_planes = {
-            n0: keep.tile([P, PACK, n1 - n0], BF16, name=f"y_planes{n0}", align_bytes=64)
+            n0: keep.tile([P, PACK, n1 - n0], BF16, name=f"y_planes{n0}", align_bytes=256)
             for n0, n1 in zip(edges, edges[1:])
         }
         y_grouped = {}
@@ -278,7 +278,7 @@ def tile_pls_concentration_loadings_s7_kernel(
 
         def interleave_y(n0, n1, b0, b1, engine, tag="y_slice"):
             if n0 not in y_grouped:
-                y_grouped[n0] = stage.tile([P, n1 - n0, PACK], BF16, tag=tag, name=f"y_grouped{n0}", align_bytes=64)
+                y_grouped[n0] = stage.tile([P, n1 - n0, PACK], BF16, tag=tag, name=f"y_grouped{n0}", align_bytes=256)
             edge = max(e for e in edges if e <= n0 + b0)
             a0 = n0 + b0 - edge
             interleave(engine, y_grouped[n0][:, b0:b1, :], y_planes[edge][:, :, a0 : a0 + b1 - b0])
@@ -305,7 +305,7 @@ def tile_pls_concentration_loadings_s7_kernel(
             )
 
         def store_cov(m, a0, engine, width=HALF_A):
-            res = keep.tile([P, width], F32, name=f"res{m}_{a0}")
+            res = keep.tile([P, width], F32, name=f"res{m}_{a0}", align_bytes=256)
             scale_out(engine, res[:], cov_banks[m, a0][:, :width], inv_sb[:, m : m + 1])
             nc.sync.dma_start(out=out[P * m : P * (m + 1), a0 : a0 + width], in_=res[:])
 
@@ -461,7 +461,7 @@ def tile_pls_concentration_loadings_s7_kernel(
         for g in range(EARLY, G_S):
             multiply_cov(2, HALF_A, g, 3)
         store_cov(2, HALF_A, nc.vector)
-        for a0, width, b, engine in ((512, 256, 0, nc.scalar), (768, 128, 4, nc.vector), (896, 128, 5, nc.scalar)):
+        for a0, width, b, engine in ((512, 256, 0, nc.scalar), (768, 256, 4, nc.vector)):
             for g in range(G_S):
                 multiply_cov(3, a0, g, b, width)
             store_cov(3, a0, engine, width)

@@ -21,7 +21,7 @@ V_WEIGH = 1
 TAIL_S = 224
 TAIL_V = 64
 EARLY = 1
-WARM = (0, 0)
+WARM = (3, 1)
 EXTRA = (8, 9, 11, 12, 13, 14)
 X_BUFS = 12
 Y_ORDER = [(0, 0), (0, 1), (1, 0), (1, 1), (2, 0), (3, 0), (2, 1), (3, 1)]

@@ -12,7 +12,7 @@ G_S = S // PASS
 N_TILES = S // P
 HALF_A = A // 2
 HALF_C = C // 2
-POOL = 192
+POOL = 216
 R_POOL = 192
 Y_VECTOR = 80
 SORTED = ()
@@ -130,18 +130,14 @@ def tile_pls_concentration_loadings_s7_kernel(
             return psum.tile([P, 512], F32, tag=f"bank{b}", name=name)
 
         def interleave(engine, dst, src):
+            dst = dst.rearrange("p (a i) j -> p a j i", i=4)
+            src = src.rearrange("p j (a i) -> p a j i", i=4)
             if engine is nc.gpsimd:
-                nc.gpsimd.tensor_scalar(
-                    out=dst, in0=src.rearrange("p j a -> p a j"),
-                    scalar1=1.0, scalar2=0.0, op0=MULT, op1=ADD,
-                )
+                nc.gpsimd.tensor_scalar(out=dst, in0=src, scalar1=1.0, scalar2=0.0, op0=MULT, op1=ADD)
+            elif engine is nc.scalar:
+                nc.scalar.activation(dst, src, COPY)
             else:
-                dst = dst.rearrange("p (a i) j -> p a j i", i=4)
-                src = src.rearrange("p j (a i) -> p a j i", i=4)
-                if engine is nc.scalar:
-                    nc.scalar.activation(dst, src, COPY)
-                else:
-                    nc.vector.tensor_copy(out=dst, in_=src)
+                nc.vector.tensor_copy(out=dst, in_=src)
 
         def scale_out(engine, dst, src, factor):
             if engine is nc.vector:

@@ -12,6 +12,7 @@ G_S = S // PASS
 N_TILES = S // P
 HALF_A = A // 2
 HALF_C = C // 2
+QUARTER = A // 4
 POOL = 216
 R_POOL = 192
 Y_VECTOR = 80
@@ -24,7 +25,8 @@ EARLY = 1
 WARM = (3, 1)
 EXTRA = (8, 9, 11, 12, 13, 14)
 X_BUFS = 12
-Y_ORDER = [(0, 0), (0, 1), (1, 0), (1, 1), (2, 0), (3, 0), (2, 1), (3, 1)]
+Y_ORDER = [(0, 0), (0, 1), (1, 0), (2, 0), (3, 0), (1, 1), (2, 1), (3, 1)]
+QUARTERS = [(0, 0), (0, 1), (0, 2), (0, 3), (1, 0), (1, 1), (2, 0), (2, 1), (3, 0), (3, 1), (1, 2), (2, 2), (3, 2), (1, 3), (2, 3), (3, 3)]
 
 FLOPS = 2 * S * K * C + 2 * S * C * A
 
@@ -110,14 +112,14 @@ def tile_pls_concentration_loadings_s7_kernel(
         load_y(1)
         load_x(7)
         load_x(8)
-        load_x(9)
         load_scale(2)
         load_y(2)
+        load_x(9)
+        load_scale(3)
+        load_y(3)
         load_x(10)
         load_x(11)
         nc.sync.dma_start(out=inv_bf[:, :, 0:1], in_=inv_score.rearrange("(m p o) -> p m o", p=P, o=1))
-        load_scale(3)
-        load_y(3)
 
         r_codes = keep.tile([P, G_K, C], U32, name="r_codes", align_bytes=256)
         r_scales = keep.tile([P, G_K, C], U8, name="r_scales", align_bytes=256)
@@ -233,11 +235,11 @@ def tile_pls_concentration_loadings_s7_kernel(
                     stop=(g == G_K - 1),
                 )
 
-        def weigh_t(i, engine, c0=0, c1=C):
+        def weigh_t(i, engine, c0=0, c1=C, b0=0, b1=None):
             g, j = i // PACK, i % PACK
             if g not in z_planes:
                 z_planes[g] = work.tile([P, PACK, C], BF16, tag="z_planes", name=f"z_planes{g}", align_bytes=256)
-            scale_out(engine, z_planes[g][:, j, c0:c1], t_banks[i, c0][:, : c1 - c0], weight_sb[:, i : i + 1])
+            scale_out(engine, z_planes[g][:, j, c0 + b0 : c0 + (b1 or c1 - c0)], t_banks[i, c0][:, b0 : b1 or c1 - c0], weight_sb[:, i : i + 1])
 
         def interleave_z(n, b0, b1, engine, tag="z_half"):
             g, c0 = n // 2, HALF_C * (n % 2)
@@ -245,9 +247,9 @@ def tile_pls_concentration_loadings_s7_kernel(
                 z_grouped[n] = stage.tile([P, HALF_C, PACK], BF16, tag=tag, name=f"z_grouped{n}", align_bytes=256)
             interleave(engine, z_grouped[n][:, b0:b1, :], z_planes[g][:, :, c0 + b0 : c0 + b1])
 
-        def quantise_z(n):
-            g, cols = n // 2, slice(HALF_C * (n % 2), HALF_C * (n % 2 + 1))
-            quantise(z_codes[g][:, cols], z_scales[g][:, cols], z_grouped[n][:].rearrange("p c j -> p (c j)"))
+        def quantise_z(n, b0=0, b1=HALF_C):
+            g, cols = n // 2, slice(HALF_C * (n % 2) + b0, HALF_C * (n % 2) + b1)
+            quantise(z_codes[g][:, cols], z_scales[g][:, cols], z_grouped[n][:, b0:b1].rearrange("p c j -> p (c j)"))
 
         edges = [0, 256] + [HALF_A * n for n in range(1, len(Y_ORDER) + 1)]
         y_planes = {
@@ -275,8 +277,10 @@ def tile_pls_concentration_loadings_s7_kernel(
         def interleave_y(n0, n1, b0, b1, engine, tag="y_slice"):
             if n0 not in y_grouped:
                 y_grouped[n0] = stage.tile([P, n1 - n0, PACK], BF16, tag=tag, name=f"y_grouped{n0}", align_bytes=256)
-            edge = max(e for e in edges if e <= n0 + b0)
-            a0 = n0 + b0 - edge
+            g, q = QUARTERS[(n0 + b0) // QUARTER]
+            first = HALF_A * Y_ORDER.index((g, q // 2)) + QUARTER * (q % 2) + (n0 + b0) % QUARTER
+            edge = max(e for e in edges if e <= first)
+            a0 = first - edge
             interleave(engine, y_grouped[n0][:, b0:b1, :], y_planes[edge][:, :, a0 : a0 + b1 - b0])
 
         def quantise_y(n0, n1):
@@ -284,25 +288,28 @@ def tile_pls_concentration_loadings_s7_kernel(
 
         cov_banks = {}
 
-        def multiply_cov(m, a0, g, b=None, width=HALF_A):
-            if g == 0:
-                cov_banks[m, a0] = bank(b, f"cov_sum{m}_{a0}")
+        def multiply_cov(m, a0, g, b=None, width=HALF_A, shares=None):
+            first_m, last_m = shares or (m, m)
+            if g == 0 and m == first_m:
+                whole = bank(b, f"cov_sum{m}_{a0}")
+                for n in range(first_m, last_m + 1):
+                    cov_banks[n, a0] = whole[:, width * (n - first_m) : width * (n - first_m + 1)]
             c_cols = slice(P * m, P * (m + 1))
-            n0 = HALF_A * Y_ORDER.index((g, a0 // HALF_A)) + a0 % HALF_A
+            n0 = QUARTER * QUARTERS.index((g, a0 // QUARTER)) + a0 % QUARTER
             n_cols = slice(n0, n0 + width)
             nc.tensor.matmul_mx(
-                out=cov_banks[m, a0][:, :width],
+                out=cov_banks[m, a0],
                 lhsT=z_codes[g][:, c_cols].bitcast(FP8X4),
                 lhsT_scale=z_scales[g][:, c_cols],
                 rhs=y_codes[:, n_cols].bitcast(FP8X4),
                 rhs_scale=y_scales[:, n_cols],
-                start=(g == 0),
-                stop=(g == G_S - 1),
+                start=(g == 0 and m == first_m),
+                stop=(g == G_S - 1 and m == last_m),
             )
 
         def store_cov(m, a0, engine, width=HALF_A):
             res = keep.tile([P, width], F32, name=f"res{m}_{a0}", align_bytes=256)
-            scale_out(engine, res[:], cov_banks[m, a0][:, :width], inv_sb[:, m : m + 1])
+            scale_out(engine, res[:], cov_banks[m, a0], inv_sb[:, m : m + 1])
             nc.sync.dma_start(out=out[P * m : P * (m + 1), a0 : a0 + width], in_=res[:])
 
         last = G_S - 1
@@ -412,52 +419,61 @@ def tile_pls_concentration_loadings_s7_kernel(
         quantise_x(30, 0, 1)
         quantise_x(30, 1, 2)
         multiply_t(13, 1)
-        multiply_t(14, 2)
+        multiply_t(14, 2, c1=HALF_C)
+        multiply_cov(3, 0, 1)
         multiply_t(15, 3, c1=HALF_C)
-        multiply_t(15, 0, c0=HALF_C)
+        multiply_t(14, 0, c0=HALF_C)
+        nc.scalar.copy(out=inv_sb[:], in_=inv_bf[:, :, 0])
         interleave_y(2816, 3328, POOL, 256, nc.scalar)
         interleave_y(2816, 3328, 256, 512, nc.scalar)
         weigh_t(13, nc.scalar)
-        nc.scalar.copy(out=inv_sb[:], in_=inv_bf[:, :, 0])
-        interleave_y(3328, 3584, 0, GAP, nc.scalar, shared[0])
+        multiply_t(15, 1, c0=HALF_C)
+        weigh_t(14, nc.scalar, c1=HALF_C)
+        interleave_y(3328, 3840, 0, 64, nc.scalar, shared[0])
         quantise_z(4)
         interleave_z(5, 0, HALF_C, nc.vector, "tail_a")
         quantise_y(2816, 3328)
         quantise_z(5)
-        weigh_t(14, nc.scalar)
-        weigh_t(15, nc.scalar, c1=HALF_C)
+        weigh_t(15, nc.scalar, c1=HALF_C, b1=P)
+        weigh_t(15, nc.scalar, c1=HALF_C, b0=P)
+        weigh_t(14, nc.scalar, c0=HALF_C)
         weigh_t(15, nc.scalar, c0=HALF_C)
-        interleave_z(6, 0, HALF_C, nc.vector)
-        interleave_y(3328, 3584, GAP, 256, nc.scalar)
-        interleave_y(3584, 4096, 0, TAIL_S, nc.scalar, "tail_b")
+        interleave_z(6, 0, P, nc.vector)
+        interleave_z(6, P, HALF_C, nc.vector)
+        quantise_z(6, 0, P)
+        quantise_z(6, P, HALF_C)
+        interleave_y(3328, 3840, 64, 256, nc.scalar, shared[0])
+
         interleave_z(7, 0, HALF_C, nc.vector, "tail_a")
-        quantise_z(6)
-        interleave_y(3584, 4096, TAIL_S, TAIL_S + TAIL_V, nc.vector)
+        interleave_y(3328, 3840, 256 + 0, 512, nc.vector)
         quantise_z(7)
-        interleave_y(3584, 4096, TAIL_S + TAIL_V, 512, nc.vector)
-        quantise_y(3328, 3584)
-        quantise_y(3584, 4096)
-        multiply_cov(3, 0, 1)
-        for m in range(4):
+        interleave_y(3840, 4096, 0, 256, nc.vector, "tail_b")
+        quantise_y(3328, 3840)
+        quantise_y(3840, 4096)
+
+        def narrow(m, q, groups, b=None, engine=None, a0=0, width=QUARTER):
+            for g in groups:
+                multiply_cov(m, QUARTER * q + a0, g, b, width)
+            if engine is not None:
+                store_cov(m, QUARTER * q + a0, engine, width)
+
+        for m in range(2):
             multiply_cov(m, 0, 2)
-        for g in range(2):
-            multiply_cov(0, HALF_A, g, 1)
-        multiply_cov(1, HALF_A, 0, 2)
-        for m in range(4):
+        narrow(0, 2, range(3), 2)
+        for m in range(2):
             multiply_cov(m, 0, last)
             store_cov(m, 0, nc.scalar)
-        multiply_cov(1, HALF_A, 1)
-        for m in range(2):
-            multiply_cov(m, HALF_A, 2)
-        for g in range(EARLY):
-            multiply_cov(2, HALF_A, g, 3)
-        for m in range(2):
-            multiply_cov(m, HALF_A, last)
-            store_cov(m, HALF_A, nc.scalar if m else nc.vector)
-        for g in range(EARLY, G_S):
-            multiply_cov(2, HALF_A, g, 3)
-        store_cov(2, HALF_A, nc.vector)
-        for a0, width, b, engine in ((512, 256, 0, nc.scalar), (768, 256, 4, nc.vector)):
-            for g in range(G_S):
-                multiply_cov(3, a0, g, b, width)
-            store_cov(3, a0, engine, width)
+        narrow(0, 2, range(3, G_S), 2, nc.scalar)
+        for m in range(2, 4):
+            multiply_cov(m, 0, 2)
+        narrow(1, 2, range(G_S), 3, nc.scalar)
+        for m in range(2, 4):
+            multiply_cov(m, 0, last)
+            store_cov(m, 0, nc.scalar)
+        narrow(2, 2, range(G_S), 0, nc.vector)
+        narrow(3, 2, range(G_S), 1, nc.scalar)
+        narrow(0, 3, range(G_S), 4, nc.vector)
+        narrow(1, 3, range(G_S), 5, nc.scalar)
+        narrow(2, 3, range(G_S), 2, nc.vector)
+        narrow(3, 3, range(G_S), 6, nc.scalar, 0, P)
+        narrow(3, 3, range(G_S), 7, nc.vector, P, P)

@@ -13,10 +13,12 @@ N_TILES = S // P
 HALF_A = A // 2
 HALF_C = C // 2
 QUARTER = A // 4
-POOL = 216
+POOL = 232
+LATE = 2560
+EARLY_Z = 64
 R_POOL = 192
 Y_VECTOR = 80
-SORTED = ()
+SORTED = (15,)
 GAP = 64
 V_WEIGH = 1
 TAIL_S = 224
@@ -170,7 +172,7 @@ def tile_pls_concentration_loadings_s7_kernel(
 
         def sort_x(i):
             x_sorted[i] = work.tile([P, 2, K // PACK], F32, tag="x_sorted", name=f"x_sorted{i}", align_bytes=256)
-            nc.scalar.copy(out=x_sorted[i][:], in_=x_raw[i][:].bitcast(F32).rearrange("p (w u) -> p u w", u=2))
+            nc.vector.tensor_copy(out=x_sorted[i][:], in_=x_raw[i][:].bitcast(F32).rearrange("p (w u) -> p u w", u=2))
 
         def transpose_x(h0, banks):
             for h, b in enumerate(banks, h0):
@@ -376,12 +378,13 @@ def tile_pls_concentration_loadings_s7_kernel(
         for i in range(5, 15):
             use = 2 * i if i < 10 else 3 * i - 10
             n0 = 256 * (i - 4 - (i + 1) % 2)
+            n1 = min(n0 + 512, LATE)
             z = (i - 6) // 2
             if i + 7 < N_TILES:
                 load_x(i + 7)
             transpose_x(2 * i, (use % 4, (use + 1) % 4))
             if i % 2:
-                interleave_y(n0, n0 + 512, 0, POOL, nc.gpsimd, shared[i // 2 % 2])
+                interleave_y(n0, n1, 0, POOL, nc.gpsimd, shared[i // 2 % 2])
             else:
                 interleave_z(z, 0, POOL, nc.gpsimd)
             centre_x(2 * i, 2, "x_odd" if i % 2 else shared[i // 2 % 2])
@@ -390,11 +393,12 @@ def tile_pls_concentration_loadings_s7_kernel(
                 multiply_cov((i - 8) % PACK, 0, (i - 8) // PACK, 4 + (i - 8) % PACK)
             if i % 2:
                 widen_next(3 if i in EXTRA else 2)
+                weigh_t(i - 2, nc.scalar)
+                if n1 - n0 > QUARTER:
+                    interleave_y(n0, n1, 256 + Y_VECTOR, 512, nc.scalar)
+                interleave_y(n0, n1, POOL, 256, nc.vector)
                 if i + 2 in SORTED:
                     sort_x(i + 2)
-                weigh_t(i - 2, nc.scalar)
-                interleave_y(n0, n0 + 512, 256 + Y_VECTOR, 512, nc.scalar)
-                interleave_y(n0, n0 + 512, POOL, 256, nc.vector)
                 if i > 5:
                     quantise_z(z)
                 else:
@@ -403,18 +407,20 @@ def tile_pls_concentration_loadings_s7_kernel(
                 widen_next(3 if i in EXTRA else 2)
                 if i == 6:
                     nc.scalar.copy(out=weight_sb[:, PACK:], in_=later_weight[:].rearrange("p g j -> p (g j)"))
-                if Y_VECTOR:
-                    interleave_y(n0, n0 + 512, 256, 256 + Y_VECTOR, nc.vector)
+                if n1 - n0 > QUARTER:
+                    interleave_y(n0, n1, 256, 256 + Y_VECTOR, nc.vector)
+                else:
+                    interleave_z(z + 1, 0, EARLY_Z, nc.vector, "tail_a")
                 interleave_z(z, POOL, HALF_C, nc.vector)
-                if i + 2 in SORTED:
-                    sort_x(i + 2)
                 weigh_t(i - 2, nc.scalar)
+            if i % 2 == 0 and i + 2 in SORTED:
+                sort_x(i + 2)
             quantise_x(2 * i, 0, 2)
             if i % 2 == 0:
-                quantise_y(n0, n0 + 512)
+                quantise_y(n0, n1)
 
         transpose_x(30, (3, 0))
-        interleave_y(2816, 3328, 0, POOL, nc.gpsimd, shared[1])
+        interleave_y(2560, 3072, 0, POOL, nc.gpsimd, shared[1])
         centre_x(30, 2, "x_odd")
         quantise_x(30, 0, 1)
         quantise_x(30, 1, 2)
@@ -424,15 +430,16 @@ def tile_pls_concentration_loadings_s7_kernel(
         multiply_t(15, 3, c1=HALF_C)
         multiply_t(14, 0, c0=HALF_C)
         nc.scalar.copy(out=inv_sb[:], in_=inv_bf[:, :, 0])
-        interleave_y(2816, 3328, POOL, 256, nc.scalar)
-        interleave_y(2816, 3328, 256, 512, nc.scalar)
+        interleave_y(2560, 3072, 256, 512, nc.scalar)
+        interleave_y(2560, 3072, POOL, 256, nc.scalar)
+        interleave_y(3072, 3328, 0, 96, nc.scalar, "tail_b")
         weigh_t(13, nc.scalar)
         multiply_t(15, 1, c0=HALF_C)
         weigh_t(14, nc.scalar, c1=HALF_C)
-        interleave_y(3328, 3840, 0, 64, nc.scalar, shared[0])
+        interleave_y(3072, 3328, 96, 160, nc.scalar, "tail_b")
         quantise_z(4)
-        interleave_z(5, 0, HALF_C, nc.vector, "tail_a")
-        quantise_y(2816, 3328)
+        interleave_z(5, EARLY_Z, HALF_C, nc.vector)
+        quantise_y(2560, 3072)
         quantise_z(5)
         weigh_t(15, nc.scalar, c1=HALF_C, b1=P)
         weigh_t(15, nc.scalar, c1=HALF_C, b0=P)
@@ -442,12 +449,14 @@ def tile_pls_concentration_loadings_s7_kernel(
         interleave_z(6, P, HALF_C, nc.vector)
         quantise_z(6, 0, P)
         quantise_z(6, P, HALF_C)
-        interleave_y(3328, 3840, 64, 256, nc.scalar, shared[0])
-
+        interleave_y(3072, 3328, 160, 256, nc.scalar)
+        interleave_y(3328, 3840, 0, 96, nc.scalar, shared[0])
         interleave_z(7, 0, HALF_C, nc.vector, "tail_a")
-        interleave_y(3328, 3840, 256 + 0, 512, nc.vector)
+        quantise_y(3072, 3328)
         quantise_z(7)
-        interleave_y(3840, 4096, 0, 256, nc.vector, "tail_b")
+        interleave_y(3328, 3840, 96, 256, nc.vector, shared[0])
+        interleave_y(3328, 3840, 256, 512, nc.vector)
+        interleave_y(3840, 4096, 0, 256, nc.vector, "x_odd")
         quantise_y(3328, 3840)
         quantise_y(3840, 4096)
 
@@ -463,14 +472,14 @@ def tile_pls_concentration_loadings_s7_kernel(
         for m in range(2):
             multiply_cov(m, 0, last)
             store_cov(m, 0, nc.scalar)
-        narrow(0, 2, range(3, G_S), 2, nc.scalar)
         for m in range(2, 4):
             multiply_cov(m, 0, 2)
+        narrow(0, 2, range(3, G_S), 2, nc.scalar)
         narrow(1, 2, range(G_S), 3, nc.scalar)
         for m in range(2, 4):
             multiply_cov(m, 0, last)
             store_cov(m, 0, nc.scalar)
-        narrow(2, 2, range(G_S), 0, nc.vector)
+        narrow(2, 2, range(G_S), 0, nc.scalar)
         narrow(3, 2, range(G_S), 1, nc.scalar)
         narrow(0, 3, range(G_S), 4, nc.vector)
         narrow(1, 3, range(G_S), 5, nc.scalar)

@@ -134,8 +134,8 @@ def tile_pls_concentration_loadings_s7_kernel(
             return psum.tile([P, 512], F32, tag=f"bank{b}", name=name)
 
         def interleave(engine, dst, src):
-            dst = dst.rearrange("p (a i) j -> p a j i", i=4)
-            src = src.rearrange("p j (a i) -> p a j i", i=4)
+            dst = dst.rearrange("p (a i) j -> p a j i", i=8)
+            src = src.rearrange("p j (a i) -> p a j i", i=8)
             if engine is nc.gpsimd:
                 nc.gpsimd.tensor_scalar(out=dst, in0=src, scalar1=1.0, scalar2=0.0, op0=MULT, op1=ADD)
             elif engine is nc.scalar:

from contextlib import ExitStack

import concourse.mybir as mybir
from concourse.masks import make_identity

S, K, C, A = 2048, 2048, 512, 1024
P = 128
PACK = 4
PASS = P * PACK
G_K = K // PASS
G_S = S // PASS
N_TILES = S // P
HALF_A = A // 2
HALF_C = C // 2
QUARTER = A // 4
POOL = 232
LATE = 2560
EARLY_Z = 64
R_POOL = 192
Y_VECTOR = 80
SORTED = (15,)
GAP = 64
V_WEIGH = 1
TAIL_S = 224
TAIL_V = 64
EARLY = 1
WARM = (3, 1)
EXTRA = (8, 9, 11, 12, 13, 14)
X_BUFS = 12
Y_ORDER = [(0, 0), (0, 1), (1, 0), (2, 0), (3, 0), (1, 1), (2, 1), (3, 1)]
QUARTERS = [(0, 0), (0, 1), (0, 2), (0, 3), (1, 0), (1, 1), (2, 0), (2, 1), (3, 0), (3, 1), (1, 2), (2, 2), (3, 2), (1, 3), (2, 3), (3, 3)]

FLOPS = 2 * S * K * C + 2 * S * C * A

F32 = mybir.dt.float32
BF16 = mybir.dt.bfloat16
U32 = mybir.dt.uint32
U8 = mybir.dt.uint8
FP8 = mybir.dt.float8_e4m3fn
FP8X4 = mybir.dt.float8_e4m3fn_x4
COPY = mybir.ActivationFunctionType.Copy
MULT = mybir.AluOpType.mult
SUB = mybir.AluOpType.subtract
ADD = mybir.AluOpType.add


def tile_pls_concentration_loadings_s7_kernel(
    tc, spectra, mean, r, weight, y_bytes, y_scale, inv_score, out
):
    nc = tc.nc
    with ExitStack() as ctx:
        keep = ctx.enter_context(tc.tile_pool(name="keep", bufs=1))
        work = ctx.enter_context(tc.tile_pool(name="work", bufs=2))
        stage = ctx.enter_context(tc.tile_pool(name="stage", bufs=1))
        psum = ctx.enter_context(tc.psum_pool(name="psum", bufs=1))

        ident = keep.tile([P, P], F32, name="ident")
        make_identity(nc, ident[:])

        ctx.enter_context(tc.manual_schedule())

        mean_sb = keep.tile([P, G_K, 2, 2], BF16, name="mean_sb")
        first_weight = keep.tile([P, 1, PACK], BF16, name="first_weight")
        later_weight = keep.tile([P, G_S - 1, PACK], BF16, name="later_weight")
        weight_sb = keep.tile([P, G_S * PACK], F32, name="weight_sb")
        y_scale_sb = [keep.tile([P, PACK], F32, name=f"y_scale_sb{g}") for g in range(G_S)]
        inv_bf = keep.tile([P, 4, 2], BF16, name="inv_bf")
        inv_sb = keep.tile([P, 4], F32, name="inv_sb")

        x_raw = {}
        r_raw = [keep.tile([P, PACK, C], BF16, name=f"r_raw{g}", align_bytes=256) for g in range(G_K)]
        y_raw = [keep.tile([P, PACK, A], U8, name=f"y_raw{g}", align_bytes=256) for g in range(G_S)]

        x_hbm = spectra.rearrange("(g p j) k -> g j p k", p=P, j=PACK)
        r_hbm = r.rearrange("(g p j) c -> g p j c", p=P, j=PACK)
        y_hbm = y_bytes.rearrange("(g p j) a -> g p j a", p=P, j=PACK)

        def load_x(i, pieces=1):
            x_raw[i] = work.tile([P, K], BF16, tag="x_raw", name=f"x_raw{i}", bufs=X_BUFS, align_bytes=256)
            for n in range(pieces):
                cols = slice(K * n // pieces, K * (n + 1) // pieces)
                nc.sync.dma_start(out=x_raw[i][:, cols], in_=x_hbm[i // PACK, i % PACK][:, cols])

        def load_r(g):
            nc.sync.dma_start(out=r_raw[g][:], in_=r_hbm[g])

        def load_y(g, a0=0, a1=A):
            nc.sync.dma_start(out=y_raw[g][:, :, a0:a1], in_=y_hbm[g][:, :, a0:a1])

        def load_scale(g):
            nc.sync.dma_start(out=y_scale_sb[g][:], in_=y_scale_hbm[:, g])

        mean_hbm = mean.rearrange("(g p t) -> p g t", p=P, t=PACK)
        y_scale_hbm = y_scale.rearrange("(g p j) o -> p g (j o)", p=P, j=PACK)
        weight_hbm = weight.rearrange("(g p j) -> p g j", p=P, j=PACK)
        nc.scalar.dma_start(out=mean_sb[:].rearrange("p g u e -> p g (u e)"), in_=mean_hbm)
        load_x(0, 2)
        load_r(0)
        load_x(1)
        load_r(1)
        load_x(2)
        load_r(2)
        load_x(3)
        load_r(3)
        load_scale(0)
        load_x(4)
        load_y(0, 0, 256)
        nc.sync.dma_start(out=first_weight[:], in_=weight_hbm[:, :1])
        load_y(0, 256, 1024)
        load_x(5)
        load_x(6)
        nc.sync.dma_start(out=later_weight[:], in_=weight_hbm[:, 1:])
        load_scale(1)
        load_y(1)
        load_x(7)
        load_x(8)
        load_scale(2)
        load_y(2)
        load_x(9)
        load_scale(3)
        load_y(3)
        load_x(10)
        load_x(11)
        nc.sync.dma_start(out=inv_bf[:, :, 0:1], in_=inv_score.rearrange("(m p o) -> p m o", p=P, o=1))

        r_codes = keep.tile([P, G_K, C], U32, name="r_codes", align_bytes=256)
        r_scales = keep.tile([P, G_K, C], U8, name="r_scales", align_bytes=256)
        y_codes = keep.tile([P, G_S * A], U32, name="y_codes", align_bytes=256)
        y_scales = keep.tile([P, G_S * A], U8, name="y_scales", align_bytes=256)
        z_codes = [keep.tile([P, C], U32, name=f"z_codes{g}", align_bytes=256) for g in range(G_S)]
        z_scales = [keep.tile([P, C], U8, name=f"z_scales{g}", align_bytes=256) for g in range(G_S)]

        def bank(b, name):
            return psum.tile([P, 512], F32, tag=f"bank{b}", name=name)

        def interleave(engine, dst, src):
            dst = dst.rearrange("p (a i) j -> p a j i", i=8)
            src = src.rearrange("p j (a i) -> p a j i", i=8)
            if engine is nc.gpsimd:
                nc.gpsimd.tensor_scalar(out=dst, in0=src, scalar1=1.0, scalar2=0.0, op0=MULT, op1=ADD)
            elif engine is nc.scalar:
                nc.scalar.activation(dst, src, COPY)
            else:
                nc.vector.tensor_copy(out=dst, in_=src)

        def scale_out(engine, dst, src, factor):
            if engine is nc.vector:
                nc.vector.tensor_scalar(out=dst, in0=src, scalar1=factor, scalar2=None, op0=MULT)
            else:
                nc.scalar.activation(dst, src, COPY, scale=factor)

        def quantise(codes, scales, grouped):
            nc.vector.quantize_mx(out=codes.bitcast(FP8X4), scales=scales, in_=grouped)

        r_grouped = {}

        def interleave_r(g, c0, c1, engine):
            if g not in r_grouped:
                r_grouped[g] = stage.tile([P, C, PACK], BF16, tag=("tail_a", "x_even", "x_odd", "tail_a")[g], name=f"r_grouped{g}", align_bytes=256)
            interleave(engine, r_grouped[g][:, c0:c1, :], r_raw[g][:, :, c0:c1])

        def quantise_r(g):
            quantise(r_codes[:, g, :], r_scales[:, g, :], r_grouped[g][:].rearrange("p c j -> p (c j)"))

        x_banks = {}
        x_grouped = {}
        x_codes = {}
        x_scales = {}
        x_quantised = {}

        x_sorted = {}

        def sort_x(i):
            x_sorted[i] = work.tile([P, 2, K // PACK], F32, tag="x_sorted", name=f"x_sorted{i}", align_bytes=256)
            nc.vector.tensor_copy(out=x_sorted[i][:], in_=x_raw[i][:].bitcast(F32).rearrange("p (w u) -> p u w", u=2))

        def transpose_x(h0, banks):
            for h, b in enumerate(banks, h0):
                words = x_raw[h // 2][:].bitcast(F32)
                x_banks[h] = bank(b, f"x_turned{h}")
                view = x_banks[h][:].rearrange("p (u g s) -> p u g s", u=2, g=2)
                for gl in range(2):
                    g = 2 * (h % 2) + gl
                    for u in range(2):
                        if h // 2 in x_sorted:
                            source = x_sorted[h // 2][:, u, P * g : P * (g + 1)]
                        else:
                            source = words[:, 256 * g + u : 256 * (g + 1) : 2]
                        nc.tensor.transpose(view[:, u, gl, :], source, ident[:])

        def centre_x(h0, count, tag=None):
            tag = tag or ("x_even", "x_odd")[h0 // 2 % 2]
            x_grouped[h0] = stage.tile(
                [P, count, 2, P, 2, 2], BF16, tag=tag, name=f"x_grouped{h0}", align_bytes=256
            )
            codes = work.tile([P, 2 * P * count], U32, tag="x_codes", name=f"x_codes{h0}", bufs=5, align_bytes=256)
            scales = work.tile([P, 2 * P * count], U8, tag="x_scales", name=f"x_scales{h0}", bufs=5, align_bytes=256)
            x_quantised[h0] = (codes, scales)
            for n in range(count):
                b = (h0 + n) % 2
                x_codes[h0 + n] = codes[:, 2 * P * n : 2 * P * (n + 1)]
                x_scales[h0 + n] = scales[:, 2 * P * n : 2 * P * (n + 1)]
                nc.vector.tensor_tensor(
                    out=x_grouped[h0][:, n],
                    in0=x_banks[h0 + n][:].bitcast(BF16).rearrange("p (u g s e) -> p g s u e", u=2, g=2, e=2),
                    in1=mean_sb[:, 2 * b : 2 * b + 2].unsqueeze(2).to_broadcast([P, 2, P, 2, 2]),
                    op=SUB,
                )

        def quantise_x(h0, n0, n1):
            codes, scales = x_quantised[h0]
            flat = x_grouped[h0][:].rearrange("p n g s u e -> p (n g s u e)")
            cols = slice(2 * P * n0, 2 * P * n1)
            quantise(codes[:, cols], scales[:, cols], flat[:, PACK * cols.start : PACK * cols.stop])

        def warm_up(count):
            idle = bank(7, "warm_up")
            for n in range(count):
                nc.tensor.matmul(idle[:], lhsT=x_raw[0][:, :P], rhs=x_raw[0][:, :512], start=True, stop=True)

        t_banks = {}
        z_planes = {}
        z_grouped = {}

        def multiply_t(i, b, passes=range(G_K), c0=0, c1=C):
            for g in passes:
                if g == 0:
                    t_banks[i, c0] = bank(b, f"t_sum{i}_{c0}")
                h, cols = 2 * i + g // 2, slice(P * (g % 2), P * (g % 2 + 1))
                nc.tensor.matmul_mx(
                    out=t_banks[i, c0][:, : c1 - c0],
                    lhsT=x_codes[h][:, cols].bitcast(FP8X4),
                    lhsT_scale=x_scales[h][:, cols],
                    rhs=r_codes[:, g, c0:c1].bitcast(FP8X4),
                    rhs_scale=r_scales[:, g, c0:c1],
                    start=(g == 0),
                    stop=(g == G_K - 1),
                )

        def weigh_t(i, engine, c0=0, c1=C, b0=0, b1=None):
            g, j = i // PACK, i % PACK
            if g not in z_planes:
                z_planes[g] = work.tile([P, PACK, C], BF16, tag="z_planes", name=f"z_planes{g}", align_bytes=256)
            scale_out(engine, z_planes[g][:, j, c0 + b0 : c0 + (b1 or c1 - c0)], t_banks[i, c0][:, b0 : b1 or c1 - c0], weight_sb[:, i : i + 1])

        def interleave_z(n, b0, b1, engine, tag="z_half"):
            g, c0 = n // 2, HALF_C * (n % 2)
            if n not in z_grouped:
                z_grouped[n] = stage.tile([P, HALF_C, PACK], BF16, tag=tag, name=f"z_grouped{n}", align_bytes=256)
            interleave(engine, z_grouped[n][:, b0:b1, :], z_planes[g][:, :, c0 + b0 : c0 + b1])

        def quantise_z(n, b0=0, b1=HALF_C):
            g, cols = n // 2, slice(HALF_C * (n % 2) + b0, HALF_C * (n % 2) + b1)
            quantise(z_codes[g][:, cols], z_scales[g][:, cols], z_grouped[n][:, b0:b1].rearrange("p c j -> p (c j)"))

        edges = [0, 256] + [HALF_A * n for n in range(1, len(Y_ORDER) + 1)]
        y_planes = {
            n0: keep.tile([P, PACK, n1 - n0], BF16, name=f"y_planes{n0}", align_bytes=256)
            for n0, n1 in zip(edges, edges[1:])
        }
        y_grouped = {}

        def widen_y(n, rows=range(PACK), a0=0, a1=HALF_A):
            g, half = Y_ORDER[n]
            for j in rows:
                nc.scalar.activation(
                    y_planes[HALF_A * n + a0][:, j, :],
                    y_raw[g][:, j, HALF_A * half + a0 : HALF_A * half + a1].bitcast(FP8),
                    COPY, scale=y_scale_sb[g][:, j : j + 1],
                )

        rows_left = [(n, j) for n in range(1, len(Y_ORDER)) for j in range(PACK)]

        def widen_next(count):
            for n, j in rows_left[:count]:
                widen_y(n, [j])
                rows_left.remove((n, j))

        def interleave_y(n0, n1, b0, b1, engine, tag="y_slice"):
            if n0 not in y_grouped:
                y_grouped[n0] = stage.tile([P, n1 - n0, PACK], BF16, tag=tag, name=f"y_grouped{n0}", align_bytes=256)
            g, q = QUARTERS[(n0 + b0) // QUARTER]
            first = HALF_A * Y_ORDER.index((g, q // 2)) + QUARTER * (q % 2) + (n0 + b0) % QUARTER
            edge = max(e for e in edges if e <= first)
            a0 = first - edge
            interleave(engine, y_grouped[n0][:, b0:b1, :], y_planes[edge][:, :, a0 : a0 + b1 - b0])

        def quantise_y(n0, n1):
            quantise(y_codes[:, n0:n1], y_scales[:, n0:n1], y_grouped[n0][:].rearrange("p a j -> p (a j)"))

        cov_banks = {}

        def multiply_cov(m, a0, g, b=None, width=HALF_A, shares=None):
            first_m, last_m = shares or (m, m)
            if g == 0 and m == first_m:
                whole = bank(b, f"cov_sum{m}_{a0}")
                for n in range(first_m, last_m + 1):
                    cov_banks[n, a0] = whole[:, width * (n - first_m) : width * (n - first_m + 1)]
            c_cols = slice(P * m, P * (m + 1))
            n0 = QUARTER * QUARTERS.index((g, a0 // QUARTER)) + a0 % QUARTER
            n_cols = slice(n0, n0 + width)
            nc.tensor.matmul_mx(
                out=cov_banks[m, a0],
                lhsT=z_codes[g][:, c_cols].bitcast(FP8X4),
                lhsT_scale=z_scales[g][:, c_cols],
                rhs=y_codes[:, n_cols].bitcast(FP8X4),
                rhs_scale=y_scales[:, n_cols],
                start=(g == 0 and m == first_m),
                stop=(g == G_S - 1 and m == last_m),
            )

        def store_cov(m, a0, engine, width=HALF_A):
            res = keep.tile([P, width], F32, name=f"res{m}_{a0}", align_bytes=256)
            scale_out(engine, res[:], cov_banks[m, a0], inv_sb[:, m : m + 1])
            nc.sync.dma_start(out=out[P * m : P * (m + 1), a0 : a0 + width], in_=res[:])

        last = G_S - 1

        transpose_x(0, (0, 1))
        centre_x(0, 2, "x_even")
        interleave_r(0, 0, 256, nc.scalar)
        interleave_r(0, 256, 512, nc.vector)
        quantise_x(0, 0, 1)
        quantise_x(0, 1, 2)
        quantise_r(0)
        if WARM[0]:
            warm_up(WARM[0])
        transpose_x(2, (2, 3))
        multiply_t(0, 4, [0])
        if WARM[1]:
            warm_up(WARM[1])
        interleave_r(1, 0, R_POOL, nc.gpsimd)
        interleave_r(1, R_POOL, 512, nc.scalar)
        centre_x(2, 2, "x_odd")
        quantise_x(2, 0, 1)
        quantise_x(2, 1, 2)
        quantise_r(1)
        transpose_x(4, (0, 1))
        multiply_t(1, 5, [0])
        multiply_t(0, 4, [1])
        multiply_t(1, 5, [1])
        interleave_r(2, 0, R_POOL, nc.gpsimd)
        interleave_r(2, R_POOL, 512, nc.scalar)
        centre_x(4, 2, "tail_a")
        quantise_x(4, 0, 1)
        quantise_x(4, 1, 2)
        quantise_r(2)
        transpose_x(6, (2, 3))
        multiply_t(2, 6, [0, 1])
        for n in range(3):
            multiply_t(n, None, [2])
        interleave_r(3, 0, R_POOL, nc.gpsimd)
        interleave_r(3, R_POOL, 512, nc.scalar)
        centre_x(6, 2, "y_slice")
        quantise_x(6, 0, 1)
        quantise_x(6, 1, 2)
        quantise_r(3)
        widen_y(0, a1=256)
        nc.scalar.copy(out=weight_sb[:, :PACK], in_=first_weight[:, 0])
        widen_y(0, a0=256)

        transpose_x(8, (0, 1))
        interleave_y(0, 256, 0, 256, nc.gpsimd, "z_half")
        centre_x(8, 1, "y_slice")
        centre_x(9, 1, "tail_a")
        multiply_t(3, 7, [0])
        for n in range(3):
            multiply_t(n, None, [3])
        multiply_t(3, None, [1])
        weigh_t(0, nc.vector)
        weigh_t(1, nc.vector if V_WEIGH else nc.scalar)
        widen_next(2)
        weigh_t(2, nc.scalar)
        quantise_x(8, 0, 1)
        quantise_x(9, 0, 1)

        shared = ("y_slice", "x_even")
        for i in range(5, 15):
            use = 2 * i if i < 10 else 3 * i - 10
            n0 = 256 * (i - 4 - (i + 1) % 2)
            n1 = min(n0 + 512, LATE)
            z = (i - 6) // 2
            if i + 7 < N_TILES:
                load_x(i + 7)
            transpose_x(2 * i, (use % 4, (use + 1) % 4))
            if i % 2:
                interleave_y(n0, n1, 0, POOL, nc.gpsimd, shared[i // 2 % 2])
            else:
                interleave_z(z, 0, POOL, nc.gpsimd)
            centre_x(2 * i, 2, "x_odd" if i % 2 else shared[i // 2 % 2])
            multiply_t(i - 2, 4 + (i - 2) % 4 if i < 10 else (use + 2) % 4, range(2 if i == 5 else 0, G_K))
            if i >= 8:
                multiply_cov((i - 8) % PACK, 0, (i - 8) // PACK, 4 + (i - 8) % PACK)
            if i % 2:
                widen_next(3 if i in EXTRA else 2)
                weigh_t(i - 2, nc.scalar)
                if n1 - n0 > QUARTER:
                    interleave_y(n0, n1, 256 + Y_VECTOR, 512, nc.scalar)
                interleave_y(n0, n1, POOL, 256, nc.vector)
                if i + 2 in SORTED:
                    sort_x(i + 2)
                if i > 5:
                    quantise_z(z)
                else:
                    quantise_y(0, 256)
            else:
                widen_next(3 if i in EXTRA else 2)
                if i == 6:
                    nc.scalar.copy(out=weight_sb[:, PACK:], in_=later_weight[:].rearrange("p g j -> p (g j)"))
                if n1 - n0 > QUARTER:
                    interleave_y(n0, n1, 256, 256 + Y_VECTOR, nc.vector)
                else:
                    interleave_z(z + 1, 0, EARLY_Z, nc.vector, "tail_a")
                interleave_z(z, POOL, HALF_C, nc.vector)
                weigh_t(i - 2, nc.scalar)
            if i % 2 == 0 and i + 2 in SORTED:
                sort_x(i + 2)
            quantise_x(2 * i, 0, 2)
            if i % 2 == 0:
                quantise_y(n0, n1)

        transpose_x(30, (3, 0))
        interleave_y(2560, 3072, 0, POOL, nc.gpsimd, shared[1])
        centre_x(30, 2, "x_odd")
        quantise_x(30, 0, 1)
        quantise_x(30, 1, 2)
        multiply_t(13, 1)
        multiply_t(14, 2, c1=HALF_C)
        multiply_cov(3, 0, 1)
        multiply_t(15, 3, c1=HALF_C)
        multiply_t(14, 0, c0=HALF_C)
        nc.scalar.copy(out=inv_sb[:], in_=inv_bf[:, :, 0])
        interleave_y(2560, 3072, 256, 512, nc.scalar)
        interleave_y(2560, 3072, POOL, 256, nc.scalar)
        interleave_y(3072, 3328, 0, 96, nc.scalar, "tail_b")
        weigh_t(13, nc.scalar)
        multiply_t(15, 1, c0=HALF_C)
        weigh_t(14, nc.scalar, c1=HALF_C)
        interleave_y(3072, 3328, 96, 160, nc.scalar, "tail_b")
        quantise_z(4)
        interleave_z(5, EARLY_Z, HALF_C, nc.vector)
        quantise_y(2560, 3072)
        quantise_z(5)
        weigh_t(15, nc.scalar, c1=HALF_C, b1=P)
        weigh_t(15, nc.scalar, c1=HALF_C, b0=P)
        weigh_t(14, nc.scalar, c0=HALF_C)
        weigh_t(15, nc.scalar, c0=HALF_C)
        interleave_z(6, 0, P, nc.vector)
        interleave_z(6, P, HALF_C, nc.vector)
        quantise_z(6, 0, P)
        quantise_z(6, P, HALF_C)
        interleave_y(3072, 3328, 160, 256, nc.scalar)
        interleave_y(3328, 3840, 0, 96, nc.scalar, shared[0])
        interleave_z(7, 0, HALF_C, nc.vector, "tail_a")
        quantise_y(3072, 3328)
        quantise_z(7)
        interleave_y(3328, 3840, 96, 256, nc.vector, shared[0])
        interleave_y(3328, 3840, 256, 512, nc.vector)
        interleave_y(3840, 4096, 0, 256, nc.vector, "x_odd")
        quantise_y(3328, 3840)
        quantise_y(3840, 4096)

        def narrow(m, q, groups, b=None, engine=None, a0=0, width=QUARTER):
            for g in groups:
                multiply_cov(m, QUARTER * q + a0, g, b, width)
            if engine is not None:
                store_cov(m, QUARTER * q + a0, engine, width)

        for m in range(2):
            multiply_cov(m, 0, 2)
        narrow(0, 2, range(3), 2)
        for m in range(2):
            multiply_cov(m, 0, last)
            store_cov(m, 0, nc.scalar)
        for m in range(2, 4):
            multiply_cov(m, 0, 2)
        narrow(0, 2, range(3, G_S), 2, nc.scalar)
        narrow(1, 2, range(G_S), 3, nc.scalar)
        for m in range(2, 4):
            multiply_cov(m, 0, last)
            store_cov(m, 0, nc.scalar)
        narrow(2, 2, range(G_S), 0, nc.scalar)
        narrow(3, 2, range(G_S), 1, nc.scalar)
        narrow(0, 3, range(G_S), 4, nc.vector)
        narrow(1, 3, range(G_S), 5, nc.scalar)
        narrow(2, 3, range(G_S), 2, nc.vector)
        narrow(3, 3, range(G_S), 6, nc.scalar, 0, P)
        narrow(3, 3, range(G_S), 7, nc.vector, P, P)
